import numpy as np, ml_dtypes
CORES = [16,17,18,19,32,33,34,35]
N = 8
BF = ml_dtypes.bfloat16
def gentries(a):
    return np.ascontiguousarray(a.reshape(8, 16, -1).transpose(0, 2, 1)).reshape(8, -1)
def gtable(e):
    e = np.asarray(e); return np.ascontiguousarray(e.reshape(8, -1, 16).transpose(0, 2, 1)).reshape(128, -1).astype(np.int32)
W, R, NR, TV = 4096, 8, 512, 3
K = R * NR; NONE = W - 1; SH = (N, 8, R, NR)
def hsh(a, b):
    return (((a * b) >> 5) + 37 * a + b) & (W - 1)
def pack(x, y, g, a, b, t):
    o = {"xt": np.ascontiguousarray(x.reshape(N, 128, W)).astype(np.float32).astype(BF), "yv": np.ascontiguousarray(y.reshape(N, 128, TV * NR)).astype(np.float32).astype(BF)}
    for k, v in (("gl", g), ("al", a), ("bl", b), ("th", t)): o[k] = np.stack([gtable(w.reshape(8, -1)) for w in v])
    return o
def robots(rng, share, mem):
    g = np.where(rng.random(SH) < share, rng.integers(0, NONE, SH), NONE); keep = rng.random(SH) < mem
    return g, np.where(keep, rng.integers(0, NONE, SH), NONE), np.where(keep, rng.integers(0, NONE, SH), NONE)
def pool(rng, goals, m):
    a = rng.permutation(NONE)[:64]; a[0] = 64; a[1] = 128
    lut = np.zeros(W, bool); lut[goals] = True
    i, j = np.nonzero(lut[hsh(a[:, None], np.arange(NONE)[None, :])]); s = rng.integers(0, len(i), m)
    return a[i[s]], j[s]
def halves(rng, x, y, q, e):
    near = np.zeros(W, bool); near[rng.permutation(NONE)[:W // 2]] = True
    x[q, e] = np.where(near[None, :], rng.integers(0, 64, (16, W)), rng.integers(128, 256, (16, W)))
    y[q, e, :, 0] = rng.integers(0, 64, (16, NR))
    return near
def pairs(rng, near):
    far = rng.permutation(np.nonzero(~near[:NONE])[0]); a = far[:128]
    i, j = np.nonzero(near[hsh(a[:, None], far[None, :])]); s = rng.permutation(len(i))
    u, v = a[i[s]], far[j[s]]
    return u, v, hsh(u, v)
def setup_inputs(rng):
    x = rng.integers(0, 256, (N, 8, 16, W)); y = rng.integers(0, 256, (N, 8, 16, TV, NR))
    g, a, b = robots(rng, rng.choice(np.array([0.3, 0.6, 0.9, 1.0]), (N, 8, 1, NR)), 0.4)
    return pack(x, y, g, a, b, rng.integers(900, 1700, SH))
def setup_inputs_clash(rng):
    x = rng.integers(0, 256, (N, 8, 16, W)); y = rng.integers(0, 256, (N, 8, 16, TV, NR)); g, a, b = robots(rng, 1.0, 0.3)
    for q in range(N):
        for e in range(8):
            goals = np.concatenate([np.array([0, W - 2]), rng.integers(1, W - 2, 2)]); c = rng.integers(0, 256, 16)
            x[q, e][:, goals] = c[:, None]; y[q, e][:, 0, :] = c[:, None]
            u, v = pool(rng, goals, (R // 2) * NR)
            g[q, e, 0::2] = u.reshape(R // 2, NR); g[q, e, 1::2] = v.reshape(R // 2, NR)
    g = np.where((rng.random((N, 8, 1, NR)) < 0.3) | (rng.random(SH) < 0.1), NONE, g)
    for q in range(N):
        for s, e in enumerate(rng.permutation(8)[:2]):
            u, v, n = pairs(rng, halves(rng, x, y, q, e))
            if s == 0:
                w = np.nonzero(n == n[0])[0]; i = w[rng.integers(0, len(w), K // 2)]
            else:
                i = rng.integers(0, len(n), K // 2); i[:NR] = rng.permutation(np.unique(n, return_index=True)[1])[:NR]
            g[q, e, 0::2] = u[i].reshape(R // 2, NR); g[q, e, 1::2] = v[i].reshape(R // 2, NR)
    return pack(x, y, g, a, b, rng.integers(900, 1700, SH))
def setup_inputs_ties(rng):
    s = rng.integers(0, 2, (N, 8, 1, 1)) * 3 + 1
    x = 100 + s * rng.integers(0, 8, (N, 8, 16, W)); y = 100 + s[..., None] * rng.integers(0, 8, (N, 8, 16, TV, NR))
    g, a, b = robots(rng, rng.choice(np.array([0.4, 0.7, 1.0]), (N, 8, 1, NR)), 0.6)
    return pack(x, y, g, a, b, np.where(s == 1, rng.integers(0, 60, SH), rng.integers(60, 200, SH)))
def setup_inputs_corners(rng):
    x = rng.integers(0, 256, (N, 8, 16, W)); y = rng.integers(0, 256, (N, 8, 16, TV, NR)); g, a, b = robots(rng, 1.0, 1.0)
    kd = rng.integers(0, 11, (N, 8, 1, NR)); k = np.arange(R)[None, None, :, None]
    none = g.copy()
    for q in range(N):
        for e in range(8):
            u, v = pool(rng, np.array([NONE]), (R // 2) * NR)
            none[q, e, 0::2] = u.reshape(R // 2, NR); none[q, e, 1::2] = v.reshape(R // 2, NR)
    g = np.where(kd == 6, g[:, :, :1], np.where(kd == 8, none, np.where((kd == 10) & (k % 2 == 0), 0, g)))
    full = (kd == 1) | ((kd == 2) & (k % 2 == 0)) | ((kd == 3) & (k % 2 == 1)) | ((kd == 4) & (k == R - 1)) | ((kd == 5) & (k == 0)) | (kd == 6) | ((kd == 7) & (k % 4 < 2)) | (kd == 8) | ((kd == 9) & (rng.random(SH) < 0.5)) | (kd == 10)
    g = np.where(full, g, NONE)
    a = np.where((kd == 9) | ((kd == 10) & (rng.random(SH) < 0.5)), NONE, a); b = np.where(kd == 7, NONE, b)
    a = np.where(rng.random(SH) < 0.05, rng.choice(np.array([0, W - 2]), SH), a)
    t = rng.choice(np.array([0, 4080, 1300, 1400]), SH, p=[0.3, 0.2, 0.25, 0.25])
    for q in range(N):
        for s, e in enumerate(rng.permutation(8)[:2]):
            near = halves(rng, x, y, q, e); far = np.nonzero(~near[:NONE])[0]
            second = (np.arange(R)[:, None] + rng.integers(0, 2, NR)[None, :]) % 2 == 0
            if s == 0:
                a[q, e] = rng.integers(0, NONE, (R, NR)); t[q, e] = rng.integers(0, 1000, (R, NR))
            else:
                far = far[near[hsh(NONE, far)]]; w = rng.random((R, NR)) < 0.5
                a[q, e] = np.where(w, NONE, a[q, e]); t[q, e] = np.where(w, t[q, e], 4080)
            g[q, e] = np.where(second, far[rng.integers(0, len(far), (R, NR))], NONE)
    return pack(x, y, g, a, b, t)
def setup_inputs_ends(rng):
    v = 255 * rng.integers(0, 2, (N, 1, 1, 1)); e = rng.integers(0, 4, (N, 8, 1, W))
    x = np.where(e == 0, 0, np.where(e == 1, 255, 255 * rng.integers(0, 2, (N, 8, 16, W))))
    near = (rng.random((N, 8, 1, W)) < 0.25) & (np.arange(16)[None, None, :, None] == rng.integers(0, 16, (N, 8, 1, W)))
    x = np.where(near, np.abs(x - 1), x)
    x[..., 0] = v[..., 0]; x[..., W - 2] = v[..., 0]; x[..., W - 74] = 255 - v[..., 0]
    e = rng.integers(0, 3, (N, 8, 1, TV, NR)); y = np.where(e == 0, 0, np.where(e == 1, 255, 255 * rng.integers(0, 2, (N, 8, 16, TV, NR))))
    S = np.array([0, 1, int(rng.integers(2, NR - 2)), NR - 2, NR - 1])
    k = np.arange(R)[None, None, :, None]
    ty = rng.choice(np.array([0, 1, 2]), (N, 8, 1, NR), p=[0.6, 0.3, 0.1])
    ty[..., S] = 1
    g = np.where(ty == 0, rng.choice(np.array([0, NONE]), SH), np.where(ty == 1, np.where(k % 2 == 0, W - 2, 0), np.where(rng.random(SH) < 0.3, NONE, rng.integers(0, NONE, SH))))
    a = rng.choice(np.array([0, NONE, W - 2]), SH, p=[0.45, 0.45, 0.1]); b = rng.choice(np.array([0, NONE, W - 2]), SH, p=[0.45, 0.45, 0.1])
    t = rng.choice(np.array([0, 4080, 4079, 1]), SH, p=[0.4, 0.4, 0.1, 0.1])
    far = np.roll(v, -1, axis=0)
    for i in S:
        y[:, :, :, 0, i] = 255 - v[..., 0]; y[:, :, :, 1, i] = 255 - far[..., 0]
        t[:, :, :, i] = 4080 - 4 * R - (np.arange(R)[None, None, :] // 2) % 2
    return pack(x, y, g, a, b, t)
def setup_inputs_spread(rng):
    x = np.minimum((np.exp2(8 * rng.random((N, 8, 1, W))) * rng.random((N, 8, 16, W))).astype(np.int64), 255)
    y = np.minimum((np.exp2(8 * rng.random((N, 8, 1, TV, NR))) * rng.random((N, 8, 16, TV, NR))).astype(np.int64), 255)
    g, a, b = robots(rng, rng.random((N, 8, 1, NR)), rng.random((N, 8, 1, NR)))
    few = rng.random((N, 8, 1, NR)) < 0.5
    g = np.where(few & (g != NONE), np.minimum((NONE * rng.random(SH) ** 6).astype(np.int64), NONE - 1), g)
    t = np.minimum(np.exp2(12 * rng.random(SH)).astype(np.int64) - 1, 4080)
    return pack(x, y, g, a, b, t)
def check_inputs(d):
    bad = []
    for k, hi in (("xt", 255), ("yv", 255), ("gl", NONE), ("al", NONE), ("bl", NONE), ("th", 4080)):
        v = np.asarray(d[k]).astype(np.float64)
        if not (np.all(v >= 0) and np.all(v <= hi)): bad.append("range of " + k)
        elif np.any(v != np.floor(v)): bad.append("whole numbers of " + k)
    return bad
def reference(xt, yv, gl, al, bl, th):
    x = xt.astype(np.float32).astype(np.int32).reshape(N, 8, 16, W); y = yv.astype(np.float32).astype(np.int32).reshape(N, 8, 16, TV, NR)
    g, a, b, h = [np.stack([gentries(v) for v in w]).astype(np.int32).reshape(N, 8, R, NR) for w in (gl, al, bl, th)]
    c = np.zeros((N, NR), np.int32); row = np.arange(R)[None, :, None]; rob = np.arange(NR)[None, :]
    for t in range(TV):
        for r in range(N):
            q = (r + t) % N; G, A, B = g[r].copy(), a[r].copy(), b[r].copy()
            G1 = np.roll(G, -1, axis=1); n = hsh(G, G1); view = y[r][:, :, t][:, :, None, :]
            xg = np.take_along_axis(x[q], G.reshape(8, 1, K), 2); xn = np.take_along_axis(x[q], n.reshape(8, 1, K), 2)
            dg = np.add.reduce(np.abs(xg.reshape(8, 16, R, NR) - view), axis=1); dn = np.add.reduce(np.abs(xn.reshape(8, 16, R, NR) - view), axis=1)
            dg1 = np.roll(dg, -1, axis=1); full = G != NONE; full1 = np.roll(full, -1, axis=1)
            opens = full & (A != NONE) & ~full1 & (dg > h[r] + c[r][None, None, :])
            opened = np.roll(opens, 1, axis=1)
            merge = full & full1 & ~np.roll(opens, -1, axis=1) & ((row + t) % 2 == 0) & (n != NONE) & (dn < np.minimum(dg, dg1))
            gone = np.roll(merge, 1, axis=1)
            take = ~full & ~opened & full1 & (n != NONE) & (dn < dg1)
            some = np.any(merge, axis=1); low = np.argmax(merge, axis=1)
            i0 = low * NR + rob; i1 = ((low + 1) % R) * NR + rob
            val = (np.take_along_axis(xg, i0[:, None, :], 2) + np.take_along_axis(xg, i1[:, None, :], 2)) >> 1
            goal = np.take_along_axis(n.reshape(8, K), i0, 1)
            for e in range(8):
                w = np.nonzero(some[e])[0]; u, first = np.unique(goal[e][w], return_index=True)
                x[q, e][:, u] = val[e][:, w[first]]
            clear = opens | opened | gone | take
            g[r] = np.where(opens, A, np.where(opened, np.roll(B, 1, axis=1), np.where(merge | take, n, np.where(gone, NONE, G))))
            na = np.where(merge, G, np.where(clear, NONE, A)); nb = np.where(merge, G1, np.where(clear, NONE, B))
            a[r] = na; b[r] = nb; c[r] = np.add.reduce(merge.astype(np.int32), axis=(0, 1))
    o = [np.stack([gtable(v.reshape(8, -1)) for v in w]).astype(np.float32) for w in (g, a, b)]
    return {"og": o[0], "oa": o[1], "ob": o[2], "ox": x.reshape(N, 128, W).astype(np.float32).astype(BF)}

@@ -1,0 +1,472 @@
+import numpy as np
+from concourse.mybir import AluOpType as A, ActivationFunctionType as F
+
+M = 4
+NB = 32 // M
+NE = NB * M * (M - 1) // 2
+f32, f16, bf, i32, u16 = "float32", "float16", "bfloat16", "int32", "uint16"
+SCRATCH = {
+    "win": ("sbuf", [128, 4608], bf), "sv": ("sbuf", [128, 16], bf),
+    "yv0": ("sbuf", [128, 1024], bf), "yv1": ("sbuf", [128, 1024], bf), "yv2": ("sbuf", [128, 1024], bf),
+    "yi1": ("sbuf", [128, 1024], bf), "yi2": ("sbuf", [128, 1024], bf),
+    "gn": ("sbuf", [128, 4, 2, 32], i32), "an": ("sbuf", [128, 4, 2, 32], i32), "bn": ("sbuf", [128, 4, 2, 32], i32),
+    "tn": ("sbuf", [128, 4, 2, 32], i32), "tf0": ("sbuf", [128, 8, 32], f32),
+    "ti1": ("sbuf", [128, 8, 32], f32), "ti2": ("sbuf", [128, 8, 32], f32),
+    "l0": ("sbuf", [128, 384], u16), "l1": ("sbuf", [128, 384], u16), "l2": ("sbuf", [128, 384], u16),
+    "lo1": ("sbuf", [128, 384], u16), "lo2": ("sbuf", [128, 384], u16),
+    "dd": ("sbuf", [128, 6144], bf), "ab": ("sbuf", [128, 6144], bf),
+    "E": ("sbuf", [128, 8, 32], bf), "AE": ("sbuf", [128, 8, 32], bf), "O": ("sbuf", [128, 8, 32], bf),
+    "UX": ("sbuf", [128, 8, 32], bf), "Mf": ("sbuf", [128, 4, 32], bf),
+    "Eo": ("sbuf", [128, 4, 32], bf), "Cb": ("sbuf", [128, 1, 32], bf),
+    "thr": ("sbuf", [128, 8, 32], f32), "dsb": ("sbuf", [128, 8, 32], f32), "mn": ("sbuf", [128, 4, 32], f32),
+    "nv": ("sbuf", [128, 12, 32], f32), "keys": ("sbuf", [128, 12, 32], f16), "fall": ("sbuf", [128, 32], f32),
+    "fallc": ("sbuf", [128, 32], f32), "code": ("sbuf", [128, 32], f16), "BH": ("sbuf", [128, 16, 128], f16), "IH": ("sbuf", [128, 128], f16),
+    "Kb": ("sbuf", [128, 8, 32], bf),
+    "xg": ("sbuf", [128, 512], bf), "zz": ("sbuf", [128, 16, 128], bf), "Tf": ("sbuf", [128, 8, 32], bf), "Ff": ("sbuf", [128, 4, 32], bf), "lgg": ("sbuf", [128, 64], u16), "hi": ("sbuf", [128, 32], bf),
+    "lw": ("sbuf", [128, 32], bf), "own": ("sbuf", [128, 16, NB, M], f32), "eq": ("sbuf", [128, 16, 32], bf), "ee": ("sbuf", [128, 16, NE], bf), "ce": ("sbuf", [128, NE], bf),
+    "gab": ("sbuf", [128, 1024], bf), "vf": ("sbuf", [128, 512], f32), "vals": ("sbuf", [128, 512], bf), "dm": ("sbuf", [128, 32], i32),
+    "dst": ("sbuf", [128, 32], u16),
+    "oab": ("sbuf", [128, 16, 32], f16), "kab": ("sbuf", [128, 16, 32], f16), "mz": ("sbuf", [128, 8, 32], f16),
+    "vz": ("sbuf", [128, 12, 32], f16), "X": ("sbuf", [128, 8, 32], f32),
+    "P": ("sbuf", [128, 8, 32], i32), "H": ("sbuf", [128, 8, 32], i32), "NQ": ("sbuf", [128, 8, 32], i32),
+    "IDX": ("sbuf", [128, 8, 32], i32),
+    "fog": ("sbuf", [128, 8, 32], u16), "foab": ("sbuf", [128, 16, 32], u16),
+    "fig": ("sbuf", [128, 8, 32], u16), "fiab": ("sbuf", [128, 16, 32], u16),
+    "og_": ("sbuf", [128, 4, 2, 32], f32), "oa_": ("sbuf", [128, 4, 2, 32], f32), "ob_": ("sbuf", [128, 4, 2, 32], f32),
+    "ones": ("sbuf", [128, 256], bf), "on5": ("sbuf", [128, 512], bf), "SS": ("sbuf", [128, 2048], bf), "BB": ("sbuf", [128, 16, 128], bf),
+    "MK": ("sbuf", [128, 16, 128], bf), "SG": ("sbuf", [128, 128], bf),
+    "pi": ("sbuf", [128, 1], i32), "pa": ("sbuf", [128, 1], i32), "pb": ("sbuf", [128, 1], i32),
+    "pm": ("sbuf", [128, 1], f32), "pg": ("sbuf", [128, 1], f32), "io8": ("sbuf", [128, 8], f32),
+    "iop": ("sbuf", [128, 8, 16], f32), "bm8": ("sbuf", [128, 8], f32), "ioi": ("sbuf", [128, 32], f32),
+}
+for _n in ("st0", "st1", "st2", "po1", "po2"):
+    SCRATCH[_n] = ("sbuf", [128, 33, 32], f32)
+WB = {"I1": 1, "Im1": -1, "I8k": 8192, "Im8k": -8192, "I16k": 16384, "Im16k": -16384, "I1920": 1920, "I28": 28, "I2k": 2048, "Im2k": -2048}
+WF = {"J1": 1, "Jm1": -1, "Jm101": -101, "Jm129": -129}
+CM = {"c230": -230 / 128, "cm1": -1 / 128, "c2k": 16.0, "cp1": 1 / 128, "cmh": -0.5 / 128, "c8k": 64.0}
+for _n in WB: SCRATCH[_n] = ("sbuf", [128, 128], bf)
+for _n in WF: SCRATCH[_n] = ("sbuf", [128, 128], f32)
+for _n in CM: SCRATCH[_n] = ("sbuf", [128, 128], bf)
+for _n in ("b0", "b3", "b4", "b5", "b6", "b7"): SCRATCH[_n] = ("psum", [128, 16, 32], f32)
+for _n in ("b1", "b2"): SCRATCH[_n] = ("psum", [128, 16, NB, M], f32)
+NDMA = 16
+HELP = True
+ARR = ["yi1", "yi2", "ti1", "ti2", "l1", "l2", "s1a", "s1b", "s1c", "s2a", "s2b", "s2c", "fg", "fab"]
+SEMAPHORES = ["qv", "qs", "qt", "qg", "loc"] + ["d%d" % k for k in range(NDMA)] + ["a_" + n for n in ARR]
+_cache = {}
+
+
+def rank_program(g, core, T, topo):
+    rank = T.rank_of(core)
+    if rank is None:
+        return
+    N = len(T.cores)
+    eng = {"v": g.vector, "s": g.scalar, "t": g.tensor, "g": g, "y": g.sync}
+    cnt = {}
+    known = {q: {} for q in eng}
+    hist = {n: [] for n in SCRATCH}
+
+    def X(name, *idx):
+        key = (name,) + tuple(("s", i.start, i.stop, i.step) if isinstance(i, slice) else i for i in idx)
+        if key not in _cache:
+            shp = SCRATCH[name][1][1:]
+            a = np.arange(int(np.prod(shp))).reshape(shp)[idx].ravel()
+            b = np.zeros(int(np.prod(shp)), np.uint8)
+            b[a] = 1
+            _cache[key] = int.from_bytes(np.packbits(b).tobytes(), "big")
+        return (T[name][(slice(None),) + idx], name, _cache[key])
+
+    def sync(q, rd, wr):
+        need = {}
+        for regs, w in ((rd, False), (wr, True)):
+            for r in regs:
+                psum = SCRATCH[r[1]][0] == "psum"
+                for (m, pw, pq, sem, c, clk) in hist[r[1]]:
+                    if psum and pq != q:
+                        hit = True
+                    elif psum and q == "t":
+                        hit = False
+                    else:
+                        hit = bool(m & r[2]) and (pw or w)
+                    if hit and known[q].get(sem, 0) < c and (sem not in need or need[sem][0] < c):
+                        need[sem] = (c, clk)
+        for sem in sorted(need, key=lambda s: -len(need[s][1])):
+            c, clk = need[sem]
+            if known[q].get(sem, 0) >= c: continue
+            eng[q].wait_ge(T.sem[sem], c)
+            for k in clk: known[q][k] = max(known[q].get(k, 0), clk[k])
+
+    def record(q, rd, wr, sem, c):
+        clk = dict(known[q]); clk[sem] = c
+        for regs, w in ((rd, False), (wr, True)):
+            for r in regs:
+                h = hist[r[1]]
+                if w:
+                    h[:] = [e for e in h if (e[0] & ~r[2]) or clk.get(e[3], 0) < e[4]]
+                else:
+                    h[:] = [e for e in h if e[1] or e[2] != q or (e[0] & ~r[2])]
+                h.append((r[2], w, q, sem, c, clk))
+
+    def emit(q, call, rd, wr):
+        sem = "q" + q
+        sync(q, rd, wr)
+        cnt[sem] = cnt.get(sem, 0) + 1
+        call().then_inc(T.sem[sem], 1)
+        record(q, rd, wr, sem, cnt[sem])
+
+    v, s, te = g.vector, g.scalar, g.tensor
+    def tt(o, a, b, op): emit("v", lambda: v.tensor_tensor(o[0], a[0], b[0], op), [a, b], [o])
+    def ts(o, a, s1, s2, op0, op1=None):
+        sc = [x for x in (s1,) if isinstance(x, tuple)]
+        p1 = s1[0] if sc else s1
+        if op1 is None: emit("v", lambda: v.tensor_scalar(o[0], a[0], p1, None, op0), [a] + sc, [o])
+        else: emit("v", lambda: v.tensor_scalar(o[0], a[0], p1, s2, op0, op1), [a] + sc, [o])
+    def cp(o, a): emit("v", lambda: v.tensor_copy(o[0], a[0]), [a], [o])
+    def ms(o, c): emit("v", lambda: v.memset(o[0], c), [], [o])
+    def act(o, a, f=F.Identity, bias=0.0, scale=1.0):
+        if isinstance(scale, tuple): emit("s", lambda: s.activation(o[0], a[0], f, scale=scale[0]), [a, scale], [o])
+        elif bias == 0.0: emit("s", lambda: s.activation(o[0], a[0], f, scale=scale), [a], [o])
+        else: emit("s", lambda: s.activation(o[0], a[0], f, bias=bias, scale=scale), [a], [o])
+    def mm(o, w, r, first, last): emit("t", lambda: te.matmul(o[0], w[0], r[0], first, last), [w, r], [o])
+    W = lambda n: X(n)
+    ndma = [0]
+    def dma(q, o, a, rd, wr):
+        sem = "d%d" % ndma[0]; ndma[0] += 1
+        sync(q, rd, wr)
+        eng[q].dma_start(o, a).then_inc(T.sem[sem], 16)
+        cnt[sem] = 16
+        record(q, rd, wr, sem, 16)
+    def nengines(a, b): return len(topo.engines(a, b))
+    def send(to, o, i, sem):
+        dst = T.cores[to % N]
+        sync("g", [i], [])
+        rid, pid, _ = topo.addr(dst)
+        cnt["loc"] = cnt.get("loc", 0) + nengines(core, dst)
+        g.remote_dma(o[0], i[0], T.sem["a_" + sem], T.sem.loc, pid, rid, topo.mask(core, dst))
+    def arrives(frm, sem, o):
+        c = nengines(T.cores[frm % N], core)
+        cnt["a_" + sem] = c
+        hist[o[1]].append((o[2], True, "r", "a_" + sem, c, {"a_" + sem: c}))
+    S = slice
+    def rows(n, a, b): return X(n, S(a, b))
+
+    dma("y", T.gn[:], T.gl[:], [], [W("gn")])
+    dma("y", T.win[:, 0:4096], T.xt[:], [], [X("win", S(0, 4096))])
+    for k in (0, 1, 2):
+        if k == 1:
+            for n, src in (("an", T.al), ("bn", T.bl), ("tn", T.th)): dma("y", T[n][:], src[:], [], [W(n)])
+        for h in (0, 1)[:2 if k == 0 else 1]:
+            n = "yv%d" % k
+            dma("y", T[n][:, h * 512:h * 512 + 512], T.yv[:, k * 512:k * 512 + 512], [], [X(n, S(h * 512, h * 512 + 512))])
+    for k in (1, 2):
+        arrives(rank - k, "yi%d" % k, X("yi%d" % k, S(0, 512)))
+        arrives(rank - k, "ti%d" % k, W("ti%d" % k))
+        n = T["yi%d" % k]
+        dma("y", n[:, 512:1024], n[:, 0:512], [X("yi%d" % k, S(0, 512))], [X("yi%d" % k, S(512, 1024))])
+    for k in (1, 2):
+        arrives(rank - 1, "l%d" % k, W("l%d" % k))
+        arrives(rank - 1, "s%da" % k, rows("st%d" % k, 0, 8))
+        arrives(rank - 1, "s%db" % k, rows("st%d" % k, 24, 33))
+        arrives(rank - 1, "s%dc" % k, rows("st%d" % k, 8, 24))
+    arrives(rank + 2, "fg", W("fig")); arrives(rank + 2, "fab", W("fiab"))
+
+    emit("g", lambda: g.iota(T.pi[:], [[0, 1]], 0, 1), [], [W("pi")])
+    ms(W("ones"), 1.0)
+    big = dict(allow_small_or_imprecise_dtypes=True)
+    emit("g", lambda: g.affine_select(T.I1[:], T.ones[:, 0:128], [[-1, 128]], A.is_equal, 0.0, 0, 1), [X("ones", S(0, 128))], [W("I1")])
+    emit("g", lambda: g.iota(T.io8[:], [[1, 8]], 0, 0, **big), [], [W("io8")])
+    emit("g", lambda: g.iota(T.iop[:], [[0, 8], [1, 16]], 0, 0, **big), [], [W("iop")])
+    emit("g", lambda: g.iota(T.ioi[:], [[16, 32]], 2048, 0, **big), [], [W("ioi")])
+    ms(W("zz"), 0.0)
+    emit("g", lambda: g.affine_select(T.BB[:], T.zz[:], [[-1, 16], [-16, 8], [0, 16]], A.not_equal, 1.0, 0, 1), [W("zz")], [W("BB")])
+    for n in CM: ms(W(n), CM[n])
+    ts(W("pa"), W("pi"), 15, None, A.bitwise_and)
+    ts(W("pb"), W("pi"), 4, None, A.arith_shift_right)
+    cp(W("pm"), W("pa")); cp(W("pg"), W("pb"))
+    ts(W("bm8"), W("io8"), W("pg"), None, A.is_equal)
+    ts(W("SG"), W("iop"), W("pm"), None, A.is_equal)
+    ts(W("fall"), W("ioi"), W("pm"), None, A.add)
+    ts(W("fallc"), W("fall"), 2.0, -2046.0, A.mult, A.add)
+    cp(W("IH"), W("I1"))
+    for n in ("J1", "Jm1", "Jm101", "Jm129"): act(W(n), W("I1"), F.Identity, scale=float(WF[n]))
+    for n in ("I1920", "I28"): act(W(n), W("I1"), F.Identity, scale=float(WB[n]))
+
+    def pieces(sh): return {0: [(0, 4, 0)], 1: [(0, 3, 1), (3, 4, 0)], -1: [(1, 4, 0), (0, 1, 3)]}[sh]
+    def add(bank, base, w, src, sbase, sh, first=False, last=False):
+        ps = pieces(sh)
+        for j, (a, b, c) in enumerate(ps):
+            mm(rows(bank, base + a, base + b), W(w), rows(src, sbase + c, sbase + c + b - a), first and j == 0, last and j == len(ps) - 1)
+
+    def index_stage(po, lo, meanwhile=None, goals=None, pair=None):
+        ts(rows("X", 4, 8), rows("b7", 0, 4), -2047.0, -4127.0, A.is_equal, A.mult)
+        act(rows(po, 0, 4), rows("b7", 0, 4), F.Identity, bias=-1.0)
+        act(W("Eo"), rows("b7", 0, 4), F.Relu, bias=-2046.0, scale=-1.0)
+        ts(X(lo, S(0, 128)), rows("b6", 0, 4), -1.0, 2048.0, A.mult, A.add)
+        tt(rows("P", 4, 7), rows("X", 4, 7), rows("b6", 1, 4), A.mult)
+        tt(rows("P", 7, 8), rows("X", 7, 8), rows("b6", 0, 1), A.mult)
+        act(rows("X", 0, 4), rows("b6", 0, 4), F.Identity, bias=2048.0)
+        act(rows(po, 4, 8), rows("b6", 0, 4), F.Identity, bias=-1.0)
+        if meanwhile: meanwhile()
+        tt(rows("P", 0, 4), rows("X", 0, 4), rows("b7", 0, 4), A.mult)
+        one = X("ones", S(0, 128))
+        mm(rows("b5", 4, 8), W("cm1"), one, True, False)
+        mm(rows("b5", 4, 8), W("c2k"), one, False, False)
+        add("b5", 4, "Jm1", po, 0, 0)
+        add("b5", 4, "I1920", "Eo", 0, 0)
+        add("b5", 4, "I28", "Eo", 0, 0, last=True)
+        mm(rows("b5", 0, 4), W("c230"), one, True, False)
+        add("b5", 0, "Jm129", po, 0, 0)
+        add("b5", 0, "Jm101", po, 4, 0, last=True)
+        ts(W("H"), W("P"), 5, None, A.arith_shift_right)
+        if goals: goals()
+        tt(W("NQ"), W("H"), rows("b5", 0, 8), A.add)
+        ts(W("IDX"), W("NQ"), 4095, None, A.bitwise_and)
+        if pair: pair(3)
+        cp(X(lo, S(128, 384)), W("IDX"))
+
+    def index_rest(po):
+        ts(rows(po, 8, 16), W("IDX"), -1.0, 2047.0, A.mult, A.add)
+
+    for h in (0, 1): ts(rows("b%d" % (6 + h), 0, 4), X("gn", S(0, 4), h), -1.0, 2048.0, A.mult, A.add)
+    index_stage("st0", "l0")
+    act(W("SS"), W("zz"), F.Copy)
+    for e in range(8):
+        act(X("SS", S(16 * e, 16 * e + 129 * 15 + 1, 129)), X("ones", S(0, 16)), F.Identity, scale=X("bm8", S(e, e + 1)))
+    for n in ("Im1", "I8k", "Im8k", "I16k", "Im16k", "I2k", "Im2k"): act(W(n), W("I1"), F.Identity, scale=float(WB[n]))
+    def home_rest():
+        index_rest("st0")
+        for n, b in (("an", 24), ("bn", 16)):
+            for h in (0, 1): ts(rows("st0", b + 4 * h, b + 4 * h + 4), X(n, S(0, 4), h), -1.0, 2047.0, A.mult, A.add)
+        for h in (0, 1): cp(rows("tf0", 4 * h, 4 * h + 4), X("tn", S(0, 4), h))
+        for k in (1, 2): send(rank + k, W("ti%d" % k), W("tf0"), "ti%d" % k)
+    for k in (1, 2): send(rank + k, X("yi%d" % k, S(0, 512)), X("yv%d" % k, S(0, 512)), "yi%d" % k)
+    def goal_constants():
+        act(W("on5"), X("zz", S(0, 4)), F.Identity, bias=1.0)
+        emit("g", lambda: g.affine_select(T.MK[:], T.zz[:], [[0, 16], [-16, 8], [-1, 16]], A.not_equal, 8192.0, 0, 1), [W("zz")], [W("MK")])
+        emit("g", lambda: g.affine_select(T.MK[:], T.MK[:], [[-1, 16], [0, 8], [1, 16]], A.is_gt, 0.0, 0, 0), [W("MK")], [W("MK")])
+    cp(W("BH"), W("BB"))
+    cp(X("sv", S(0, 1)), X("win", S(4095, 4096)))
+    ms(X("win", S(4095, 4096)), 512.0)
+
+    CALLS = [(0, 64), (64, 64), (256, 64), (320, 64), (128, 64), (192, 32 if HELP else 64)]
+    def visit(t):
+        st, ls, yv, th = "st%d" % t, "l%d" % t, ("yi%d" % t if t else "yv0"), ("ti%d" % t if t else "tf0")
+
+        def gather(c, n):
+            e = 16 * n
+            o, off, vw, wn = X("dd", S(16 * c, 16 * c + e)), X(ls, S(c, c + n)), X(yv, S(0, e)), X("win", S(0, 4096))
+            emit("v", lambda: v.tensor_tensor(o[0], T.win[:, 0:4096].indirect(off[0]), vw[0], A.subtract), [wn, off, vw], [o])
+        def size(c, n): act(X("ab", S(16 * c, 16 * c + 16 * n)), X("dd", S(16 * c, 16 * c + 16 * n)), F.Abs)
+        def total(c, n):
+            bank, r0 = ("b1", (c - 128) // 32) if 128 <= c < 256 else ("b0", c // 32 if c < 128 else c // 32 - 4)
+            for j in range(16):
+                mm(rows(bank, r0, r0 + n // 32), X("SS", S(128 * j, 128 * j + 128)), X("ab", S(16 * c + j, 16 * c + 16 * n, 16)),
+                   j == 0 and bank == "b0", j == 15 and (bank == "b0" or c == 192))
+        def prep_a():
+            act(rows("E", 0, 4), rows(st, 4, 8), F.Relu, bias=-2047.0, scale=-1.0)
+            act(rows("E", 4, 8), rows(st, 0, 4), F.Relu, bias=-2047.0, scale=-1.0)
+            mm(rows("b6", 0, 8), W("I16k"), rows("E", 0, 8), True, False)
+            add("b6", 0, "Im16k", "E", 4, 0)
+            add("b6", 4, "Im16k", "E", 0, 1)
+            if t == 1:
+                add("b6", 0, "J1", th, 4, 0); add("b6", 4, "J1", th, 0, 1)
+            else:
+                mm(rows("b6", 0, 8), W("J1"), rows(th, 0, 8), False, False)
+        def prep_b():
+            act(W("AE"), rows(st, 24, 32), F.Relu, bias=-2047.0, scale=-1.0)
+            if t: act(W("Cb"), rows(st, 32, 33), F.Copy)
+            mm(rows("b6", 0, 8), W("I16k"), rows("AE", 0, 8), False, t == 0)
+            if t:
+                for k in range(8): mm(rows("b6", k, k + 1), W("I1"), W("Cb"), False, k == 7)
+
+        one, o1 = X("ones", S(0, 256)), X("ones", S(0, 128))
+        def empty_gates():
+            mm(rows("b3", 0, 4), W("Im1"), rows("E", 0, 4), True, False)
+            mm(rows("b2", 0, 8), W("I1"), W("E"), True, False)
+            add("b2", 4, "Im1", "E", 0, 1)
+            mm(rows("b4", 0, 12), W("I1"), X("zz", S(0, 3)), True, False)
+            mm(rows("b4", 0, 4), W("I1"), o1, False, False)
+            mm(rows("b4", 8, 12), W("I1"), o1, False, False)
+            add("b4", 8, "Im1", "E", 4, 0)
+        def open_gates():
+            add("b3", 0, "Im1", "O", 4, 0)
+            add("b2", 0, "Im1", "O", 4, -1)
+            add("b2", 4, "Im1", "O", 0, 0)
+            add("b4", 0, "Im1", "O", 0, 0)
+            add("b4", 8, "Im1", "O", 4, 0)
+        de, do = (0, 1) if t == 0 else (-1, 0) if t == 1 else (0, 0)
+        be, bo = ("b7", "b6") if t < 2 else ("b6", "b7")
+        def places_0():
+            for bank in (be, bo):
+                mm(rows(bank, 0, 4), W("cp1"), o1, True, False)
+        def places_e():
+            add(be, 0, "IH", "oab", 8, do)
+            add(be, 0, "IH", "oab", 4, do - 1)
+            add(be, 0, "I2k", "O", 4, do - 1)
+        def places_o():
+            add(bo, 0, "IH", "oab", 12, de)
+            add(bo, 0, "IH", "oab", 0, de)
+            add(bo, 0, "I2k", "O", 0, de)
+            add(bo, 0, "Im2k", "E", 4, de)
+        if HELP:
+            off0 = X(ls, S(224, 256))
+            emit("s", lambda: s.activation(T.xg[:], T.win[:, 0:4096].indirect(off0[0]), F.Copy), [X("win", S(0, 4096)), off0], [W("xg")])
+        for k, (c, n) in enumerate(CALLS):
+            gather(c, n)
+            if k == 1 and t == 0:
+                home_rest()
+                goal_constants()
+            if k == 4:
+                tt(W("O"), rows("b0", 0, 8), W("thr"), A.is_gt)
+                mm(rows("b5", 0, 8), W("I1"), W("O"), True, True)
+                mm(rows("b5", 8, 16), W("I1"), W("O"), True, True)
+            if k == len(CALLS) - 1: tt(W("oab"), W("b5"), rows(st, 16, 32), A.mult)
+            if k == 3: prep_b()
+            size(c, n)
+            if k == 2: prep_a()
+            if k == 4:
+                act(W("dsb"), rows("b0", 0, 8), F.Copy)
+                mm(rows("b1", 0, 4), W("I8k"), rows("E", 4, 8), True, False)
+            if k == 0 and HELP:
+                mm(W("b4"), W("I1"), W("xg"), True, False)
+                mm(W("b4"), W("Im1"), X(yv, S(0, 512)), False, True)
+            if k == 1 and HELP: act(X("ab", S(16 * 224, 16 * 256)), W("b4"), F.Abs)
+            if k < 5: total(c, n)
+            if k == 3:
+                act(W("thr"), rows("b6", 0, 8), F.Identity, bias=16384.0)
+                empty_gates()
+            if k == 4: open_gates()
+        act(W("nv"), rows(st, 0, 12), F.Identity, bias=-1.0, scale=-1.0)
+        total(192, 64)
+        places_0()
+        tt(W("mn"), rows("b0", 0, 4), rows("dsb", 4, 8), A.min)
+        tt(rows("UX", 4, 7), rows("b0", 4, 7), rows("dsb", 1, 4), A.is_lt)
+        tt(rows("UX", 7, 8), rows("b0", 7, 8), rows("dsb", 0, 1), A.is_lt)
+        add("b2", 4, "I1", "UX", 4, 0)
+        tt(rows("UX", 0, 4), rows("b1", 0, 4), W("mn"), A.is_lt)
+        add("b3", 0, "I1", "UX", 0, 0, last=True)
+        add("b2", 0, "I1", "UX", 0, 0, last=True)
+        ts(W("Mf"), rows("b3", 0, 4), 0.0, None, A.max)
+        act(W("Tf"), rows("b2", 0, 8), F.Relu, bias=-1.0)
+        if t < 2: places_e()
+        mm(rows("b3", 4, 8), W("I1"), W("Mf"), True, False)
+        for k in (1, 2, 3): mm(rows("b3", 4 + k, 8), W("Im1"), rows("Mf", 0, 4 - k), False, k == 3)
+        act(W("Ff"), rows("b3", 4, 8), F.Relu)
+        add("b4", 0, "Im1", "Mf", 0, 0)
+        add("b4", 4, "I1", "Mf", 0, 0)
+        add("b4", 8, "Im1", "Mf", 0, 0)
+        mm(rows("b4", 4, 12), W("I1"), W("Tf"), False, True)
+        if t < 2: places_o()
+        for k in range(3): mm(rows("b2", 4 * k, 4 * k + 4), W("I1"), W("Ff"), True, True)
+        for k in range(2): mm(rows("b5", 8 + 4 * k, 12 + 4 * k), W("I1"), W("Mf"), True, True)
+        tt(W("vz"), rows("b4", 0, 12), rows(st, 4, 16), A.mult)
+        tt(W("keys"), rows("b2", 0, 12), W("nv"), A.mult)
+        def places_b():
+            add(be, 0, "I2k", "Tf", 0, do)
+            add(bo, 0, "I2k", "Tf", 4, de)
+            add(bo, 0, "Im2k", "Mf", 0, de)
+            add(be, 0, "IH", "vz", 0, do)
+            add(be, 0, "IH", "vz", 4, do, last=True)
+            add(bo, 0, "IH", "vz", 8, de, last=True)
+        if t < 2: places_b()
+        for a in range(4): mm(rows("b3", 8, 11), W("IH"), X("keys", S(a, 12, 4)), a == 0, False)
+        mm(rows("b3", 10, 11), W("c8k"), X("ones", S(0, 32)), False, False)
+        for a in range(4): mm(rows("b3", 10, 11), W("Im8k"), rows("Ff", a, a + 1), False, a == 3)
+        def first_goals():
+            tt(W("code"), rows("b3", 10, 11), W("fallc"), A.min)
+            for k in range(4): tt(X("own", k), rows("b3", 10, 11), W("fallc"), A.min)
+            ts(W("lgg"), rows("b3", 8, 10), 2048.0, None, A.add)
+            for k in (4, 8): act(rows("own", k, 2 * k), rows("own", 0, k), F.Copy)
+        def keeps():
+            mm(rows("b3", 4, 12), W("I1"), one, True, False)
+            mm(rows("b3", 4, 12), W("Im1"), W("O"), False, False)
+            mm(rows("b3", 4, 12), W("Im1"), W("Tf"), False, False)
+            add("b3", 4, "Im1", "Mf", 0, 0)
+            add("b3", 4, "Im1", "O", 4, -1)
+            add("b3", 8, "Im1", "O", 0, 0)
+            add("b3", 8, "Im1", "Mf", 0, 0, last=True)
+            if t < 2:
+                for a in range(4): mm(rows("b3", 12, 13), W("SG"), rows("Mf", a, a + 1), a == 0, a == 3)
+        def memories():
+            tt(rows("kab", 0, 8), rows("b3", 4, 12), rows(st, 16, 24), A.mult)
+            tt(rows("kab", 8, 16), rows("b3", 4, 12), rows(st, 24, 32), A.mult)
+            tt(rows("mz", 0, 8), rows("b5", 8, 16), rows(st, 0, 8), A.mult)
+            act(W("Kb"), rows("b3", 4, 12), F.Copy)
+        def memory_sums():
+            for j, mzr in ((0, 0), (1, 4)):
+                ev, od = (4, 0) if t < 2 else (0, 4)
+                se, so = (do, de) if t < 2 else (0, 0)
+                for (a, b, c) in pieces(se):
+                    r = rows("b0", 8 * j + ev + a, 8 * j + ev + b)
+                    mm(r, W("IH"), rows("kab", 8 * j + c, 8 * j + c + b - a), True, False)
+                    mm(r, W("I2k"), rows("Kb", c, c + b - a), False, False)
+                    mm(r, W("IH"), rows("mz", mzr + c, mzr + c + b - a), False, False)
+                    mm(r, W("I2k"), rows("Mf", c, c + b - a), False, True)
+                for (a, b, c) in pieces(so):
+                    r = rows("b0", 8 * j + od + a, 8 * j + od + b)
+                    mm(r, W("IH"), rows("kab", 8 * j + 4 + c, 8 * j + 4 + c + b - a), True, False)
+                    mm(r, W("I2k"), rows("Kb", 4 + c, 4 + c + b - a), False, True)
+        def goals():
+            for j in range(16):
+                mm(X("b1", j), X("BH", j), W("code"), True, True)
+        ec = [NB * (M * (e - 1) - e * (e - 1) // 2) for e in range(M + 1)]
+        def pair(e):
+            if e == 0: tt(W("eq"), rows("b1", 0, 16), rows("own", 0, 16), A.is_equal)
+            else: tt(X("ee", S(0, 16), S(ec[e], ec[e + 1])), X("b1", S(0, 16), S(0, NB), S(0, M - e)), X("own", S(0, 16), S(0, NB), S(e, M)), A.is_equal)
+        out = "po%d" % (t + 1)
+        if t < 2:
+            index_stage(out, "lo%d" % (t + 1), first_goals, goals, pair)
+            send(rank + 1, W("l%d" % (t + 1)), W("lo%d" % (t + 1)), "l%d" % (t + 1))
+            keeps()
+        else:
+            first_goals()
+            keeps()
+            places_e(); places_o()
+            goals()
+            places_b()
+            memories()
+            memory_sums()
+            for h in (0, 1): ts(rows("fog", 4 * h, 4 * h + 4), rows("b%d" % (6 + h), 0, 4), -1.0, 2048.0, A.mult, A.add)
+            send(rank - 2, W("fig"), W("fog"), "fg")
+        off = X("lgg", S(0, 64))
+        emit("s", lambda: s.activation(T.gab[:], T.win[:, 0:4096].indirect(off[0]), F.Copy), [X("win", S(0, 4096)), off], [W("gab")])
+        pe = X("b7" if t < 2 else "b5", S(8, 10), S(0, NE // 2))
+        def count(lo, hi):
+            for j in range(lo, min(hi, 15)): mm(X("b2", 0), X("MK", j), X("eq", j), False, False)
+            for j in range(lo, hi): mm(pe, W("I1"), X("ee", j), j == 0, j == 15)
+        mm(X("b2", 0), W("IH"), W("code"), True, False)
+        mm(W("b4"), W("cmh"), W("on5"), True, False)
+        for h in (0, 1): mm(W("b4"), W("I1"), X("gab", S(512 * h, 512 * h + 512)), False, h == 1)
+        act(W("vf"), W("b4"), F.Identity, bias=8388608.0, scale=0.5)
+        act(W("vals"), W("vf"), F.Identity, bias=-8388608.0)
+        for e in (0, 1, 2) if t < 2 else (0, 1, 2, 3): pair(e)
+        count(0, 16)
+        if t < 2:
+            send(rank + 1, rows("st%d" % (t + 1), 0, 8), rows(out, 0, 8), "s%da" % (t + 1))
+            memories()
+        else:
+            ts(W("foab"), W("b0"), -1.0, 4095.0, A.mult, A.add)
+            send(rank - 2, W("fiab"), W("foab"), "fab")
+        cp(W("ce"), pe)
+        for e in range(1, M): mm(X("b2", 0, S(0, NB), S(e, M)), W("I8k"), X("ce", S(ec[e], ec[e + 1])), False, e == M - 1)
+        if t < 2:
+            index_rest(out)
+            memory_sums()
+            act(rows(out, 24, 32), rows("b0", 8, 16), F.Identity, bias=-2048.0)
+            act(rows(out, 32, 33), rows("b3", 12, 13), F.Copy)
+            send(rank + 1, rows("st%d" % (t + 1), 24, 33), rows(out, 24, 33), "s%db" % (t + 1))
+            act(rows(out, 16, 24), rows("b0", 0, 8), F.Identity, bias=-2048.0)
+            send(rank + 1, rows("st%d" % (t + 1), 8, 24), rows(out, 8, 24), "s%dc" % (t + 1))
+        for u in range(M):
+            ts(X("dst", S(u, 32, M)), X("b2", 0, S(0, NB), u), X("fall", S(u, u + 1)), 2048.0, A.min, A.add)
+        for q in range(NB - 1, -1, -1):
+            off2, va, wn = X("dst", S(q * M, q * M + M)), X("vals", S(16 * M * q, 16 * M * (q + 1))), W("win")
+            emit("v", lambda: v.tensor_copy(T.win[:, 0:4608].indirect(off2[0]), va[0]), [off2, va], [wn])
+
+    for t in range(3): visit(t)
+    cp(X("win", S(4095, 4096)), X("sv", S(0, 1)))
+    dma("y", T.ox[:], T.win[:, 0:4096], [X("win", S(0, 4096))], [])
+    for src, r0, buf, dst in (("fig", 0, "og_", T.og), ("fiab", 8, "oa_", T.oa), ("fiab", 0, "ob_", T.ob)):
+        for h in (0, 1): cp(X(buf, S(0, 4), h), rows(src, r0 + 4 * h, r0 + 4 * h + 4))
+        dma("y" if buf == "ob_" else "s", dst[:], T[buf][:], [W(buf)], [])
+    for sem in cnt: g.wait_ge(T.sem[sem], cnt[sem])

@@ -1,59 +1,80 @@
 import numpy as np
 from concourse.mybir import AluOpType as A, ActivationFunctionType as F
 
-M = 4
-NB = 32 // M
-NE = NB * M * (M - 1) // 2
 f32, f16, bf, i32, u16 = "float32", "float16", "bfloat16", "int32", "uint16"
+PIECES = (1, 0)
+BY_SCALAR = {1: (4,), 0: ()}
+COPIES = 0
+CHUNK, CROSS_Q, BC = {1: 1, 0: 2}, "s", "XV"
+AE_Q = "vvs"
+VAL_Q = ("ss", "sv")
+WB = {"Im1": -1, "Ih": 0.5, "I8k": 8192, "Im8k": -8192, "I16k": 16384, "Im16k": -16384, "Im32k": -32768, "Imag": 12582912,
+      "I64k": 65536, "Im3232": -3232, "Im4096": -4096, "Im31": -31, "Im32": -32, "Im2080": -2080, "H62k": 62336}
 SCRATCH = {
-    "win": ("sbuf", [128, 4608], bf), "sv": ("sbuf", [128, 16], bf),
-    "yv0": ("sbuf", [128, 1024], bf), "yv1": ("sbuf", [128, 1024], bf), "yv2": ("sbuf", [128, 1024], bf),
-    "yi1": ("sbuf", [128, 1024], bf), "yi2": ("sbuf", [128, 1024], bf),
+    "win0": ("sbuf", [128, 4752], bf),
+    "yr0": ("sbuf", [128, 1024], bf), "yr1": ("sbuf", [128, 1024], bf), "yr2": ("sbuf", [128, 1024], bf),
+    "yo": ("sbuf", [128, 2, 512], bf),
     "gn": ("sbuf", [128, 4, 2, 32], i32), "an": ("sbuf", [128, 4, 2, 32], i32), "bn": ("sbuf", [128, 4, 2, 32], i32),
-    "tn": ("sbuf", [128, 4, 2, 32], i32), "tf0": ("sbuf", [128, 8, 32], f32),
-    "ti1": ("sbuf", [128, 8, 32], f32), "ti2": ("sbuf", [128, 8, 32], f32),
-    "l0": ("sbuf", [128, 384], u16), "l1": ("sbuf", [128, 384], u16), "l2": ("sbuf", [128, 384], u16),
-    "lo1": ("sbuf", [128, 384], u16), "lo2": ("sbuf", [128, 384], u16),
-    "dd": ("sbuf", [128, 6144], bf), "ab": ("sbuf", [128, 6144], bf),
-    "E": ("sbuf", [128, 8, 32], bf), "AE": ("sbuf", [128, 8, 32], bf), "O": ("sbuf", [128, 8, 32], bf),
-    "UX": ("sbuf", [128, 8, 32], bf), "Mf": ("sbuf", [128, 4, 32], bf),
-    "Eo": ("sbuf", [128, 4, 32], bf), "Cb": ("sbuf", [128, 1, 32], bf),
-    "thr": ("sbuf", [128, 8, 32], f32), "dsb": ("sbuf", [128, 8, 32], f32), "mn": ("sbuf", [128, 4, 32], f32),
-    "nv": ("sbuf", [128, 12, 32], f32), "keys": ("sbuf", [128, 12, 32], f16), "fall": ("sbuf", [128, 32], f32),
-    "fallc": ("sbuf", [128, 32], f32), "code": ("sbuf", [128, 32], f16), "BH": ("sbuf", [128, 16, 128], f16), "IH": ("sbuf", [128, 128], f16),
-    "Kb": ("sbuf", [128, 8, 32], bf),
-    "xg": ("sbuf", [128, 512], bf), "zz": ("sbuf", [128, 16, 128], bf), "Tf": ("sbuf", [128, 8, 32], bf), "Ff": ("sbuf", [128, 4, 32], bf), "lgg": ("sbuf", [128, 64], u16), "hi": ("sbuf", [128, 32], bf),
-    "lw": ("sbuf", [128, 32], bf), "own": ("sbuf", [128, 16, NB, M], f32), "eq": ("sbuf", [128, 16, 32], bf), "ee": ("sbuf", [128, 16, NE], bf), "ce": ("sbuf", [128, NE], bf),
-    "gab": ("sbuf", [128, 1024], bf), "vf": ("sbuf", [128, 512], f32), "vals": ("sbuf", [128, 512], bf), "dm": ("sbuf", [128, 32], i32),
-    "dst": ("sbuf", [128, 32], u16),
-    "oab": ("sbuf", [128, 16, 32], f16), "kab": ("sbuf", [128, 16, 32], f16), "mz": ("sbuf", [128, 8, 32], f16),
-    "vz": ("sbuf", [128, 12, 32], f16), "X": ("sbuf", [128, 8, 32], f32),
-    "P": ("sbuf", [128, 8, 32], i32), "H": ("sbuf", [128, 8, 32], i32), "NQ": ("sbuf", [128, 8, 32], i32),
-    "IDX": ("sbuf", [128, 8, 32], i32),
-    "fog": ("sbuf", [128, 8, 32], u16), "foab": ("sbuf", [128, 16, 32], u16),
-    "fig": ("sbuf", [128, 8, 32], u16), "fiab": ("sbuf", [128, 16, 32], u16),
+    "tn": ("sbuf", [128, 4, 2, 32], i32),
+    "th0": ("sbuf", [128, 8, 32], f16), "th1": ("sbuf", [128, 8, 32], f16), "th2": ("sbuf", [128, 8, 32], f16),
     "og_": ("sbuf", [128, 4, 2, 32], f32), "oa_": ("sbuf", [128, 4, 2, 32], f32), "ob_": ("sbuf", [128, 4, 2, 32], f32),
-    "ones": ("sbuf", [128, 256], bf), "on5": ("sbuf", [128, 512], bf), "SS": ("sbuf", [128, 2048], bf), "BB": ("sbuf", [128, 16, 128], bf),
-    "MK": ("sbuf", [128, 16, 128], bf), "SG": ("sbuf", [128, 128], bf),
-    "pi": ("sbuf", [128, 1], i32), "pa": ("sbuf", [128, 1], i32), "pb": ("sbuf", [128, 1], i32),
-    "pm": ("sbuf", [128, 1], f32), "pg": ("sbuf", [128, 1], f32), "io8": ("sbuf", [128, 8], f32),
-    "iop": ("sbuf", [128, 8, 16], f32), "bm8": ("sbuf", [128, 8], f32), "ioi": ("sbuf", [128, 32], f32),
+    "ones": ("sbuf", [128, 256], bf), "I1": ("sbuf", [128, 128], bf), "Z": ("sbuf", [128, 144], bf), "SG": ("sbuf", [128, 128], bf),
+    "BB": ("sbuf", [128, 16, 128], bf), "d0c": ("sbuf", [128, 384], bf), "cf": ("sbuf", [128, 16], f32),
+    "ZI": ("sbuf", [128, 144], bf), "J1": ("sbuf", [128, 128], f32),
+    "WD": ("sbuf", [128, 15, 128], bf), "pi": ("sbuf", [128, 2], i32), "rm": ("sbuf", [128, 128], f32), "pm": ("sbuf", [128, 1], f32),
+    "fb": ("sbuf", [128, 5], f32), "iod": ("sbuf", [128, 320], f32),
+    "pof": ("sbuf", [128, 64], f16), "pgc": ("sbuf", [128, 128], bf), "pdd": ("sbuf", [128, 2, 256], f16),
+    "d0g": ("sbuf", [128, 128], f32), "d0d": ("sbuf", [128, 256], bf), "d0p": ("sbuf", [128, 512], f16), "d0a": ("sbuf", [128, 400], f16),
 }
-for _n in ("st0", "st1", "st2", "po1", "po2"):
-    SCRATCH[_n] = ("sbuf", [128, 33, 32], f32)
-WB = {"I1": 1, "Im1": -1, "I8k": 8192, "Im8k": -8192, "I16k": 16384, "Im16k": -16384, "I1920": 1920, "I28": 28, "I2k": 2048, "Im2k": -2048}
-WF = {"J1": 1, "Jm1": -1, "Jm101": -101, "Jm129": -129}
-CM = {"c230": -230 / 128, "cm1": -1 / 128, "c2k": 16.0, "cp1": 1 / 128, "cmh": -0.5 / 128, "c8k": 64.0}
-for _n in WB: SCRATCH[_n] = ("sbuf", [128, 128], bf)
-for _n in WF: SCRATCH[_n] = ("sbuf", [128, 128], f32)
-for _n in CM: SCRATCH[_n] = ("sbuf", [128, 128], bf)
-for _n in ("b0", "b3", "b4", "b5", "b6", "b7"): SCRATCH[_n] = ("psum", [128, 16, 32], f32)
-for _n in ("b1", "b2"): SCRATCH[_n] = ("psum", [128, 16, NB, M], f32)
-NDMA = 16
-HELP = True
-ARR = ["yi1", "yi2", "ti1", "ti2", "l1", "l2", "s1a", "s1b", "s1c", "s2a", "s2b", "s2c", "fg", "fab"]
+for _n in WB: SCRATCH[_n] = ("sbuf", [128, 128], f16 if _n[0] == "H" else bf)
+for _p in PIECES:
+    for _n, _w, _d in (("dq", 3072, bf), ("ab", 3072, bf), ("w8", 128, f16), ("ae", 128, bf), ("dsb", 128, f16), ("mn", 64, f16),
+                       ("sO", 128, bf), ("sM", 64, bf), ("sT", 128, bf), ("kn", 128, bf), ("gc", 128, f16), ("off", 16, u16),
+                       ("dst", 32, u16), ("ge", 256, f16), ("go", 256, bf), ("vals", 256, bf),
+                       ("gs", 512, f16), ("P", 128, f32), ("Q", 128, i32), ("IDX", 128, i32),
+                       ("li0", 192, u16), ("li1", 192, u16), ("li2", 192, u16), ("lo1", 192, u16), ("lo2", 192, u16),
+                       ("si0", 592, f16), ("si1", 592, f16), ("si2", 592, f16), ("si3", 592, f16),
+                       ("so1", 592, f16), ("so2", 592, f16), ("so3", 592, f16)):
+        SCRATCH[_n + str(_p)] = ("sbuf", [128, _w], _d)
+    for _n in ("da", "dr"): SCRATCH[_n + str(_p)] = ("sbuf", [128, 384], f32)
+for _n in ("XV", "DB", "GA", "GB", "GP", "AB", "HS"): SCRATCH[_n] = ("psum", [128, 512], f32)
+SCRATCH["DD"] = ("psum", [128, 32, 16], f32)
+NDMA = 30
+ARR = ["yr1", "yr2", "th1", "th2"] + [n + str(p) for n in ("li1", "li2", "si1", "si2", "si3") for p in PIECES]
 SEMAPHORES = ["qv", "qs", "qt", "qg", "loc"] + ["d%d" % k for k in range(NDMA)] + ["a_" + n for n in ARR]
 _cache = {}
+CY, WAKE, HOP = 0.83e-3, 0.15, 4.0
+
+
+def plan(ops):
+    n = len(ops)
+    succ = [[] for _ in ops]
+    for k, o in enumerate(ops):
+        for d in o["dep"]: succ[d].append(k)
+    def lat(d, k): return 0.0 if ops[d]["q"] == "t" and ops[k]["q"] == "t" else WAKE + ops[d]["lat"]
+    way = [0.0] * n
+    for k in range(n - 1, -1, -1):
+        way[k] = ops[k]["cost"] + max([way[j] + lat(k, j) for j in succ[k]] + [ops[k]["lat"]])
+    left = [len(o["dep"]) for o in ops]
+    ready = {q: {} for q in "vstgyr"}
+    free = {q: 0.0 for q in ready}
+    end = [0.0] * n
+    for k in range(n):
+        if not left[k]: ready[ops[k]["q"]][k] = 0.0
+    order = []
+    while len(order) < n:
+        t0, q = min((max(free[q], min(ready[q].values())), q) for q in ready if ready[q])
+        k = max((k for k in ready[q] if ready[q][k] <= t0 + SLACK), key=lambda k: (ops[k].get("rank", way[k]), -k))
+        start = max(free[q], ready[q].pop(k))
+        end[k] = start + ops[k]["cost"]
+        if q != "r": free[q] = end[k]
+        order.append((start, len(order), k))
+        for j in succ[k]:
+            left[j] -= 1
+            if not left[j]: ready[ops[j]["q"]][j] = max(end[d] + lat(d, j) for d in ops[j]["dep"])
+    return [k for _, _, k in order]
+SLACK = 0.05
+GC, PE = 1.5, 0.5
 
 
 def rank_program(g, core, T, topo):
@@ -62,9 +83,8 @@ def rank_program(g, core, T, topo):
         return
     N = len(T.cores)
     eng = {"v": g.vector, "s": g.scalar, "t": g.tensor, "g": g, "y": g.sync}
-    cnt = {}
-    known = {q: {} for q in eng}
-    hist = {n: [] for n in SCRATCH}
+    ops, hist, runs = [], {n: [] for n in SCRATCH}, {}
+    S = slice
 
     def X(name, *idx):
         key = (name,) + tuple(("s", i.start, i.stop, i.step) if isinstance(i, slice) else i for i in idx)
@@ -73,400 +93,325 @@ def rank_program(g, core, T, topo):
             a = np.arange(int(np.prod(shp))).reshape(shp)[idx].ravel()
             b = np.zeros(int(np.prod(shp)), np.uint8)
             b[a] = 1
-            _cache[key] = int.from_bytes(np.packbits(b).tobytes(), "big")
-        return (T[name][(slice(None),) + idx], name, _cache[key])
+            _cache[key] = (int.from_bytes(np.packbits(b).tobytes(), "big"), int(a.size))
+        return (T[name][(slice(None),) + idx], name) + _cache[key]
 
-    def sync(q, rd, wr):
-        need = {}
+    def put(q, call, rd, wr, cost, lat=0.03, sem=None, inc=1, after=()):
+        k, dep = len(ops), set(after)
         for regs, w in ((rd, False), (wr, True)):
             for r in regs:
-                psum = SCRATCH[r[1]][0] == "psum"
-                for (m, pw, pq, sem, c, clk) in hist[r[1]]:
-                    if psum and pq != q:
-                        hit = True
-                    elif psum and q == "t":
-                        hit = False
-                    else:
-                        hit = bool(m & r[2]) and (pw or w)
-                    if hit and known[q].get(sem, 0) < c and (sem not in need or need[sem][0] < c):
-                        need[sem] = (c, clk)
-        for sem in sorted(need, key=lambda s: -len(need[s][1])):
-            c, clk = need[sem]
-            if known[q].get(sem, 0) >= c: continue
-            eng[q].wait_ge(T.sem[sem], c)
-            for k in clk: known[q][k] = max(known[q].get(k, 0), clk[k])
-
-    def record(q, rd, wr, sem, c):
-        clk = dict(known[q]); clk[sem] = c
-        for regs, w in ((rd, False), (wr, True)):
-            for r in regs:
-                h = hist[r[1]]
-                if w:
-                    h[:] = [e for e in h if (e[0] & ~r[2]) or clk.get(e[3], 0) < e[4]]
+                if SCRATCH[r[1]][0] == "psum":
+                    owner, now, before = runs.get(r[1], (q, [], []))
+                    if owner != q: now, before = [], now
+                    dep.update(before)
+                    if q == "t": dep.update(now[-1:])
+                    runs[r[1]] = (q, now + [k], before)
                 else:
-                    h[:] = [e for e in h if e[1] or e[2] != q or (e[0] & ~r[2])]
-                h.append((r[2], w, q, sem, c, clk))
-
-    def emit(q, call, rd, wr):
-        sem = "q" + q
-        sync(q, rd, wr)
-        cnt[sem] = cnt.get(sem, 0) + 1
-        call().then_inc(T.sem[sem], 1)
-        record(q, rd, wr, sem, cnt[sem])
+                    h = hist[r[1]]
+                    dep.update(e[2] for e in h if e[0] & r[2] and (e[1] or w))
+                    if w: h[:] = [e for e in h if e[0] & ~r[2]]
+                    h.append((r[2], w, k))
+        dep.discard(k)
+        ops.append(dict(q=q, call=call, dep=dep, cost=cost, lat=lat, sem=sem or "q" + q, inc=inc))
+        return k
 
     v, s, te = g.vector, g.scalar, g.tensor
-    def tt(o, a, b, op): emit("v", lambda: v.tensor_tensor(o[0], a[0], b[0], op), [a, b], [o])
+    def wide(*regs): return 0.5 if all(SCRATCH[r[1]][2] in (f16, bf, u16) for r in regs) else 1.0
+    def cy(n): return max(64, n) * CY
+    def tt(o, a, b, op):
+        both = 2 if SCRATCH[a[1]][0] == SCRATCH[b[1]][0] else 1
+        put("v", lambda: v.tensor_tensor(o[0], a[0], b[0], op), [a, b], [o], cy(o[3] * both * wide(o, a, b)))
     def ts(o, a, s1, s2, op0, op1=None):
-        sc = [x for x in (s1,) if isinstance(x, tuple)]
-        p1 = s1[0] if sc else s1
-        if op1 is None: emit("v", lambda: v.tensor_scalar(o[0], a[0], p1, None, op0), [a] + sc, [o])
-        else: emit("v", lambda: v.tensor_scalar(o[0], a[0], p1, s2, op0, op1), [a] + sc, [o])
-    def cp(o, a): emit("v", lambda: v.tensor_copy(o[0], a[0]), [a], [o])
-    def ms(o, c): emit("v", lambda: v.memset(o[0], c), [], [o])
+        sc = [x for x in (s1, s2) if isinstance(x, tuple)]
+        p1, p2 = (x[0] if isinstance(x, tuple) else x for x in (s1, s2))
+        if op1 is None: put("v", lambda: v.tensor_scalar(o[0], a[0], p1, None, op0), [a] + sc, [o], cy(o[3] * wide(o, a)))
+        else: put("v", lambda: v.tensor_scalar(o[0], a[0], p1, p2, op0, op1), [a] + sc, [o], cy(o[3] * wide(o, a)))
+    def cp(o, a): put("v", lambda: v.tensor_copy(o[0], a[0]), [a], [o], cy(o[3] * wide(o, a)))
+    def ms(o, c): put("v", lambda: v.memset(o[0], c), [], [o], cy(o[3] * wide(o)))
+    def scan(o, d0, d1, op0, op1): put("v", lambda: v.tensor_tensor_scan(o[0], d0[0], d1[0], 0.0, op0, op1), [d0, d1], [o], cy(o[3]))
     def act(o, a, f=F.Identity, bias=0.0, scale=1.0):
-        if isinstance(scale, tuple): emit("s", lambda: s.activation(o[0], a[0], f, scale=scale[0]), [a, scale], [o])
-        elif bias == 0.0: emit("s", lambda: s.activation(o[0], a[0], f, scale=scale), [a], [o])
-        else: emit("s", lambda: s.activation(o[0], a[0], f, bias=bias, scale=scale), [a], [o])
-    def mm(o, w, r, first, last): emit("t", lambda: te.matmul(o[0], w[0], r[0], first, last), [w, r], [o])
-    W = lambda n: X(n)
-    ndma = [0]
-    def dma(q, o, a, rd, wr):
-        sem = "d%d" % ndma[0]; ndma[0] += 1
-        sync(q, rd, wr)
-        eng[q].dma_start(o, a).then_inc(T.sem[sem], 16)
-        cnt[sem] = 16
-        record(q, rd, wr, sem, 16)
-    def nengines(a, b): return len(topo.engines(a, b))
-    def send(to, o, i, sem):
-        dst = T.cores[to % N]
-        sync("g", [i], [])
+        if bias == 0.0: put("s", lambda: s.activation(o[0], a[0], f, scale=scale), [a], [o], cy(o[3]))
+        else: put("s", lambda: s.activation(o[0], a[0], f, bias=bias, scale=scale), [a], [o], cy(o[3]))
+    def mm(o, w, r, first=False, last=False):
+        w = X(w) if isinstance(w, str) else w
+        put("t", lambda: te.matmul(o[0], w[0], r[0], first, last), [w, r], [o], cy(r[3]) * (4 if w[1] == "J1" else 1) * PE, 0.06)
+    def pick(q, o, wn, off, sub=None, bias=0.0):
+        src, c = wn[0].indirect(off[0]), 0.06 + GC * o[3] * CY
+        if sub: put("v", lambda: v.tensor_tensor(o[0], src, sub[0], A.subtract), [wn, off, sub], [o], c)
+        elif q == "v" and bias: put("v", lambda: v.tensor_scalar(o[0], src, bias, None, A.add), [wn, off], [o], c)
+        elif q == "v": put("v", lambda: v.tensor_copy(o[0], src), [wn, off], [o], c)
+        elif bias: put("s", lambda: s.activation(o[0], src, F.Identity, bias=bias), [wn, off], [o], c)
+        else: put("s", lambda: s.activation(o[0], src, F.Copy), [wn, off], [o], c)
+    mine = []
+    def own(call, rd, o): mine.append(put("g", call, rd, [o], 0.17 + 2 * o[3] * CY, after=mine[-1:]))
+    dmas = []
+    def dma(q, o, a, rd, wr, kb, first=False):
+        k = put(q, lambda: eng[q].dma_start(o, a), rd, wr, 0.05, 2.0 + kb / 250, "d%d" % len(dmas), 16)
+        if first: ops[k]["rank"] = 1e3 - len(dmas)
+        dmas.append(k)
+    def send(to, name, i, *idx):
+        dst, o = T.cores[(rank + to) % N], X(name, *idx)
         rid, pid, _ = topo.addr(dst)
-        cnt["loc"] = cnt.get("loc", 0) + nengines(core, dst)
-        g.remote_dma(o[0], i[0], T.sem["a_" + sem], T.sem.loc, pid, rid, topo.mask(core, dst))
-    def arrives(frm, sem, o):
-        c = nengines(T.cores[frm % N], core)
-        cnt["a_" + sem] = c
-        hist[o[1]].append((o[2], True, "r", "a_" + sem, c, {"a_" + sem: c}))
-    S = slice
-    def rows(n, a, b): return X(n, S(a, b))
+        k = put("g", lambda: g.remote_dma(o[0], i[0], T.sem["a_" + name], T.sem.loc, pid, rid, topo.mask(core, dst)), [i], [], 0.3, 0.0,
+                "loc", len(topo.engines(core, dst)))
+        put("r", None, [], [o], HOP, 0.0, "a_" + name, len(topo.engines(T.cores[(rank - to) % N], core)), [k])
 
-    dma("y", T.gn[:], T.gl[:], [], [W("gn")])
-    dma("y", T.win[:, 0:4096], T.xt[:], [], [X("win", S(0, 4096))])
-    for k in (0, 1, 2):
-        if k == 1:
-            for n, src in (("an", T.al), ("bn", T.bl), ("tn", T.th)): dma("y", T[n][:], src[:], [], [W(n)])
-        for h in (0, 1)[:2 if k == 0 else 1]:
-            n = "yv%d" % k
-            dma("y", T[n][:, h * 512:h * 512 + 512], T.yv[:, k * 512:k * 512 + 512], [], [X(n, S(h * 512, h * 512 + 512))])
-    for k in (1, 2):
-        arrives(rank - k, "yi%d" % k, X("yi%d" % k, S(0, 512)))
-        arrives(rank - k, "ti%d" % k, W("ti%d" % k))
-        n = T["yi%d" % k]
-        dma("y", n[:, 512:1024], n[:, 0:512], [X("yi%d" % k, S(0, 512))], [X("yi%d" % k, S(512, 1024))])
-    for k in (1, 2):
-        arrives(rank - 1, "l%d" % k, W("l%d" % k))
-        arrives(rank - 1, "s%da" % k, rows("st%d" % k, 0, 8))
-        arrives(rank - 1, "s%db" % k, rows("st%d" % k, 24, 33))
-        arrives(rank - 1, "s%dc" % k, rows("st%d" % k, 8, 24))
-    arrives(rank + 2, "fg", W("fig")); arrives(rank + 2, "fab", W("fiab"))
+    dma("y", T.gn[:], T.gl[:], [], [X("gn")], 128, True)
+    dma("s", T.win0[:, 4088:4096], T.xt[:, 4088:4096], [], [X("win0", S(4088, 4096))], 0, True)
+    dma("y", T.yr0[:, 256:768], T.yv[:, 0:512], [], [X("yr0", S(256, 768))], 256, True)
+    dma("y", T.win0[:, 0:4088], T.xt[:, 0:4088], [], [X("win0", S(0, 4088))], 1280, True)
+    for k, (n, src) in enumerate((("an", T.al), ("bn", T.bl), ("tn", T.th))): dma("y", T[n][:], src[:], [], [X(n)], 1408 + 128 * k, True)
+    dma("y", T.yo[:], T.yv[:, 512:1536], [], [X("yo")], 2048, True)
+    for p in PIECES: cp(X("yr0", S(768 * p, 768 * p + 256)), X("yr0", S(256 + 256 * p, 512 + 256 * p)))
+    cp(X("ZI", S(143, 144)), X("win0", S(4095, 4096)))
+    ms(X("win0", S(4095, 4096)), 512.0)
 
-    emit("g", lambda: g.iota(T.pi[:], [[0, 1]], 0, 1), [], [W("pi")])
-    ms(W("ones"), 1.0)
     big = dict(allow_small_or_imprecise_dtypes=True)
-    emit("g", lambda: g.affine_select(T.I1[:], T.ones[:, 0:128], [[-1, 128]], A.is_equal, 0.0, 0, 1), [X("ones", S(0, 128))], [W("I1")])
-    emit("g", lambda: g.iota(T.io8[:], [[1, 8]], 0, 0, **big), [], [W("io8")])
-    emit("g", lambda: g.iota(T.iop[:], [[0, 8], [1, 16]], 0, 0, **big), [], [W("iop")])
-    emit("g", lambda: g.iota(T.ioi[:], [[16, 32]], 2048, 0, **big), [], [W("ioi")])
-    ms(W("zz"), 0.0)
-    emit("g", lambda: g.affine_select(T.BB[:], T.zz[:], [[-1, 16], [-16, 8], [0, 16]], A.not_equal, 1.0, 0, 1), [W("zz")], [W("BB")])
-    for n in CM: ms(W(n), CM[n])
-    ts(W("pa"), W("pi"), 15, None, A.bitwise_and)
-    ts(W("pb"), W("pi"), 4, None, A.arith_shift_right)
-    cp(W("pm"), W("pa")); cp(W("pg"), W("pb"))
-    ts(W("bm8"), W("io8"), W("pg"), None, A.is_equal)
-    ts(W("SG"), W("iop"), W("pm"), None, A.is_equal)
-    ts(W("fall"), W("ioi"), W("pm"), None, A.add)
-    ts(W("fallc"), W("fall"), 2.0, -2046.0, A.mult, A.add)
-    cp(W("IH"), W("I1"))
-    for n in ("J1", "Jm1", "Jm101", "Jm129"): act(W(n), W("I1"), F.Identity, scale=float(WF[n]))
-    for n in ("I1920", "I28"): act(W(n), W("I1"), F.Identity, scale=float(WB[n]))
+    one = lambda n: X("ones", S(0, n))
+    ms(X("ones"), 1.0)
+    own(lambda: g.affine_select(T.I1[:], T.ones[:, 0:128], [[-1, 128]], A.is_equal, 0.0, 0, 1), [one(128)], X("I1"))
+    own(lambda: g.iota(T.pi[:, 0:1], [[0, 1]], 0, 1), [], X("pi", S(0, 1)))
+    for k, n in enumerate(WB):
+        if k % 2: act(X(n), X("I1"), scale=float(WB[n]))
+        else: ts(X(n), X("I1"), float(WB[n]), None, A.mult)
+    ms(X("Z"), 0.0)
+    zc = X("Z", S(15, 143, 16))
+    own(lambda: g.affine_select(zc[0], T.ones[:, 0:8], [[-16, 8]], A.is_ge, 0.0, 0, 1), [one(8)], zc)
+    own(lambda: g.affine_select(zc[0], zc[0], [[16, 8]], A.is_ge, 0.0, 15, -1), [zc], zc)
+    own(lambda: g.iota(T.iod[:, 0:256], [[0, 16], [1, 16]], 0, 0, **big), [], X("iod", S(0, 256)))
+    own(lambda: g.iota(T.iod[:, 256:320], [[16, 16], [256, 4]], 0, 0, **big), [], X("iod", S(256, 320)))
+    own(lambda: g.iota(T.pgc[:, 64:128], [[0, 16], [8192, 4]], 8192, 0, **big), [], X("pgc", S(64, 128)))
+    ms(X("pgc", S(0, 64)), 8192.0)
+    ts(X("pi", S(1, 2)), X("pi", S(0, 1)), 15, None, A.bitwise_and)
+    cp(X("pm"), X("pi", S(1, 2)))
+    fb = [X("fb", S(k, k + 1)) for k in range(5)]
+    ts(fb[4], X("pm"), 2.0, 2050.0, A.mult, A.add)
+    for u in range(2): ts(fb[u], X("pm"), 2.0, 4612.0 + 32 * u, A.mult, A.add)
+    ts(X("SG"), X("iod", S(0, 128)), X("pm"), 0.5, A.is_equal, A.mult)
+    ms(X("cf"), -2048.0)
+    ts(X("pof"), X("iod", S(256, 320)), X("pm"), None, A.add)
+    for p in PIECES:
+        ts(X("pdd", p), X("iod", S(0, 256)), X("pm"), 4096.0, A.is_gt, A.mult)
+        for u in range(CHUNK[p]): ts(X("pdd", p, S(16 * u, 256, 16 * CHUNK[p])), X("cf", S(0, 16 // CHUNK[p])), fb[u], 1 / 8192, A.add, A.mult)
+    ms(X("d0g"), -60000.0); ms(X("d0g", S(0, 64, 4)), 1023.0)
+    ts(X("d0g", S(64, 128, 4)), X("iod", S(256, 320, 4)), 2.0, fb[4], A.mult, A.add)
+    ms(X("d0d"), 0.0); ms(X("d0d", S(0, 256, 16)), 1e9)
+    ms(X("d0p"), 60000.0); ms(X("d0p", S(0, 512, 4)), -2047.0)
+    ms(X("d0a"), -2047.0); ms(X("d0a", S(129, 384, 2)), 60000.0)
+    ms(X("ZI", S(0, 16)), 0.0); cp(X("ZI", S(15, 143)), X("I8k"))
+    for k in range(1, 16): tt(X("WD", k - 1), X("ZI", S(15 - k, 143 - k)), X("I8k"), A.subtract)
+    act(X("J1"), X("I1"))
+    m = max(CHUNK.values())
+    if m > 1:
+        ms(X("BB"), 0.0)
+        own(lambda: g.affine_select(T.BB[:], T.BB[:], [[-1, 16], [-16, 8], [0, 16]], A.not_equal, 8192.0, 0, 1), [X("BB")], X("BB"))
+        ms(X("d0c"), 0.0); ms(X("d0c", S(0, 128, 16)), 1e9); ms(X("d0c", S(128, 384, 32)), 1e9)
 
-    def pieces(sh): return {0: [(0, 4, 0)], 1: [(0, 3, 1), (3, 4, 0)], -1: [(1, 4, 0), (0, 1, 3)]}[sh]
-    def add(bank, base, w, src, sbase, sh, first=False, last=False):
-        ps = pieces(sh)
-        for j, (a, b, c) in enumerate(ps):
-            mm(rows(bank, base + a, base + b), W(w), rows(src, sbase + c, sbase + c + b - a), first and j == 0, last and j == len(ps) - 1)
+    def four(name, base, step=1, k=0): return lambda a=0, b=4: X(name, S(base + 16 * step * a + k, base + 16 * step * b, step))
+    def add(out, w, src, sh=0, first=False, last=False):
+        ps = {0: [(0, 4, 0)], 1: [(0, 3, 1), (3, 4, 0)], -1: [(1, 4, 0), (0, 1, 3)]}[sh]
+        for j, (a, b, c) in enumerate(ps): mm(out(a, b), w, src(c, c + b - a), first and j == 0, last and j == len(ps) - 1)
+    ones4 = four("ones", 0)
+    def none(q, o, a):
+        if q == "v": ts(o, a, -2047.0, None, A.is_equal)
+        else: act(o, a, F.Relu, bias=-2046.0, scale=-1.0)
 
-    def index_stage(po, lo, meanwhile=None, goals=None, pair=None):
-        ts(rows("X", 4, 8), rows("b7", 0, 4), -2047.0, -4127.0, A.is_equal, A.mult)
-        act(rows(po, 0, 4), rows("b7", 0, 4), F.Identity, bias=-1.0)
-        act(W("Eo"), rows("b7", 0, 4), F.Relu, bias=-2046.0, scale=-1.0)
-        ts(X(lo, S(0, 128)), rows("b6", 0, 4), -1.0, 2048.0, A.mult, A.add)
-        tt(rows("P", 4, 7), rows("X", 4, 7), rows("b6", 1, 4), A.mult)
-        tt(rows("P", 7, 8), rows("X", 7, 8), rows("b6", 0, 1), A.mult)
-        act(rows("X", 0, 4), rows("b6", 0, 4), F.Identity, bias=2048.0)
-        act(rows(po, 4, 8), rows("b6", 0, 4), F.Identity, bias=-1.0)
-        if meanwhile: meanwhile()
-        tt(rows("P", 0, 4), rows("X", 0, 4), rows("b7", 0, 4), A.mult)
-        one = X("ones", S(0, 128))
-        mm(rows("b5", 4, 8), W("cm1"), one, True, False)
-        mm(rows("b5", 4, 8), W("c2k"), one, False, False)
-        add("b5", 4, "Jm1", po, 0, 0)
-        add("b5", 4, "I1920", "Eo", 0, 0)
-        add("b5", 4, "I28", "Eo", 0, 0, last=True)
-        mm(rows("b5", 0, 4), W("c230"), one, True, False)
-        add("b5", 0, "Jm129", po, 0, 0)
-        add("b5", 0, "Jm101", po, 4, 0, last=True)
-        ts(W("H"), W("P"), 5, None, A.arith_shift_right)
-        if goals: goals()
-        tt(W("NQ"), W("H"), rows("b5", 0, 8), A.add)
-        ts(W("IDX"), W("NQ"), 4095, None, A.bitwise_and)
-        if pair: pair(3)
-        cp(X(lo, S(128, 384)), W("IDX"))
+    def index_stage(p, st, ls):
+        gs, P, Q, IDX = ("%s%d" % (n, p) for n in ("gs", "P", "Q", "IDX"))
+        we, wo = four(gs, 0, 4, 3), four(gs, 256, 4, 3)
+        none(AE_Q[2], X(st, S(0, 128)), X(gs, S(3, 512, 4)))
+        act(X(st, S(128, 192)), we())
+        add(four("HS", 0), "Im4096", we, 1, first=True)
+        add(four("HS", 0), "Im31", we, 1)
+        add(four("HS", 64), "I1", wo)
+        add(four("HS", 64), "Im3232", ones4)
+        add(four("HS", 128), "I64k", ones4)
+        add(four("HS", 128), "Im32", wo)
+        add(four("HS", 192), "Im2080", wo)
+        add(four("HS", 128), "H62k", four(st, 64), last=True)
+        tt(X(P), X("HS", S(0, 128)), X(st, S(64, 192)), A.mult)
+        tt(X(Q), X("HS", S(128, 256)), X(P), A.add)
+        ts(X(IDX), X(Q), 5, 4095, A.arith_shift_right, A.bitwise_and)
+        ts(X(ls, S(0, 64)), we(), -1.0, 2048.0, A.mult, A.add)
+        cp(X(ls, S(64, 192)), X(IDX))
 
-    def index_rest(po):
-        ts(rows(po, 8, 16), W("IDX"), -1.0, 2047.0, A.mult, A.add)
+    for p in PIECES:
+        c = S(16 * p, 16 * p + 16)
+        for h in (0, 1): ts(four("gs%d" % p, 256 * h, 4, 3)(), X("gn", S(0, 4), h, c), -1.0, 2048.0, A.mult, A.add)
+        index_stage(p, "si0%d" % p, "li0%d" % p)
+        for j, n in enumerate(("an", "bn")):
+            ts(four("si0%d" % p, 192 + 64 * j)(), X(n, S(0, 4), 0, c), -1.0, 2048.0, A.mult, A.add)
+            ts(four("si0%d" % p, 320 + 128 * j, 2, 1)(), X(n, S(0, 4), 1, c), -1.0, 2048.0, A.mult, A.add)
+    for h in (0, 1): ts(X("th0", S(4 * h, 4 * h + 4)), X("tn", S(0, 4), h), -2048.0, None, A.add)
+    for k in (1, 2):
+        send(k, "yr%d" % k, X("yo", k - 1), S(256, 768))
+        send(k, "th%d" % k, X("th0"))
+        n = "yr%d" % k
+        for p in PIECES:
+            o, a = X(n, S(768 * p, 768 * p + 256)), X(n, S(256 + 256 * p, 512 + 256 * p))
+            dma("y", o[0], a[0], [a], [o], 64)
 
-    for h in (0, 1): ts(rows("b%d" % (6 + h), 0, 4), X("gn", S(0, 4), h), -1.0, 2048.0, A.mult, A.add)
-    index_stage("st0", "l0")
-    act(W("SS"), W("zz"), F.Copy)
-    for e in range(8):
-        act(X("SS", S(16 * e, 16 * e + 129 * 15 + 1, 129)), X("ones", S(0, 16)), F.Identity, scale=X("bm8", S(e, e + 1)))
-    for n in ("Im1", "I8k", "Im8k", "I16k", "Im16k", "I2k", "Im2k"): act(W(n), W("I1"), F.Identity, scale=float(WB[n]))
-    def home_rest():
-        index_rest("st0")
-        for n, b in (("an", 24), ("bn", 16)):
-            for h in (0, 1): ts(rows("st0", b + 4 * h, b + 4 * h + 4), X(n, S(0, 4), h), -1.0, 2047.0, A.mult, A.add)
-        for h in (0, 1): cp(rows("tf0", 4 * h, 4 * h + 4), X("tn", S(0, 4), h))
-        for k in (1, 2): send(rank + k, W("ti%d" % k), W("tf0"), "ti%d" % k)
-    for k in (1, 2): send(rank + k, X("yi%d" % k, S(0, 512)), X("yv%d" % k, S(0, 512)), "yi%d" % k)
-    def goal_constants():
-        act(W("on5"), X("zz", S(0, 4)), F.Identity, bias=1.0)
-        emit("g", lambda: g.affine_select(T.MK[:], T.zz[:], [[0, 16], [-16, 8], [-1, 16]], A.not_equal, 8192.0, 0, 1), [W("zz")], [W("MK")])
-        emit("g", lambda: g.affine_select(T.MK[:], T.MK[:], [[-1, 16], [0, 8], [1, 16]], A.is_gt, 0.0, 0, 0), [W("MK")], [W("MK")])
-    cp(W("BH"), W("BB"))
-    cp(X("sv", S(0, 1)), X("win", S(4095, 4096)))
-    ms(X("win", S(4095, 4096)), 512.0)
-
-    CALLS = [(0, 64), (64, 64), (256, 64), (320, 64), (128, 64), (192, 32 if HELP else 64)]
-    def visit(t):
-        st, ls, yv, th = "st%d" % t, "l%d" % t, ("yi%d" % t if t else "yv0"), ("ti%d" % t if t else "tf0")
-
-        def gather(c, n):
-            e = 16 * n
-            o, off, vw, wn = X("dd", S(16 * c, 16 * c + e)), X(ls, S(c, c + n)), X(yv, S(0, e)), X("win", S(0, 4096))
-            emit("v", lambda: v.tensor_tensor(o[0], T.win[:, 0:4096].indirect(off[0]), vw[0], A.subtract), [wn, off, vw], [o])
-        def size(c, n): act(X("ab", S(16 * c, 16 * c + 16 * n)), X("dd", S(16 * c, 16 * c + 16 * n)), F.Abs)
-        def total(c, n):
-            bank, r0 = ("b1", (c - 128) // 32) if 128 <= c < 256 else ("b0", c // 32 if c < 128 else c // 32 - 4)
+    def table(t): return "win%d" % (t % 2 if COPIES else 0)
+    def decide(t, p):
+        st, ls, yr, th = "si%d%d" % (t, p), "li%d%d" % (t, p), "yr%d" % t, "th%d" % t
+        dq, ab, w8, ae, dsb, mn, sO, sM, sT, kn, gc, off, da, dr, dst, ge, go, vals, gs = (
+            n + str(p) for n in ("dq", "ab", "w8", "ae", "dsb", "mn", "sO", "sM", "sT", "kn", "gc", "off", "da", "dr", "dst", "ge", "go", "vals", "gs"))
+        Ee, Eo, Ge, Io, Ne = four(st, 0), four(st, 64), four(st, 128), four(w8, 0), four(w8, 64)
+        Ae, Be, Ao, Bo = four(st, 192), four(st, 256), four(st, 320, 2, 1), four(st, 448, 2, 1)
+        Oe, Oo, M, Te, To, Ke, Ko = four(sO, 0), four(sO, 64), four(sM, 0), four(sT, 0), four(sT, 64), four(kn, 0), four(kn, 64)
+        De, Do = four(dsb, 0), four(dsb, 64)
+        view2, view = X(yr, S(512 * p, 512 * p + 512)), X(yr, S(256 + 256 * p, 512 + 256 * p))
+        def total(out, row, first, last):
             for j in range(16):
-                mm(rows(bank, r0, r0 + n // 32), X("SS", S(128 * j, 128 * j + 128)), X("ab", S(16 * c + j, 16 * c + 16 * n, 16)),
-                   j == 0 and bank == "b0", j == 15 and (bank == "b0" or c == 192))
-        def prep_a():
-            act(rows("E", 0, 4), rows(st, 4, 8), F.Relu, bias=-2047.0, scale=-1.0)
-            act(rows("E", 4, 8), rows(st, 0, 4), F.Relu, bias=-2047.0, scale=-1.0)
-            mm(rows("b6", 0, 8), W("I16k"), rows("E", 0, 8), True, False)
-            add("b6", 0, "Im16k", "E", 4, 0)
-            add("b6", 4, "Im16k", "E", 0, 1)
-            if t == 1:
-                add("b6", 0, "J1", th, 4, 0); add("b6", 4, "J1", th, 0, 1)
+                mm(out, X("Z", S(15 - j, 143 - j)), X(ab, S(256 * row + j, 256 * row + 1024, 16)), first and j == 0, last and j == 15)
+        for c in range(6):
+            o, a, l, wn = X(dq, S(512 * c, 512 * c + 512)), X(ab, S(512 * c, 512 * c + 512)), X(ls, S(32 * c, 32 * c + 32)), X(table(t), S(0, 4096))
+            if c in BY_SCALAR[p]:
+                pick("s", o, wn, l)
+                mm(X("XV"), "Im1", view2, True, False)
+                mm(X("XV"), "I1", o, False, True)
+                act(a, X("XV"), F.Abs)
             else:
-                mm(rows("b6", 0, 8), W("J1"), rows(th, 0, 8), False, False)
-        def prep_b():
-            act(W("AE"), rows(st, 24, 32), F.Relu, bias=-2047.0, scale=-1.0)
-            if t: act(W("Cb"), rows(st, 32, 33), F.Copy)
-            mm(rows("b6", 0, 8), W("I16k"), rows("AE", 0, 8), False, t == 0)
-            if t:
-                for k in range(8): mm(rows("b6", k, k + 1), W("I1"), W("Cb"), False, k == 7)
-
-        one, o1 = X("ones", S(0, 256)), X("ones", S(0, 128))
-        def empty_gates():
-            mm(rows("b3", 0, 4), W("Im1"), rows("E", 0, 4), True, False)
-            mm(rows("b2", 0, 8), W("I1"), W("E"), True, False)
-            add("b2", 4, "Im1", "E", 0, 1)
-            mm(rows("b4", 0, 12), W("I1"), X("zz", S(0, 3)), True, False)
-            mm(rows("b4", 0, 4), W("I1"), o1, False, False)
-            mm(rows("b4", 8, 12), W("I1"), o1, False, False)
-            add("b4", 8, "Im1", "E", 4, 0)
-        def open_gates():
-            add("b3", 0, "Im1", "O", 4, 0)
-            add("b2", 0, "Im1", "O", 4, -1)
-            add("b2", 4, "Im1", "O", 0, 0)
-            add("b4", 0, "Im1", "O", 0, 0)
-            add("b4", 8, "Im1", "O", 4, 0)
-        de, do = (0, 1) if t == 0 else (-1, 0) if t == 1 else (0, 0)
-        be, bo = ("b7", "b6") if t < 2 else ("b6", "b7")
-        def places_0():
-            for bank in (be, bo):
-                mm(rows(bank, 0, 4), W("cp1"), o1, True, False)
-        def places_e():
-            add(be, 0, "IH", "oab", 8, do)
-            add(be, 0, "IH", "oab", 4, do - 1)
-            add(be, 0, "I2k", "O", 4, do - 1)
-        def places_o():
-            add(bo, 0, "IH", "oab", 12, de)
-            add(bo, 0, "IH", "oab", 0, de)
-            add(bo, 0, "I2k", "O", 0, de)
-            add(bo, 0, "Im2k", "E", 4, de)
-        if HELP:
-            off0 = X(ls, S(224, 256))
-            emit("s", lambda: s.activation(T.xg[:], T.win[:, 0:4096].indirect(off0[0]), F.Copy), [X("win", S(0, 4096)), off0], [W("xg")])
-        for k, (c, n) in enumerate(CALLS):
-            gather(c, n)
-            if k == 1 and t == 0:
-                home_rest()
-                goal_constants()
-            if k == 4:
-                tt(W("O"), rows("b0", 0, 8), W("thr"), A.is_gt)
-                mm(rows("b5", 0, 8), W("I1"), W("O"), True, True)
-                mm(rows("b5", 8, 16), W("I1"), W("O"), True, True)
-            if k == len(CALLS) - 1: tt(W("oab"), W("b5"), rows(st, 16, 32), A.mult)
-            if k == 3: prep_b()
-            size(c, n)
-            if k == 2: prep_a()
-            if k == 4:
-                act(W("dsb"), rows("b0", 0, 8), F.Copy)
-                mm(rows("b1", 0, 4), W("I8k"), rows("E", 4, 8), True, False)
-            if k == 0 and HELP:
-                mm(W("b4"), W("I1"), W("xg"), True, False)
-                mm(W("b4"), W("Im1"), X(yv, S(0, 512)), False, True)
-            if k == 1 and HELP: act(X("ab", S(16 * 224, 16 * 256)), W("b4"), F.Abs)
-            if k < 5: total(c, n)
-            if k == 3:
-                act(W("thr"), rows("b6", 0, 8), F.Identity, bias=16384.0)
-                empty_gates()
-            if k == 4: open_gates()
-        act(W("nv"), rows(st, 0, 12), F.Identity, bias=-1.0, scale=-1.0)
-        total(192, 64)
-        places_0()
-        tt(W("mn"), rows("b0", 0, 4), rows("dsb", 4, 8), A.min)
-        tt(rows("UX", 4, 7), rows("b0", 4, 7), rows("dsb", 1, 4), A.is_lt)
-        tt(rows("UX", 7, 8), rows("b0", 7, 8), rows("dsb", 0, 1), A.is_lt)
-        add("b2", 4, "I1", "UX", 4, 0)
-        tt(rows("UX", 0, 4), rows("b1", 0, 4), W("mn"), A.is_lt)
-        add("b3", 0, "I1", "UX", 0, 0, last=True)
-        add("b2", 0, "I1", "UX", 0, 0, last=True)
-        ts(W("Mf"), rows("b3", 0, 4), 0.0, None, A.max)
-        act(W("Tf"), rows("b2", 0, 8), F.Relu, bias=-1.0)
-        if t < 2: places_e()
-        mm(rows("b3", 4, 8), W("I1"), W("Mf"), True, False)
-        for k in (1, 2, 3): mm(rows("b3", 4 + k, 8), W("Im1"), rows("Mf", 0, 4 - k), False, k == 3)
-        act(W("Ff"), rows("b3", 4, 8), F.Relu)
-        add("b4", 0, "Im1", "Mf", 0, 0)
-        add("b4", 4, "I1", "Mf", 0, 0)
-        add("b4", 8, "Im1", "Mf", 0, 0)
-        mm(rows("b4", 4, 12), W("I1"), W("Tf"), False, True)
-        if t < 2: places_o()
-        for k in range(3): mm(rows("b2", 4 * k, 4 * k + 4), W("I1"), W("Ff"), True, True)
-        for k in range(2): mm(rows("b5", 8 + 4 * k, 12 + 4 * k), W("I1"), W("Mf"), True, True)
-        tt(W("vz"), rows("b4", 0, 12), rows(st, 4, 16), A.mult)
-        tt(W("keys"), rows("b2", 0, 12), W("nv"), A.mult)
-        def places_b():
-            add(be, 0, "I2k", "Tf", 0, do)
-            add(bo, 0, "I2k", "Tf", 4, de)
-            add(bo, 0, "Im2k", "Mf", 0, de)
-            add(be, 0, "IH", "vz", 0, do)
-            add(be, 0, "IH", "vz", 4, do, last=True)
-            add(bo, 0, "IH", "vz", 8, de, last=True)
-        if t < 2: places_b()
-        for a in range(4): mm(rows("b3", 8, 11), W("IH"), X("keys", S(a, 12, 4)), a == 0, False)
-        mm(rows("b3", 10, 11), W("c8k"), X("ones", S(0, 32)), False, False)
-        for a in range(4): mm(rows("b3", 10, 11), W("Im8k"), rows("Ff", a, a + 1), False, a == 3)
-        def first_goals():
-            tt(W("code"), rows("b3", 10, 11), W("fallc"), A.min)
-            for k in range(4): tt(X("own", k), rows("b3", 10, 11), W("fallc"), A.min)
-            ts(W("lgg"), rows("b3", 8, 10), 2048.0, None, A.add)
-            for k in (4, 8): act(rows("own", k, 2 * k), rows("own", 0, k), F.Copy)
-        def keeps():
-            mm(rows("b3", 4, 12), W("I1"), one, True, False)
-            mm(rows("b3", 4, 12), W("Im1"), W("O"), False, False)
-            mm(rows("b3", 4, 12), W("Im1"), W("Tf"), False, False)
-            add("b3", 4, "Im1", "Mf", 0, 0)
-            add("b3", 4, "Im1", "O", 4, -1)
-            add("b3", 8, "Im1", "O", 0, 0)
-            add("b3", 8, "Im1", "Mf", 0, 0, last=True)
-            if t < 2:
-                for a in range(4): mm(rows("b3", 12, 13), W("SG"), rows("Mf", a, a + 1), a == 0, a == 3)
-        def memories():
-            tt(rows("kab", 0, 8), rows("b3", 4, 12), rows(st, 16, 24), A.mult)
-            tt(rows("kab", 8, 16), rows("b3", 4, 12), rows(st, 24, 32), A.mult)
-            tt(rows("mz", 0, 8), rows("b5", 8, 16), rows(st, 0, 8), A.mult)
-            act(W("Kb"), rows("b3", 4, 12), F.Copy)
-        def memory_sums():
-            for j, mzr in ((0, 0), (1, 4)):
-                ev, od = (4, 0) if t < 2 else (0, 4)
-                se, so = (do, de) if t < 2 else (0, 0)
-                for (a, b, c) in pieces(se):
-                    r = rows("b0", 8 * j + ev + a, 8 * j + ev + b)
-                    mm(r, W("IH"), rows("kab", 8 * j + c, 8 * j + c + b - a), True, False)
-                    mm(r, W("I2k"), rows("Kb", c, c + b - a), False, False)
-                    mm(r, W("IH"), rows("mz", mzr + c, mzr + c + b - a), False, False)
-                    mm(r, W("I2k"), rows("Mf", c, c + b - a), False, True)
-                for (a, b, c) in pieces(so):
-                    r = rows("b0", 8 * j + od + a, 8 * j + od + b)
-                    mm(r, W("IH"), rows("kab", 8 * j + 4 + c, 8 * j + 4 + c + b - a), True, False)
-                    mm(r, W("I2k"), rows("Kb", 4 + c, 4 + c + b - a), False, True)
-        def goals():
-            for j in range(16):
-                mm(X("b1", j), X("BH", j), W("code"), True, True)
-        ec = [NB * (M * (e - 1) - e * (e - 1) // 2) for e in range(M + 1)]
-        def pair(e):
-            if e == 0: tt(W("eq"), rows("b1", 0, 16), rows("own", 0, 16), A.is_equal)
-            else: tt(X("ee", S(0, 16), S(ec[e], ec[e + 1])), X("b1", S(0, 16), S(0, NB), S(0, M - e)), X("own", S(0, 16), S(0, NB), S(e, M)), A.is_equal)
-        out = "po%d" % (t + 1)
-        if t < 2:
-            index_stage(out, "lo%d" % (t + 1), first_goals, goals, pair)
-            send(rank + 1, W("l%d" % (t + 1)), W("lo%d" % (t + 1)), "l%d" % (t + 1))
-            keeps()
+                pick("v", o, wn, l, view2)
+                act(a, o, F.Abs)
+            if c in (1, 3): total(four("DB", 32 * (c - 1))(), 2 * (c - 1), True, True)
+        act(X(dsb), X("DB", S(0, 128)), bias=-2047.0)
+        tt(X(mn), De(), Do(), A.min)
+        ts(X(w8), X(ls, S(64, 192)), -1.0, 2048.0, A.mult, A.add)
+        none(AE_Q[0], four(ae, 0)(), Ae())
+        none(AE_Q[1], four(ae, 64)(), Ao())
+        tq = lambda h: (lambda a, b: X(th, S(4 * h + a, 4 * h + b), S(16 * p, 16 * p + 16)))
+        ge_, go_ = four("GA", 0), four("GA", 64)
+        mm(X("GA", S(0, 128)), "Im16k", X(st, S(0, 128)), True)
+        add(ge_, "I16k", Eo); add(go_, "I16k", Ee, 1)
+        add(ge_, "Im1", tq(t % 2)); add(go_, "Im1", tq(1 - t % 2), t % 2)
+        mm(X("GA", S(0, 128)), "Im16k", X(ae))
+        if t:
+            for k in range(8): mm(X("GA", S(16 * k, 16 * k + 16)), "Im1", X(st, S(576, 592)))
+        mm(X("GA", S(0, 128)), "I1", X(dsb), False, True)
+        act(X(sO), X("GA", S(0, 128)), F.Sign, bias=-16385.5 - (16 if t else 0))
+        gm = four("GB", 0)
+        add(gm, "I16k", Ee, first=True); add(gm, "I16k", Eo); add(gm, "Im1", four(mn, 0)); add(gm, "I8k", Oo)
+        total(gm(), 8, False, True)
+        act(M(), gm(), F.Sign, bias=-6145.5, scale=-1.0)
+        gt = four("XV", 0)
+        add(gt, "Im16k", Eo, first=True); add(gt, "I16k", Ee, 1); add(gt, "I1", Do); add(gt, "Im1", De, 1); add(gt, "I8k", Oe, last=True)
+        act(To(), gt(), F.Sign, bias=-24576.5, scale=-1.0)
+        gt = four("XV", 64)
+        rm = four("rm", 64 * p)
+        act(rm(), gm())
+        add(gt, "Im32k", Ee, first=True); add(gt, "Im8k", Oo); add(gt, "I8k", Oo, -1); add(gt, "J1", rm, last=True)
+        act(Te(), gt(), F.Sign, bias=-22529.5, scale=-1.0)
+        mm(X("GA", S(128, 256)), "I1", X("pgc"), True)
+        mm(X("GA", S(128, 192)), "I1", X("pof"))
+        for a in range(4): mm(X("GA", S(192 + a, 256, 4)), "Im1", Ne(a, a + 1))
+        for a in range(4):
+            mm(X("GA", S(128 + a, 192, 4)), "Im8k", M(a, a + 1))
+            for b in range(a + 1): mm(X("GA", S(192 + a, 256, 4)), "Im8k" if b == a else "I8k", M(b, b + 1), False, a == 3 and b == 3)
+        scan(X(gc), X("d0g"), X("GA", S(128, 256)), A.max, A.min)
+        code = X(gc, S(67, 128, 4))
+        cp(X(off), X(gc, S(3, 64, 4)))
+        mm(X("DD", S(0, 16)), "I8k", X("pdd", p), True)
+        if CHUNK[p] > 1:
+            for j in range(16): mm(X(BC, S(256 + j, 384, 16)), X("BB", j), X(gc, S(67, 128, 8)), j == 0, j == 15)
+        mm(X("DD", S(0, 16), 0), "Im1", code)
+        for k in range(1, 16): mm(X("DD", S(0, 16), k), X("WD", k - 1), code, False, k == 15)
+        m = CHUNK[p]
+        if m == 1:
+            act(X(da, S(0, 256)), X("DD", S(0, 16)), F.Abs)
+            scan(X(dr, S(0, 256)), X("d0d"), X(da, S(0, 256)), A.add, A.min)
+            ts(X(dst, S(0, 32, 2)), X(dr, S(15, 256, 16)), -1.0, fb[0], A.mult, A.add)
         else:
-            first_goals()
-            keeps()
-            places_e(); places_o()
-            goals()
-            places_b()
-            memories()
-            memory_sums()
-            for h in (0, 1): ts(rows("fog", 4 * h, 4 * h + 4), rows("b%d" % (6 + h), 0, 4), -1.0, 2048.0, A.mult, A.add)
-            send(rank - 2, W("fig"), W("fog"), "fg")
-        off = X("lgg", S(0, 64))
-        emit("s", lambda: s.activation(T.gab[:], T.win[:, 0:4096].indirect(off[0]), F.Copy), [X("win", S(0, 4096)), off], [W("gab")])
-        pe = X("b7" if t < 2 else "b5", S(8, 10), S(0, NE // 2))
-        def count(lo, hi):
-            for j in range(lo, min(hi, 15)): mm(X("b2", 0), X("MK", j), X("eq", j), False, False)
-            for j in range(lo, hi): mm(pe, W("I1"), X("ee", j), j == 0, j == 15)
-        mm(X("b2", 0), W("IH"), W("code"), True, False)
-        mm(W("b4"), W("cmh"), W("on5"), True, False)
-        for h in (0, 1): mm(W("b4"), W("I1"), X("gab", S(512 * h, 512 * h + 512)), False, h == 1)
-        act(W("vf"), W("b4"), F.Identity, bias=8388608.0, scale=0.5)
-        act(W("vals"), W("vf"), F.Identity, bias=-8388608.0)
-        for e in (0, 1, 2) if t < 2 else (0, 1, 2, 3): pair(e)
-        count(0, 16)
+            ts(X("cf", S(0, 8)), X(gc, S(71, 128, 8)), 8192.0, None, A.mult)
+            for k in range(8):
+                o, a, c = X(da, S(129 + 32 * k, 160 + 32 * k, 2)), X(BC, S(256 + 16 * k, 272 + 16 * k)), X("cf", S(k, k + 1))
+                if CROSS_Q == "v": ts(o, a, c, 8192.0, A.not_equal, A.mult)
+                else: put("s", lambda o=o, a=a, c=c: s.activation(o[0], a[0], F.Abs, bias=c[0], scale=-1.0), [a, c], [o], cy(o[3]))
+            act(X(da, S(0, 128)), X("DD", S(0, 16, 2)), F.Abs)
+            act(X(da, S(128, 384, 2)), X("DD", S(1, 16, 2)), F.Abs)
+            scan(X(dr), X("d0c"), X(da), A.add, A.min)
+            ts(X(dst, S(0, 16, 2)), X(dr, S(15, 128, 16)), -1.0, fb[0], A.mult, A.add)
+            ts(X(dst, S(1, 16, 2)), X(dr, S(159, 384, 32)), -1.0, fb[1], A.mult, A.add)
+        pick(VAL_Q[p][0], X(ge), X(dq, S(0, 1024)), X(off), bias=-0.5)
+        pick(VAL_Q[p][1], X(go), X(dq, S(1024, 2048)), X(off))
+        gv, less = X("GB", S(64, 320)), 2 - (0 in BY_SCALAR[p]) - (2 in BY_SCALAR[p])
+        if less: mm(gv, "I1" if less == 2 else "Ih", view, True)
+        mm(gv, "Ih", X(ge), not less)
+        mm(gv, "Ih", X(go))
+        mm(gv, "Imag", one(256), False, True)
+        act(X(vals), gv, bias=-12582912.0)
+        ke, ko = four("HS", 256), four("HS", 320)
+        add(ke, "I1", Oe, first=True); add(ke, "I1", Oo, -1); add(ko, "I1", Oo); add(ko, "I1", Oe); add(ko, "I1", To)
+        add(ke, "I1", M); add(ko, "I1", M); add(ke, "I1", Te, last=True)
+        act(X(kn), X("HS", S(256, 384)), bias=4.0)
+        de, do = ((0, 1), (-1, 0), (0, 0))[t]
+        fo, fe = (lambda k: four("GP", 0, 4, k)), (lambda k: four("GP", 256, 4, k))
+        mm(X("GP", S(0, 256)), "Im8k", one(256), True)
+        add(fe(1), "Im8k", ones4); add(fe(2), "Im8k", ones4)
+        add(fo(1), "I1", Io, de); add(fo(2), "I1", Ao, de); add(fo(3), "I1", Be, de); add(fo(1), "Im16k", Eo, de)
+        add(fe(0), "I1", Ge, do); add(fe(1), "I1", Ae, do); add(fe(2), "I1", Bo, do - 1); add(fe(3), "I1", Ne, do)
+        add(fo(1), "Im8k", Oo, de); add(fo(2), "I8k", Oo, de); add(fo(3), "I8k", Oe, de)
+        add(fe(1), "I8k", Oe, do); add(fe(2), "I8k", Oo, do - 1); add(fo(1), "I8k", To, de)
+        add(fo(1), "Im8k", M, de); add(fe(3), "I8k", M, do); add(fe(3), "I8k", Te, do); add(fe(0), "Im8k", Ke, do, last=True)
+        scan(X(gs), X("d0p"), X("GP"), A.min, A.max)
+        out = "so%d%d" % (t + 1, p)
+        mm(X("AB", S(129, 384, 2)), "Im8k", one(128), True)
+        for j, (old_o, old_e, new) in enumerate(((Ao, Ae, Ge), (Bo, Be, Io))):
+            add(four("AB", 64 * j), "I1", old_o, de); add(four("AB", 128 + 128 * j, 2, 0), "I1", old_e, do)
+            add(four("AB", 128 + 128 * j, 2, 1), "I1", new, do)
+        for j in (0, 1): add(four("AB", 128 + 128 * j, 2, 1), "I8k", M, do)
         if t < 2:
-            send(rank + 1, rows("st%d" % (t + 1), 0, 8), rows(out, 0, 8), "s%da" % (t + 1))
-            memories()
+            for a in range(4): mm(X("AB", S(384, 400)), "SG", M(a, a + 1))
+        for j in (0, 1):
+            add(four("AB", 64 * j), "Im8k", Ko, de); add(four("AB", 128 + 128 * j, 2, 0), "Im8k", Ke, do, last=j == 1)
+        n = 400 if t < 2 else 384
+        scan(X(out, S(192, 192 + n)), X("d0a", S(0, n)), X("AB", S(0, n)), A.min, A.max)
+        if t < 2:
+            index_stage(p, out, "lo%d%d" % (t + 1, p))
+            send(1, "li%d%d" % (t + 1, p), X("lo%d%d" % (t + 1, p)))
+            send(1, "si%d%d" % (t + 1, p), X(out))
         else:
-            ts(W("foab"), W("b0"), -1.0, 4095.0, A.mult, A.add)
-            send(rank - 2, W("fiab"), W("foab"), "fab")
-        cp(W("ce"), pe)
-        for e in range(1, M): mm(X("b2", 0, S(0, NB), S(e, M)), W("I8k"), X("ce", S(ec[e], ec[e + 1])), False, e == M - 1)
-        if t < 2:
-            index_rest(out)
-            memory_sums()
-            act(rows(out, 24, 32), rows("b0", 8, 16), F.Identity, bias=-2048.0)
-            act(rows(out, 32, 33), rows("b3", 12, 13), F.Copy)
-            send(rank + 1, rows("st%d" % (t + 1), 24, 33), rows(out, 24, 33), "s%db" % (t + 1))
-            act(rows(out, 16, 24), rows("b0", 0, 8), F.Identity, bias=-2048.0)
-            send(rank + 1, rows("st%d" % (t + 1), 8, 24), rows(out, 8, 24), "s%dc" % (t + 1))
-        for u in range(M):
-            ts(X("dst", S(u, 32, M)), X("b2", 0, S(0, NB), u), X("fall", S(u, u + 1)), 2048.0, A.min, A.add)
-        for q in range(NB - 1, -1, -1):
-            off2, va, wn = X("dst", S(q * M, q * M + M)), X("vals", S(16 * M * q, 16 * M * (q + 1))), W("win")
-            emit("v", lambda: v.tensor_copy(T.win[:, 0:4608].indirect(off2[0]), va[0]), [off2, va], [wn])
+            act(X(out, S(64, 192)), X(gs, S(3, 512, 4)))
+            act(X(out, S(0, 64)), X(out, S(321, 448, 2)))
+            act(X(out, S(320, 384)), X(out, S(449, 576, 2)))
+            send(-2, "si3%d" % p, X(out, S(0, 384)), S(0, 384))
 
-    for t in range(3): visit(t)
-    cp(X("win", S(4095, 4096)), X("sv", S(0, 1)))
-    dma("y", T.ox[:], T.win[:, 0:4096], [X("win", S(0, 4096))], [])
-    for src, r0, buf, dst in (("fig", 0, "og_", T.og), ("fiab", 8, "oa_", T.oa), ("fiab", 0, "ob_", T.ob)):
-        for h in (0, 1): cp(X(buf, S(0, 4), h), rows(src, r0 + 4 * h, r0 + 4 * h + 4))
-        dma("y" if buf == "ob_" else "s", dst[:], T[buf][:], [W(buf)], [])
+    def write(t, p):
+        m = CHUNK[p]
+        for c in range(16 - m, -1, -m):
+            o, va, wn = X("dst%d" % p, S(2 * c, 2 * c + 1) if m == 1 else S(c, c + m)), X("vals%d" % p, S(16 * c, 16 * (c + m))), X(table(t + 1))
+            put("v", lambda o=o, va=va, wn=wn: v.tensor_copy(wn[0].indirect(o[0]), va[0]), [o, va], [wn], 0.05 + 16 * m * 3.0 * CY)
+
+    for t in range(3):
+        for k in range(COPIES):
+            c = S(4096 // COPIES * k, 4096 // COPIES * (k + 1))
+            dma("y", T[table(t + 1)][:, c], T[table(t)][:, c], [X(table(t), c)] + ([X("yo")] if t == 0 else []), [X(table(t + 1), c)], 1024 // COPIES * (k + 1))
+        for p in PIECES: decide(t, p)
+        if t == 2: cp(X(table(3), S(4095, 4096)), X("ZI", S(143, 144)))
+        for p in PIECES: write(t, p)
+    dma("y", T.ox[:], T[table(3)][:, 0:4096], [X(table(3), S(0, 4096))], [], 1024)
+    for j, (buf, dst) in enumerate((("og_", T.og), ("oa_", T.oa), ("ob_", T.ob))):
+        for p in PIECES:
+            st = "si3%d" % p
+            src = [four(st, b) for b in ((128, 64), (0, 192), (320, 256))[j]]
+            for h in (0, 1): act(X(buf, S(0, 4), h, S(16 * p, 16 * p + 16)), src[h](), bias=2048.0, scale=-1.0)
+        dma("s", dst[:], T[buf][:], [X(buf)], [], 128)
+
+    if "order" not in _cache: _cache["order"] = plan(ops)
+    cnt, done, known = {}, {}, {q: {} for q in eng}
+    for k in _cache["order"]:
+        o = ops[k]
+        q, sem = o["q"], o["sem"]
+        cnt[sem] = cnt.get(sem, 0) + o["inc"]
+        if q == "r":
+            done[k] = (sem, cnt[sem], {sem: cnt[sem]})
+            continue
+        for dsem, c, clk in sorted((done[j] for j in o["dep"] if not (q == "t" and ops[j]["q"] == "t")), key=lambda e: (-len(e[2]), -e[1])):
+            if known[q].get(dsem, 0) >= c: continue
+            eng[q].wait_ge(T.sem[dsem], c)
+            for x in clk: known[q][x] = max(known[q].get(x, 0), clk[x])
+        ins = o["call"]()
+        if sem != "loc": ins.then_inc(T.sem[sem], o["inc"])
+        clk = dict(known[q]); clk[sem] = cnt[sem]
+        done[k] = (sem, cnt[sem], clk)
     for sem in cnt: g.wait_ge(T.sem[sem], cnt[sem])

@@ -5,9 +5,11 @@ f32, f16, bf, i32, u16 = "float32", "float16", "bfloat16", "int32", "uint16"
 PIECES = (1, 0)
 BY_SCALAR = {1: (4,), 0: ()}
 COPIES = 0
-CHUNK, CROSS_Q, BC = {1: 1, 0: 2}, "s", "XV"
+TWICE = ((2, 0),)
+MARG = 0.0
+CHUNK, CROSS_Q, BC = {1: 2, 0: 2}, "sv", "XV"
 AE_Q = "vvs"
-VAL_Q = ("ss", "sv")
+VAL_Q = ("sv", "sv")
 WB = {"Im1": -1, "Ih": 0.5, "I8k": 8192, "Im8k": -8192, "I16k": 16384, "Im16k": -16384, "Im32k": -32768, "Imag": 12582912,
       "I64k": 65536, "Im3232": -3232, "Im4096": -4096, "Im31": -31, "Im32": -32, "Im2080": -2080, "H62k": 62336}
 SCRATCH = {
@@ -24,11 +26,11 @@ SCRATCH = {
     "WD": ("sbuf", [128, 15, 128], bf), "pi": ("sbuf", [128, 2], i32), "rm": ("sbuf", [128, 128], f32), "pm": ("sbuf", [128, 1], f32),
     "fb": ("sbuf", [128, 5], f32), "iod": ("sbuf", [128, 320], f32),
     "pof": ("sbuf", [128, 64], f16), "pgc": ("sbuf", [128, 128], bf), "pdd": ("sbuf", [128, 2, 256], f16),
-    "d0g": ("sbuf", [128, 128], f32), "d0d": ("sbuf", [128, 256], bf), "d0p": ("sbuf", [128, 512], f16), "d0a": ("sbuf", [128, 400], f16),
+    "d0g": ("sbuf", [128, 128], f32), "SD": ("sbuf", [128, 128], bf), "d0p": ("sbuf", [128, 512], f16), "d0a": ("sbuf", [128, 400], f16),
 }
 for _n in WB: SCRATCH[_n] = ("sbuf", [128, 128], f16 if _n[0] == "H" else bf)
 for _p in PIECES:
-    for _n, _w, _d in (("dq", 3072, bf), ("ab", 3072, bf), ("w8", 128, f16), ("ae", 128, bf), ("dsb", 128, f16), ("mn", 64, f16),
+    for _n, _w, _d in (("dq", 3072, bf), ("ab", 3072, bf), ("w8", 128, f16), ("ae", 128, bf), ("dsb", 128, f16), ("mn", 64, f32),
                        ("sO", 128, bf), ("sM", 64, bf), ("sT", 128, bf), ("kn", 128, bf), ("gc", 128, f16), ("off", 16, u16),
                        ("dst", 32, u16), ("ge", 256, f16), ("go", 256, bf), ("vals", 256, bf),
                        ("gs", 512, f16), ("P", 128, f32), ("Q", 128, i32), ("IDX", 128, i32),
@@ -43,38 +45,44 @@ NDMA = 30
 ARR = ["yr1", "yr2", "th1", "th2"] + [n + str(p) for n in ("li1", "li2", "si1", "si2", "si3") for p in PIECES]
 SEMAPHORES = ["qv", "qs", "qt", "qg", "loc"] + ["d%d" % k for k in range(NDMA)] + ["a_" + n for n in ARR]
 _cache = {}
-CY, WAKE, HOP = 0.83e-3, 0.15, 4.0
+CY, WAKE, HOP = 0.83e-3, 0.2, 2.5
+RATE = 300
 
 
 def plan(ops):
     n = len(ops)
-    succ = [[] for _ in ops]
+    pred, succ = [[] for _ in ops], [[] for _ in ops]
     for k, o in enumerate(ops):
-        for d in o["dep"]: succ[d].append(k)
-    def lat(d, k): return 0.0 if ops[d]["q"] == "t" and ops[k]["q"] == "t" else WAKE + ops[d]["lat"]
+        for d in o["dep"] | o["behind"]:
+            wait = d in o["dep"] and not ops[d]["q"] == o["q"] == "t"
+            w = WAKE + ops[d]["lat"] + (MARG if o["q"] == "t" else 0.0) if wait else 0.0
+            pred[k].append((d, w)); succ[d].append((k, w))
+    def lay(order, before, first):
+        end, busy = [0.0] * n, {q: [] for q in "vstgy"}
+        for k in order:
+            t, c = max([end[d] + w for d, w in before[k]] + [first[k]]), ops[k]["cost"]
+            if ops[k]["q"] != "r":
+                b = busy[ops[k]["q"]]
+                j = len(b)
+                while j and b[j - 1][1] > t: j -= 1
+                while j < len(b) and b[j][0] < t + c + GAP[ops[k]["q"] == "t"] - 1e-9:
+                    t = max(t, b[j][1]); j += 1
+                b.insert(j, (t, t + c))
+            end[k] = t + c
+        return end
     way = [0.0] * n
-    for k in range(n - 1, -1, -1):
-        way[k] = ops[k]["cost"] + max([way[j] + lat(k, j) for j in succ[k]] + [ops[k]["lat"]])
-    left = [len(o["dep"]) for o in ops]
-    ready = {q: {} for q in "vstgyr"}
-    free = {q: 0.0 for q in ready}
-    end = [0.0] * n
-    for k in range(n):
-        if not left[k]: ready[ops[k]["q"]][k] = 0.0
-    order = []
-    while len(order) < n:
-        t0, q = min((max(free[q], min(ready[q].values())), q) for q in ready if ready[q])
-        k = max((k for k in ready[q] if ready[q][k] <= t0 + SLACK), key=lambda k: (ops[k].get("rank", way[k]), -k))
-        start = max(free[q], ready[q].pop(k))
-        end[k] = start + ops[k]["cost"]
-        if q != "r": free[q] = end[k]
-        order.append((start, len(order), k))
-        for j in succ[k]:
-            left[j] -= 1
-            if not left[j]: ready[ops[j]["q"]][j] = max(end[d] + lat(d, j) for d in ops[j]["dep"])
-    return [k for _, _, k in order]
-SLACK = 0.05
-GC, PE = 1.5, 0.5
+    for k in range(n - 1, -1, -1): way[k] = ops[k]["cost"] + max([way[j] + w for j, w in succ[k]] + [ops[k]["lat"]])
+    best = None
+    for _ in range(ROUNDS):
+        end = lay(sorted(range(n), key=lambda k: (-way[k], k)), pred, [0.0] * n)
+        span = max(end[k] + ops[k]["lat"] for k in range(n))
+        if best is None or span < best[0]: best = (span, end)
+        way = lay(sorted(range(n), key=lambda k: (-end[k], -k)), succ, [o["lat"] for o in ops])
+    _cache["span"] = best[0]
+    return sorted(range(n), key=lambda k: (best[1][k] - ops[k]["cost"], best[1][k], k))
+ROUNDS = 3
+GAP = (0.0, 0.0)
+GC, PE, PLAT = 1.3, 0.5, 0.06
 
 
 def rank_program(g, core, T, topo):
@@ -83,7 +91,7 @@ def rank_program(g, core, T, topo):
         return
     N = len(T.cores)
     eng = {"v": g.vector, "s": g.scalar, "t": g.tensor, "g": g, "y": g.sync}
-    ops, hist, runs = [], {n: [] for n in SCRATCH}, {}
+    ops, hist, runs, group = [], {n: [] for n in SCRATCH}, {}, {}
     S = slice
 
     def X(name, *idx):
@@ -96,7 +104,7 @@ def rank_program(g, core, T, topo):
             _cache[key] = (int.from_bytes(np.packbits(b).tobytes(), "big"), int(a.size))
         return (T[name][(slice(None),) + idx], name) + _cache[key]
 
-    def put(q, call, rd, wr, cost, lat=0.03, sem=None, inc=1, after=()):
+    def put(q, call, rd, wr, cost, lat=0.03, sem=None, inc=1, after=(), behind=(), first=False):
         k, dep = len(ops), set(after)
         for regs, w in ((rd, False), (wr, True)):
             for r in regs:
@@ -104,7 +112,9 @@ def rank_program(g, core, T, topo):
                     owner, now, before = runs.get(r[1], (q, [], []))
                     if owner != q: now, before = [], now
                     dep.update(before)
-                    if q == "t": dep.update(now[-1:])
+                    if q == "t":
+                        if first: group[r[1]] = k
+                        dep.update(now if first else [group[r[1]]])
                     runs[r[1]] = (q, now + [k], before)
                 else:
                     h = hist[r[1]]
@@ -112,7 +122,8 @@ def rank_program(g, core, T, topo):
                     if w: h[:] = [e for e in h if e[0] & ~r[2]]
                     h.append((r[2], w, k))
         dep.discard(k)
-        ops.append(dict(q=q, call=call, dep=dep, cost=cost, lat=lat, sem=sem or "q" + q, inc=inc))
+        ops.append(dict(q=q, call=call, dep=dep, behind=set(behind) - dep, cost=cost, lat=lat, sem=sem or "q" + q, inc=inc,
+                        group=group[wr[0][1]] if q == "t" else None))
         return k
 
     v, s, te = g.vector, g.scalar, g.tensor
@@ -132,9 +143,10 @@ def rank_program(g, core, T, topo):
     def act(o, a, f=F.Identity, bias=0.0, scale=1.0):
         if bias == 0.0: put("s", lambda: s.activation(o[0], a[0], f, scale=scale), [a], [o], cy(o[3]))
         else: put("s", lambda: s.activation(o[0], a[0], f, bias=bias, scale=scale), [a], [o], cy(o[3]))
-    def mm(o, w, r, first=False, last=False):
+    def mm(o, w, r, first=False, last=False, after=()):
         w = X(w) if isinstance(w, str) else w
-        put("t", lambda: te.matmul(o[0], w[0], r[0], first, last), [w, r], [o], cy(r[3]) * (4 if w[1] == "J1" else 1) * PE, 0.06)
+        return put("t", lambda stop: te.matmul(o[0], w[0], r[0], first, stop), [w, r], [o], cy(r[3]) * (4 if w[1] == "J1" else 1) * PE, PLAT,
+                   first=first, after=after)
     def pick(q, o, wn, off, sub=None, bias=0.0):
         src, c = wn[0].indirect(off[0]), 0.06 + GC * o[3] * CY
         if sub: put("v", lambda: v.tensor_tensor(o[0], src, sub[0], A.subtract), [wn, off, sub], [o], c)
@@ -142,19 +154,16 @@ def rank_program(g, core, T, topo):
         elif q == "v": put("v", lambda: v.tensor_copy(o[0], src), [wn, off], [o], c)
         elif bias: put("s", lambda: s.activation(o[0], src, F.Identity, bias=bias), [wn, off], [o], c)
         else: put("s", lambda: s.activation(o[0], src, F.Copy), [wn, off], [o], c)
-    mine = []
-    def own(call, rd, o): mine.append(put("g", call, rd, [o], 0.17 + 2 * o[3] * CY, after=mine[-1:]))
+    def own(call, rd, o): put("g", call, rd, [o], 0.17 + 2 * o[3] * CY)
     dmas = []
     def dma(q, o, a, rd, wr, kb, first=False):
-        k = put(q, lambda: eng[q].dma_start(o, a), rd, wr, 0.05, 2.0 + kb / 250, "d%d" % len(dmas), 16)
-        if first: ops[k]["rank"] = 1e3 - len(dmas)
-        dmas.append(k)
+        dmas.append(put(q, lambda: eng[q].dma_start(o, a), rd, wr, 0.05, 2.0 + kb / 300, "d%d" % len(dmas), 16, behind=dmas[-1:] if first else ()))
     def send(to, name, i, *idx):
         dst, o = T.cores[(rank + to) % N], X(name, *idx)
         rid, pid, _ = topo.addr(dst)
         k = put("g", lambda: g.remote_dma(o[0], i[0], T.sem["a_" + name], T.sem.loc, pid, rid, topo.mask(core, dst)), [i], [], 0.3, 0.0,
                 "loc", len(topo.engines(core, dst)))
-        put("r", None, [], [o], HOP, 0.0, "a_" + name, len(topo.engines(T.cores[(rank - to) % N], core)), [k])
+        put("r", None, [], [o], HOP + o[3] / RATE, 0.0, "a_" + name, len(topo.engines(T.cores[(rank - to) % N], core)), [k])
 
     dma("y", T.gn[:], T.gl[:], [], [X("gn")], 128, True)
     dma("s", T.win0[:, 4088:4096], T.xt[:, 4088:4096], [], [X("win0", S(4088, 4096))], 0, True)
@@ -195,12 +204,14 @@ def rank_program(g, core, T, topo):
         for u in range(CHUNK[p]): ts(X("pdd", p, S(16 * u, 256, 16 * CHUNK[p])), X("cf", S(0, 16 // CHUNK[p])), fb[u], 1 / 8192, A.add, A.mult)
     ms(X("d0g"), -60000.0); ms(X("d0g", S(0, 64, 4)), 1023.0)
     ts(X("d0g", S(64, 128, 4)), X("iod", S(256, 320, 4)), 2.0, fb[4], A.mult, A.add)
-    ms(X("d0d"), 0.0); ms(X("d0d", S(0, 256, 16)), 1e9)
     ms(X("d0p"), 60000.0); ms(X("d0p", S(0, 512, 4)), -2047.0)
     ms(X("d0a"), -2047.0); ms(X("d0a", S(129, 384, 2)), 60000.0)
     ms(X("ZI", S(0, 16)), 0.0); cp(X("ZI", S(15, 143)), X("I8k"))
     for k in range(1, 16): tt(X("WD", k - 1), X("ZI", S(15 - k, 143 - k)), X("I8k"), A.subtract)
     act(X("J1"), X("I1"))
+    tt(X("SD", S(0, 64)), X("I1", S(0, 64)), X("I1", S(64, 128)), A.subtract)
+    tt(X("SD", S(64, 112)), X("I1", S(64, 112)), X("I1", S(16, 64)), A.subtract)
+    tt(X("SD", S(112, 128)), X("I1", S(112, 128)), X("I1", S(0, 16)), A.subtract)
     m = max(CHUNK.values())
     if m > 1:
         ms(X("BB"), 0.0)
@@ -259,7 +270,6 @@ def rank_program(g, core, T, topo):
         Ee, Eo, Ge, Io, Ne = four(st, 0), four(st, 64), four(st, 128), four(w8, 0), four(w8, 64)
         Ae, Be, Ao, Bo = four(st, 192), four(st, 256), four(st, 320, 2, 1), four(st, 448, 2, 1)
         Oe, Oo, M, Te, To, Ke, Ko = four(sO, 0), four(sO, 64), four(sM, 0), four(sT, 0), four(sT, 64), four(kn, 0), four(kn, 64)
-        De, Do = four(dsb, 0), four(dsb, 64)
         view2, view = X(yr, S(512 * p, 512 * p + 512)), X(yr, S(256 + 256 * p, 512 + 256 * p))
         def total(out, row, first, last):
             for j in range(16):
@@ -274,9 +284,8 @@ def rank_program(g, core, T, topo):
             else:
                 pick("v", o, wn, l, view2)
                 act(a, o, F.Abs)
-            if c in (1, 3): total(four("DB", 32 * (c - 1))(), 2 * (c - 1), True, True)
+        for j in range(16): mm(X("DB", S(j, 128, 16)), X(ab, S(j, 2048, 16)), X("Z", S(15, 143, 16)), j == 0)
         act(X(dsb), X("DB", S(0, 128)), bias=-2047.0)
-        tt(X(mn), De(), Do(), A.min)
         ts(X(w8), X(ls, S(64, 192)), -1.0, 2048.0, A.mult, A.add)
         none(AE_Q[0], four(ae, 0)(), Ae())
         none(AE_Q[1], four(ae, 64)(), Ao())
@@ -288,27 +297,36 @@ def rank_program(g, core, T, topo):
         mm(X("GA", S(0, 128)), "Im16k", X(ae))
         if t:
             for k in range(8): mm(X("GA", S(16 * k, 16 * k + 16)), "Im1", X(st, S(576, 592)))
-        mm(X("GA", S(0, 128)), "I1", X(dsb), False, True)
+        mm(X("GA", S(0, 128)), dsb, X("I1"))
+        mm(X("GA", S(128, 192)), dsb, X("SD", S(0, 64)))
         act(X(sO), X("GA", S(0, 128)), F.Sign, bias=-16385.5 - (16 if t else 0))
-        gm = four("GB", 0)
-        add(gm, "I16k", Ee, first=True); add(gm, "I16k", Eo); add(gm, "Im1", four(mn, 0)); add(gm, "I8k", Oo)
+        act(X(mn), X("GA", S(128, 192)), F.Relu)
+        gm = four("DB", 128)
+        add(gm, "I16k", Ee, first=True); add(gm, "I16k", Eo); add(gm, "J1", four(mn, 0)); add(gm, "I8k", Oo)
+        mm(gm(), dsb, X("Im1", S(0, 64)))
         total(gm(), 8, False, True)
+        gt = four("DB", 192)
+        add(gt, "Im16k", Eo); add(gt, "I16k", Ee, 1); add(gt, "I8k", Oe)
+        mm(gt(), dsb, X("SD", S(64, 128)))
         act(M(), gm(), F.Sign, bias=-6145.5, scale=-1.0)
-        gt = four("XV", 0)
-        add(gt, "Im16k", Eo, first=True); add(gt, "I16k", Ee, 1); add(gt, "I1", Do); add(gt, "Im1", De, 1); add(gt, "I8k", Oe, last=True)
         act(To(), gt(), F.Sign, bias=-24576.5, scale=-1.0)
-        gt = four("XV", 64)
-        rm = four("rm", 64 * p)
-        act(rm(), gm())
-        add(gt, "Im32k", Ee, first=True); add(gt, "Im8k", Oo); add(gt, "I8k", Oo, -1); add(gt, "J1", rm, last=True)
+        gt = four("HS", 384)
+        if (t, p) in TWICE:
+            add(gt, "Im16k", Ee, first=True); add(gt, "I16k", Eo); add(gt, "I8k", Oo, -1)
+            mm(gt(), dsb, X("Im1", S(64, 128)))
+            total(gt(), 8, False, True)
+        else:
+            rm = four("rm", 64 * p)
+            act(rm(), gm())
+            add(gt, "Im32k", Ee, first=True); add(gt, "Im8k", Oo); add(gt, "I8k", Oo, -1); add(gt, "J1", rm, last=True)
         act(Te(), gt(), F.Sign, bias=-22529.5, scale=-1.0)
-        mm(X("GA", S(128, 256)), "I1", X("pgc"), True)
-        mm(X("GA", S(128, 192)), "I1", X("pof"))
-        for a in range(4): mm(X("GA", S(192 + a, 256, 4)), "Im1", Ne(a, a + 1))
+        mm(X("GB", S(0, 128)), "I1", X("pgc"), True)
+        mm(X("GB", S(0, 64)), "I1", X("pof"))
+        for a in range(4): mm(X("GB", S(64 + a, 128, 4)), "Im1", Ne(a, a + 1))
         for a in range(4):
-            mm(X("GA", S(128 + a, 192, 4)), "Im8k", M(a, a + 1))
-            for b in range(a + 1): mm(X("GA", S(192 + a, 256, 4)), "Im8k" if b == a else "I8k", M(b, b + 1), False, a == 3 and b == 3)
-        scan(X(gc), X("d0g"), X("GA", S(128, 256)), A.max, A.min)
+            mm(X("GB", S(a, 64, 4)), "Im8k", M(a, a + 1))
+            for b in range(a + 1): mm(X("GB", S(64 + a, 128, 4)), "Im8k" if b == a else "I8k", M(b, b + 1), False, a == 3 and b == 3)
+        scan(X(gc), X("d0g"), X("GB", S(0, 128)), A.max, A.min)
         code = X(gc, S(67, 128, 4))
         cp(X(off), X(gc, S(3, 64, 4)))
         mm(X("DD", S(0, 16)), "I8k", X("pdd", p), True)
@@ -325,7 +343,7 @@ def rank_program(g, core, T, topo):
             ts(X("cf", S(0, 8)), X(gc, S(71, 128, 8)), 8192.0, None, A.mult)
             for k in range(8):
                 o, a, c = X(da, S(129 + 32 * k, 160 + 32 * k, 2)), X(BC, S(256 + 16 * k, 272 + 16 * k)), X("cf", S(k, k + 1))
-                if CROSS_Q == "v": ts(o, a, c, 8192.0, A.not_equal, A.mult)
+                if CROSS_Q[p] == "v": ts(o, a, c, 8192.0, A.not_equal, A.mult)
                 else: put("s", lambda o=o, a=a, c=c: s.activation(o[0], a[0], F.Abs, bias=c[0], scale=-1.0), [a, c], [o], cy(o[3]))
             act(X(da, S(0, 128)), X("DD", S(0, 16, 2)), F.Abs)
             act(X(da, S(128, 384, 2)), X("DD", S(1, 16, 2)), F.Abs)
@@ -334,16 +352,16 @@ def rank_program(g, core, T, topo):
             ts(X(dst, S(1, 16, 2)), X(dr, S(159, 384, 32)), -1.0, fb[1], A.mult, A.add)
         pick(VAL_Q[p][0], X(ge), X(dq, S(0, 1024)), X(off), bias=-0.5)
         pick(VAL_Q[p][1], X(go), X(dq, S(1024, 2048)), X(off))
-        gv, less = X("GB", S(64, 320)), 2 - (0 in BY_SCALAR[p]) - (2 in BY_SCALAR[p])
+        gv, less = X("GB", S(128, 384)), 2 - (0 in BY_SCALAR[p]) - (2 in BY_SCALAR[p])
         if less: mm(gv, "I1" if less == 2 else "Ih", view, True)
-        mm(gv, "Ih", X(ge), not less)
-        mm(gv, "Ih", X(go))
-        mm(gv, "Imag", one(256), False, True)
+        halves = [mm(gv, "Ih", X(ge), not less), mm(gv, "Ih", X(go))]
+        mm(gv, "Imag", one(256), after=halves)
         act(X(vals), gv, bias=-12582912.0)
         ke, ko = four("HS", 256), four("HS", 320)
-        add(ke, "I1", Oe, first=True); add(ke, "I1", Oo, -1); add(ko, "I1", Oo); add(ko, "I1", Oe); add(ko, "I1", To)
-        add(ke, "I1", M); add(ko, "I1", M); add(ke, "I1", Te, last=True)
-        act(X(kn), X("HS", S(256, 384)), bias=4.0)
+        if (t, p) not in TWICE:
+            add(ke, "I1", Oe, first=True); add(ke, "I1", Oo, -1); add(ko, "I1", Oo); add(ko, "I1", Oe); add(ko, "I1", To)
+            add(ke, "I1", M); add(ko, "I1", M); add(ke, "I1", Te, last=True)
+            act(X(kn), X("HS", S(256, 384)), bias=4.0)
         de, do = ((0, 1), (-1, 0), (0, 0))[t]
         fo, fe = (lambda k: four("GP", 0, 4, k)), (lambda k: four("GP", 256, 4, k))
         mm(X("GP", S(0, 256)), "Im8k", one(256), True)
@@ -352,7 +370,8 @@ def rank_program(g, core, T, topo):
         add(fe(0), "I1", Ge, do); add(fe(1), "I1", Ae, do); add(fe(2), "I1", Bo, do - 1); add(fe(3), "I1", Ne, do)
         add(fo(1), "Im8k", Oo, de); add(fo(2), "I8k", Oo, de); add(fo(3), "I8k", Oe, de)
         add(fe(1), "I8k", Oe, do); add(fe(2), "I8k", Oo, do - 1); add(fo(1), "I8k", To, de)
-        add(fo(1), "Im8k", M, de); add(fe(3), "I8k", M, do); add(fe(3), "I8k", Te, do); add(fe(0), "Im8k", Ke, do, last=True)
+        add(fo(1), "Im8k", M, de); add(fe(3), "I8k", M, do); add(fe(3), "I8k", Te, do)
+        add(fe(0), "Im16k", ones4); add(fe(0), "Im8k", Oe, do); add(fe(0), "Im8k", M, do)
         scan(X(gs), X("d0p"), X("GP"), A.min, A.max)
         out = "so%d%d" % (t + 1, p)
         mm(X("AB", S(129, 384, 2)), "Im8k", one(128), True)
@@ -363,7 +382,13 @@ def rank_program(g, core, T, topo):
         if t < 2:
             for a in range(4): mm(X("AB", S(384, 400)), "SG", M(a, a + 1))
         for j in (0, 1):
-            add(four("AB", 64 * j), "Im8k", Ko, de); add(four("AB", 128 + 128 * j, 2, 0), "Im8k", Ke, do, last=j == 1)
+            ao, ak = four("AB", 64 * j), four("AB", 128 + 128 * j, 2, 0)
+            if (t, p) not in TWICE:
+                add(ao, "Im8k", Ko, de); add(ak, "Im8k", Ke, do)
+                continue
+            add(ao, "Im32k", ones4); add(ak, "Im32k", ones4); add(ak, "Im8k", Oo, do - 1)
+            for f in (Oo, Oe, To, M): add(ao, "Im8k", f, de)
+            for f in (Oe, M, Te): add(ak, "Im8k", f, do)
         n = 400 if t < 2 else 384
         scan(X(out, S(192, 192 + n)), X("d0a", S(0, n)), X("AB", S(0, n)), A.min, A.max)
         if t < 2:
@@ -398,7 +423,8 @@ def rank_program(g, core, T, topo):
         dma("s", dst[:], T[buf][:], [X(buf)], [], 128)
 
     if "order" not in _cache: _cache["order"] = plan(ops)
-    cnt, done, known = {}, {}, {q: {} for q in eng}
+    cnt, done, known, left = {}, {}, {q: {} for q in eng}, {}
+    for o in ops: left[o["group"]] = left.get(o["group"], 0) + 1
     for k in _cache["order"]:
         o = ops[k]
         q, sem = o["q"], o["sem"]
@@ -410,7 +436,10 @@ def rank_program(g, core, T, topo):
             if known[q].get(dsem, 0) >= c: continue
             eng[q].wait_ge(T.sem[dsem], c)
             for x in clk: known[q][x] = max(known[q].get(x, 0), clk[x])
-        ins = o["call"]()
+        if q == "t":
+            left[o["group"]] -= 1
+            ins = o["call"](not left[o["group"]])
+        else: ins = o["call"]()
         if sem != "loc": ins.then_inc(T.sem[sem], o["inc"])
         clk = dict(known[q]); clk[sem] = cnt[sem]
         done[k] = (sem, cnt[sem], clk)

@@ -3,14 +3,18 @@ from concourse.mybir import AluOpType as A, ActivationFunctionType as F
 
 f32, f16, bf, i32, u16 = "float32", "float16", "bfloat16", "int32", "uint16"
 PIECES = (1, 0)
-BY_SCALAR = {1: (4,), 0: ()}
+BY_SCALAR = {1: (0, 1), 0: ()}
 COPIES = 0
-TWICE = ((2, 0),)
-MARG = 0.0
-CHUNK, CROSS_Q, BC = {1: 2, 0: 2}, "sv", "XV"
+TWICE = ()
+MARG, GV = {}, ("GB", "GB")
+ROWS, ENDS = (("AB", "AB"), ("GP", "GP")), (("GP", "AB"), ("GP", "AB"))
+GOAL, TAKE, KEEP = ("XV", "GB"), ("DB", "HS"), ("GA", "GA")
+CHUNK, CROSS_Q, D8 = {1: 2, 0: 2}, "sv", ("XV", "DB")
+BC, TURNS, STAGE = ("XV", "HS"), (1, 0, 1, 1, 0, 0, 1, 0), ("XV", "XV", "XV")
+RULES, EARLY = (1, 1, 1, 0), (0,)
 AE_Q = "vvs"
 VAL_Q = ("sv", "sv")
-WB = {"Im1": -1, "Ih": 0.5, "I8k": 8192, "Im8k": -8192, "I16k": 16384, "Im16k": -16384, "Im32k": -32768, "Imag": 12582912,
+WB = {"Im1": -1, "Hh": 1023 / 2048, "I8k": 8192, "Im8k": -8192, "I16k": 16384, "Im16k": -16384, "Im32k": -32768, "Imag": 12582912,
       "I64k": 65536, "Im3232": -3232, "Im4096": -4096, "Im31": -31, "Im32": -32, "Im2080": -2080, "H62k": 62336}
 SCRATCH = {
     "win0": ("sbuf", [128, 4752], bf),
@@ -32,21 +36,21 @@ for _n in WB: SCRATCH[_n] = ("sbuf", [128, 128], f16 if _n[0] == "H" else bf)
 for _p in PIECES:
     for _n, _w, _d in (("dq", 3072, bf), ("ab", 3072, bf), ("w8", 128, f16), ("ae", 128, bf), ("dsb", 128, f16), ("mn", 64, f32),
                        ("sO", 128, bf), ("sM", 64, bf), ("sT", 128, bf), ("kn", 128, bf), ("gc", 128, f16), ("off", 16, u16),
-                       ("dst", 32, u16), ("ge", 256, f16), ("go", 256, bf), ("vals", 256, bf),
+                       ("dst", 32, u16), ("ge", 256, bf), ("go", 256, bf), ("vals", 256, bf),
                        ("gs", 512, f16), ("P", 128, f32), ("Q", 128, i32), ("IDX", 128, i32),
                        ("li0", 192, u16), ("li1", 192, u16), ("li2", 192, u16), ("lo1", 192, u16), ("lo2", 192, u16),
-                       ("si0", 592, f16), ("si1", 592, f16), ("si2", 592, f16), ("si3", 592, f16),
-                       ("so1", 592, f16), ("so2", 592, f16), ("so3", 592, f16)):
+                       ("si0", 592, f16), ("si1", 592, f16), ("si2", 592, f16), ("si3", 384, f16),
+                       ("so1", 592, f16), ("so2", 592, f16), ("so3", 640, f16)):
         SCRATCH[_n + str(_p)] = ("sbuf", [128, _w], _d)
     for _n in ("da", "dr"): SCRATCH[_n + str(_p)] = ("sbuf", [128, 384], f32)
 for _n in ("XV", "DB", "GA", "GB", "GP", "AB", "HS"): SCRATCH[_n] = ("psum", [128, 512], f32)
 SCRATCH["DD"] = ("psum", [128, 32, 16], f32)
 NDMA = 30
-ARR = ["yr1", "yr2", "th1", "th2"] + [n + str(p) for n in ("li1", "li2", "si1", "si2", "si3") for p in PIECES]
+ARR = ["yr1", "yr2", "th1", "th2"] + [n + str(p) for n in ("li1", "li2", "lj1", "lj2", "si1", "si2", "si3") for p in PIECES]
 SEMAPHORES = ["qv", "qs", "qt", "qg", "loc"] + ["d%d" % k for k in range(NDMA)] + ["a_" + n for n in ARR]
 _cache = {}
 CY, WAKE, HOP = 0.83e-3, 0.2, 2.5
-RATE = 300
+RATE, LAST, LOAD, SPLIT = 300, 0.5, 400, 0
 
 
 def plan(ops):
@@ -55,7 +59,7 @@ def plan(ops):
     for k, o in enumerate(ops):
         for d in o["dep"] | o["behind"]:
             wait = d in o["dep"] and not ops[d]["q"] == o["q"] == "t"
-            w = WAKE + ops[d]["lat"] + (MARG if o["q"] == "t" else 0.0) if wait else 0.0
+            w = WAKE + ops[d]["lat"] + MARG.get(o["q"], 0.0) if wait else 0.0
             pred[k].append((d, w)); succ[d].append((k, w))
     def lay(order, before, first):
         end, busy = [0.0] * n, {q: [] for q in "vstgy"}
@@ -74,13 +78,16 @@ def plan(ops):
     for k in range(n - 1, -1, -1): way[k] = ops[k]["cost"] + max([way[j] + w for j, w in succ[k]] + [ops[k]["lat"]])
     best = None
     for _ in range(ROUNDS):
+        way = [way[k] + URGENT.get(ops[k]["step"], 0.0) for k in range(n)]
+        for k in range(n - 1, -1, -1): way[k] = max([way[k]] + [way[j] + 1e-6 for j, w in succ[k]])
         end = lay(sorted(range(n), key=lambda k: (-way[k], k)), pred, [0.0] * n)
         span = max(end[k] + ops[k]["lat"] for k in range(n))
         if best is None or span < best[0]: best = (span, end)
         way = lay(sorted(range(n), key=lambda k: (-end[k], -k)), succ, [o["lat"] for o in ops])
     _cache["span"] = best[0]
     return sorted(range(n), key=lambda k: (best[1][k] - ops[k]["cost"], best[1][k], k))
-ROUNDS = 3
+URGENT = {"rows0": 0.5}
+ROUNDS = 2
 GAP = (0.0, 0.0)
 GC, PE, PLAT = 1.3, 0.5, 0.06
 
@@ -93,6 +100,7 @@ def rank_program(g, core, T, topo):
     eng = {"v": g.vector, "s": g.scalar, "t": g.tensor, "g": g, "y": g.sync}
     ops, hist, runs, group = [], {n: [] for n in SCRATCH}, {}, {}
     S = slice
+    step, mark = [""], {}
 
     def X(name, *idx):
         key = (name,) + tuple(("s", i.start, i.stop, i.step) if isinstance(i, slice) else i for i in idx)
@@ -123,7 +131,7 @@ def rank_program(g, core, T, topo):
                     h.append((r[2], w, k))
         dep.discard(k)
         ops.append(dict(q=q, call=call, dep=dep, behind=set(behind) - dep, cost=cost, lat=lat, sem=sem or "q" + q, inc=inc,
-                        group=group[wr[0][1]] if q == "t" else None))
+                        group=group[wr[0][1]] if q == "t" else None, step=step[0]))
         return k
 
     v, s, te = g.vector, g.scalar, g.tensor
@@ -147,23 +155,21 @@ def rank_program(g, core, T, topo):
         w = X(w) if isinstance(w, str) else w
         return put("t", lambda stop: te.matmul(o[0], w[0], r[0], first, stop), [w, r], [o], cy(r[3]) * (4 if w[1] == "J1" else 1) * PE, PLAT,
                    first=first, after=after)
-    def pick(q, o, wn, off, sub=None, bias=0.0):
+    def pick(q, o, wn, off, sub=None, op=A.subtract):
         src, c = wn[0].indirect(off[0]), 0.06 + GC * o[3] * CY
-        if sub: put("v", lambda: v.tensor_tensor(o[0], src, sub[0], A.subtract), [wn, off, sub], [o], c)
-        elif q == "v" and bias: put("v", lambda: v.tensor_scalar(o[0], src, bias, None, A.add), [wn, off], [o], c)
+        if sub: put("v", lambda: v.tensor_tensor(o[0], src, sub[0], op), [wn, off, sub], [o], c)
         elif q == "v": put("v", lambda: v.tensor_copy(o[0], src), [wn, off], [o], c)
-        elif bias: put("s", lambda: s.activation(o[0], src, F.Identity, bias=bias), [wn, off], [o], c)
         else: put("s", lambda: s.activation(o[0], src, F.Copy), [wn, off], [o], c)
     def own(call, rd, o): put("g", call, rd, [o], 0.17 + 2 * o[3] * CY)
     dmas = []
     def dma(q, o, a, rd, wr, kb, first=False):
-        dmas.append(put(q, lambda: eng[q].dma_start(o, a), rd, wr, 0.05, 2.0 + kb / 300, "d%d" % len(dmas), 16, behind=dmas[-1:] if first else ()))
-    def send(to, name, i, *idx):
-        dst, o = T.cores[(rank + to) % N], X(name, *idx)
+        dmas.append(put(q, lambda: eng[q].dma_start(o, a), rd, wr, 0.05, 2.0 + kb / LOAD, "d%d" % len(dmas), 16, behind=dmas[-1:] if first else ()))
+    def send(to, name, i, *idx, sem=None):
+        dst, o, name = T.cores[(rank + to) % N], X(name, *idx), sem or name
         rid, pid, _ = topo.addr(dst)
         k = put("g", lambda: g.remote_dma(o[0], i[0], T.sem["a_" + name], T.sem.loc, pid, rid, topo.mask(core, dst)), [i], [], 0.3, 0.0,
                 "loc", len(topo.engines(core, dst)))
-        put("r", None, [], [o], HOP + o[3] / RATE, 0.0, "a_" + name, len(topo.engines(T.cores[(rank - to) % N], core)), [k])
+        put("r", None, [], [o], HOP + o[3] / RATE + (LAST if to < 0 else 0), 0.0, "a_" + name, len(topo.engines(T.cores[(rank - to) % N], core)), [k])
 
     dma("y", T.gn[:], T.gl[:], [], [X("gn")], 128, True)
     dma("s", T.win0[:, 4088:4096], T.xt[:, 4088:4096], [], [X("win0", S(4088, 4096))], 0, True)
@@ -207,7 +213,12 @@ def rank_program(g, core, T, topo):
     ms(X("d0p"), 60000.0); ms(X("d0p", S(0, 512, 4)), -2047.0)
     ms(X("d0a"), -2047.0); ms(X("d0a", S(129, 384, 2)), 60000.0)
     ms(X("ZI", S(0, 16)), 0.0); cp(X("ZI", S(15, 143)), X("I8k"))
-    for k in range(1, 16): tt(X("WD", k - 1), X("ZI", S(15 - k, 143 - k)), X("I8k"), A.subtract)
+    for b, bank in enumerate(("XV", "GB", "AB", "DB")):
+        ks = range(4 * b + 1, min(4 * b + 5, 16))
+        for k in ks:
+            o = X(bank, S(128 * (k - ks[0]), 128 * (k - ks[0] + 1)))
+            mm(o, "I1", X("ZI", S(15 - k, 143 - k)), k == ks[0]); mm(o, "Im1", X("I8k"))
+        act(X("WD", S(ks[0] - 1, ks[-1])), X(bank, S(0, 128 * len(ks))))
     act(X("J1"), X("I1"))
     tt(X("SD", S(0, 64)), X("I1", S(0, 64)), X("I1", S(64, 128)), A.subtract)
     tt(X("SD", S(64, 112)), X("I1", S(64, 112)), X("I1", S(16, 64)), A.subtract)
@@ -239,7 +250,7 @@ def rank_program(g, core, T, topo):
         add(four("HS", 128), "I64k", ones4)
         add(four("HS", 128), "Im32", wo)
         add(four("HS", 192), "Im2080", wo)
-        add(four("HS", 128), "H62k", four(st, 64), last=True)
+        add(four("HS", 0), "H62k", ones4)
         tt(X(P), X("HS", S(0, 128)), X(st, S(64, 192)), A.mult)
         tt(X(Q), X("HS", S(128, 256)), X(P), A.add)
         ts(X(IDX), X(Q), 5, 4095, A.arith_shift_right, A.bitwise_and)
@@ -271,6 +282,7 @@ def rank_program(g, core, T, topo):
         Ae, Be, Ao, Bo = four(st, 192), four(st, 256), four(st, 320, 2, 1), four(st, 448, 2, 1)
         Oe, Oo, M, Te, To, Ke, Ko = four(sO, 0), four(sO, 64), four(sM, 0), four(sT, 0), four(sT, 64), four(kn, 0), four(kn, 64)
         view2, view = X(yr, S(512 * p, 512 * p + 512)), X(yr, S(256 + 256 * p, 512 + 256 * p))
+        step[0] = "gather%d" % p
         def total(out, row, first, last):
             for j in range(16):
                 mm(out, X("Z", S(15 - j, 143 - j)), X(ab, S(256 * row + j, 256 * row + 1024, 16)), first and j == 0, last and j == 15)
@@ -278,14 +290,26 @@ def rank_program(g, core, T, topo):
             o, a, l, wn = X(dq, S(512 * c, 512 * c + 512)), X(ab, S(512 * c, 512 * c + 512)), X(ls, S(32 * c, 32 * c + 32)), X(table(t), S(0, 4096))
             if c in BY_SCALAR[p]:
                 pick("s", o, wn, l)
-                mm(X("XV"), "Im1", view2, True, False)
-                mm(X("XV"), "I1", o, False, True)
-                act(a, X("XV"), F.Abs)
+                xv = X(STAGE[BY_SCALAR[p].index(c)])
+                mm(xv, "Im1", view2, True)
+                mm(xv, "I1", o)
+                act(a, xv, F.Abs)
+            elif SPLIT and p == 0 and c == 5:
+                for h in (10, 11):
+                    o = X(dq, S(256 * h, 256 * h + 256))
+                    pick("v", o, wn, X(ls, S(16 * h, 16 * h + 16)), view)
+                    act(X(ab, S(256 * h, 256 * h + 256)), o, F.Abs)
             else:
+                step[0] = "pick%d" % p
                 pick("v", o, wn, l, view2)
+                step[0], mark[c] = "gather%d" % p, len(ops) - 1
                 act(a, o, F.Abs)
-        for j in range(16): mm(X("DB", S(j, 128, 16)), X(ab, S(j, 2048, 16)), X("Z", S(15, 143, 16)), j == 0)
-        act(X(dsb), X("DB", S(0, 128)), bias=-2047.0)
+        step[0] = "flags%d" % p
+        for j in range(16): mm(X(D8[p], S(j, 128, 16)), X(ab, S(j, 2048, 16)), X("Z", S(15, 143, 16)), j == 0)
+        mark["sums"] = range(len(ops) - 16, len(ops))
+        act(X(dsb), X(D8[p], S(0, 128)), bias=-2047.0)
+        yield
+        step[0] = "flags%d" % p
         ts(X(w8), X(ls, S(64, 192)), -1.0, 2048.0, A.mult, A.add)
         none(AE_Q[0], four(ae, 0)(), Ae())
         none(AE_Q[1], four(ae, 64)(), Ao())
@@ -310,7 +334,8 @@ def rank_program(g, core, T, topo):
         mm(gt(), dsb, X("SD", S(64, 128)))
         act(M(), gm(), F.Sign, bias=-6145.5, scale=-1.0)
         act(To(), gt(), F.Sign, bias=-24576.5, scale=-1.0)
-        gt = four("HS", 384)
+        step[0] = "take%d" % p
+        gt = four(TAKE[p], 384)
         if (t, p) in TWICE:
             add(gt, "Im16k", Ee, first=True); add(gt, "I16k", Eo); add(gt, "I8k", Oo, -1)
             mm(gt(), dsb, X("Im1", S(64, 128)))
@@ -320,20 +345,30 @@ def rank_program(g, core, T, topo):
             act(rm(), gm())
             add(gt, "Im32k", Ee, first=True); add(gt, "Im8k", Oo); add(gt, "I8k", Oo, -1); add(gt, "J1", rm, last=True)
         act(Te(), gt(), F.Sign, bias=-22529.5, scale=-1.0)
-        mm(X("GB", S(0, 128)), "I1", X("pgc"), True)
-        mm(X("GB", S(0, 64)), "I1", X("pof"))
-        for a in range(4): mm(X("GB", S(64 + a, 128, 4)), "Im1", Ne(a, a + 1))
+        step[0] = "goal%d" % p
+        gb = GOAL[p]
+        mm(X(gb, S(0, 128)), "I1", X("pgc"), True)
+        mm(X(gb, S(0, 64)), "I1", X("pof"))
+        for a in range(4): mm(X(gb, S(64 + a, 128, 4)), "Im1", Ne(a, a + 1))
         for a in range(4):
-            mm(X("GB", S(a, 64, 4)), "Im8k", M(a, a + 1))
-            for b in range(a + 1): mm(X("GB", S(64 + a, 128, 4)), "Im8k" if b == a else "I8k", M(b, b + 1), False, a == 3 and b == 3)
-        scan(X(gc), X("d0g"), X("GB", S(0, 128)), A.max, A.min)
+            mm(X(gb, S(a, 64, 4)), "Im8k", M(a, a + 1))
+            for b in range(a + 1): mm(X(gb, S(64 + a, 128, 4)), "Im8k" if b == a else "I8k", M(b, b + 1), False, a == 3 and b == 3)
+        scan(X(gc), X("d0g"), X(gb, S(0, 128)), A.max, A.min)
+        if p and RULES[0]: ops[-1]["behind"].update(mark[c] for c in range(2, 6))
         code = X(gc, S(67, 128, 4))
         cp(X(off), X(gc, S(3, 64, 4)))
+        yield
+        step[0] = "pairs%d" % p
         mm(X("DD", S(0, 16)), "I8k", X("pdd", p), True)
         if CHUNK[p] > 1:
-            for j in range(16): mm(X(BC, S(256 + j, 384, 16)), X("BB", j), X(gc, S(67, 128, 8)), j == 0, j == 15)
+            for j in range(16): mm(X("DD", S(16, 24), j) if BC[p] == "DD" else X(BC[p], S(256 + j, 384, 16)), X("BB", j), X(gc, S(67, 128, 8)), j == 0 and BC[p] != "DD")
         mm(X("DD", S(0, 16), 0), "Im1", code)
         for k in range(1, 16): mm(X("DD", S(0, 16), k), X("WD", k - 1), code, False, k == 15)
+        mark["pairs"] = range(len(ops) - 32, len(ops))
+        if RULES[2]:
+            for o in ops[-16:]: o["behind"].update(range(len(ops) - 32, len(ops) - 16))
+        if p and RULES[1]:
+            for o in ops[-32:]: o["behind"].update(mark["sums"])
         m = CHUNK[p]
         if m == 1:
             act(X(da, S(0, 256)), X("DD", S(0, 16)), F.Abs)
@@ -342,7 +377,7 @@ def rank_program(g, core, T, topo):
         else:
             ts(X("cf", S(0, 8)), X(gc, S(71, 128, 8)), 8192.0, None, A.mult)
             for k in range(8):
-                o, a, c = X(da, S(129 + 32 * k, 160 + 32 * k, 2)), X(BC, S(256 + 16 * k, 272 + 16 * k)), X("cf", S(k, k + 1))
+                o, a, c = X(da, S(129 + 32 * k, 160 + 32 * k, 2)), X("DD", 16 + k) if BC[p] == "DD" else X(BC[p], S(256 + 16 * k, 272 + 16 * k)), X("cf", S(k, k + 1))
                 if CROSS_Q[p] == "v": ts(o, a, c, 8192.0, A.not_equal, A.mult)
                 else: put("s", lambda o=o, a=a, c=c: s.activation(o[0], a[0], F.Abs, bias=c[0], scale=-1.0), [a, c], [o], cy(o[3]))
             act(X(da, S(0, 128)), X("DD", S(0, 16, 2)), F.Abs)
@@ -350,21 +385,22 @@ def rank_program(g, core, T, topo):
             scan(X(dr), X("d0c"), X(da), A.add, A.min)
             ts(X(dst, S(0, 16, 2)), X(dr, S(15, 128, 16)), -1.0, fb[0], A.mult, A.add)
             ts(X(dst, S(1, 16, 2)), X(dr, S(159, 384, 32)), -1.0, fb[1], A.mult, A.add)
-        pick(VAL_Q[p][0], X(ge), X(dq, S(0, 1024)), X(off), bias=-0.5)
-        pick(VAL_Q[p][1], X(go), X(dq, S(1024, 2048)), X(off))
-        gv, less = X("GB", S(128, 384)), 2 - (0 in BY_SCALAR[p]) - (2 in BY_SCALAR[p])
-        if less: mm(gv, "I1" if less == 2 else "Ih", view, True)
-        halves = [mm(gv, "Ih", X(ge), not less), mm(gv, "Ih", X(go))]
+        step[0] = "values%d" % p
+        less = 0
+        for h, o in enumerate((ge, go)):
+            q, raw = VAL_Q[p][h], 2 * h in BY_SCALAR[p]
+            pick(q, X(o), X(dq, S(1024 * h, 1024 * h + 1024)), X(off), view if q == "v" and not raw else None, A.add)
+            less += q == "s" and not raw
+        gv = X(GV[p], S(128, 384))
+        views = [mm(gv, "Hh", view, k == 0) for k in range(less)]
+        halves = views + [mm(gv, "Hh", X(ge), not less), mm(gv, "Hh", X(go))]
         mm(gv, "Imag", one(256), after=halves)
         act(X(vals), gv, bias=-12582912.0)
-        ke, ko = four("HS", 256), four("HS", 320)
-        if (t, p) not in TWICE:
-            add(ke, "I1", Oe, first=True); add(ke, "I1", Oo, -1); add(ko, "I1", Oo); add(ko, "I1", Oe); add(ko, "I1", To)
-            add(ke, "I1", M); add(ko, "I1", M); add(ke, "I1", Te, last=True)
-            act(X(kn), X("HS", S(256, 384)), bias=4.0)
+        step[0] = "rows%d" % p if t < 2 else "home%d" % p
         de, do = ((0, 1), (-1, 0), (0, 0))[t]
-        fo, fe = (lambda k: four("GP", 0, 4, k)), (lambda k: four("GP", 256, 4, k))
-        mm(X("GP", S(0, 256)), "Im8k", one(256), True)
+        GP, AB = ENDS[p] if t == 2 else ROWS[p]
+        fo, fe = (lambda k: four(GP, 0, 4, k)), (lambda k: four(GP, 256, 4, k))
+        mm(X(GP, S(0, 256)), "Im8k", one(256), True)
         add(fe(1), "Im8k", ones4); add(fe(2), "Im8k", ones4)
         add(fo(1), "I1", Io, de); add(fo(2), "I1", Ao, de); add(fo(3), "I1", Be, de); add(fo(1), "Im16k", Eo, de)
         add(fe(0), "I1", Ge, do); add(fe(1), "I1", Ae, do); add(fe(2), "I1", Bo, do - 1); add(fe(3), "I1", Ne, do)
@@ -372,37 +408,46 @@ def rank_program(g, core, T, topo):
         add(fe(1), "I8k", Oe, do); add(fe(2), "I8k", Oo, do - 1); add(fo(1), "I8k", To, de)
         add(fo(1), "Im8k", M, de); add(fe(3), "I8k", M, do); add(fe(3), "I8k", Te, do)
         add(fe(0), "Im16k", ones4); add(fe(0), "Im8k", Oe, do); add(fe(0), "Im8k", M, do)
-        scan(X(gs), X("d0p"), X("GP"), A.min, A.max)
+        for c in (S(0, 256), S(256, 512)): scan(X(gs, c), X("d0p", c), X(GP, c), A.min, A.max)
         out = "so%d%d" % (t + 1, p)
-        mm(X("AB", S(129, 384, 2)), "Im8k", one(128), True)
-        for j, (old_o, old_e, new) in enumerate(((Ao, Ae, Ge), (Bo, Be, Io))):
-            add(four("AB", 64 * j), "I1", old_o, de); add(four("AB", 128 + 128 * j, 2, 0), "I1", old_e, do)
-            add(four("AB", 128 + 128 * j, 2, 1), "I1", new, do)
-        for j in (0, 1): add(four("AB", 128 + 128 * j, 2, 1), "I8k", M, do)
         if t < 2:
-            for a in range(4): mm(X("AB", S(384, 400)), "SG", M(a, a + 1))
+            index_stage(p, out, "lo%d%d" % (t + 1, p))
+            for sem, c in ((("lj", S(0, 64)), ("li", S(64, 192))) if p in EARLY else (("li", S(0, 192)),)):
+                send(1, "li%d%d" % (t + 1, p), X("lo%d%d" % (t + 1, p), c), c, sem="%s%d%d" % (sem, t + 1, p))
+        yield
+        step[0] = "memory%d" % p if t < 2 else "home%d" % p
+        ke, ko = four(KEEP[p], 256), four(KEEP[p], 320)
+        if (t, p) not in TWICE:
+            add(ke, "I1", Oe, first=True); add(ke, "I1", Oo, -1); add(ko, "I1", Oo); add(ko, "I1", Oe); add(ko, "I1", To)
+            add(ke, "I1", M); add(ko, "I1", M); add(ke, "I1", Te, last=True)
+            if RULES[3] and t < 2:
+                for o in ops[-9:]: o["behind"].update(mark["pairs"])
+            act(X(kn), X(KEEP[p], S(256, 384)), bias=4.0)
+        mm(X(AB, S(129, 384, 2)), "Im8k", one(128), True)
+        for j, (old_o, old_e, new) in enumerate(((Ao, Ae, Ge), (Bo, Be, Io))):
+            add(four(AB, 64 * j), "I1", old_o, de); add(four(AB, 128 + 128 * j, 2, 0), "I1", old_e, do)
+            add(four(AB, 128 + 128 * j, 2, 1), "I1", new, do)
+        for j in (0, 1): add(four(AB, 128 + 128 * j, 2, 1), "I8k", M, do)
+        if t < 2:
+            for a in range(4): mm(X(AB, S(384, 400)), "SG", M(a, a + 1))
         for j in (0, 1):
-            ao, ak = four("AB", 64 * j), four("AB", 128 + 128 * j, 2, 0)
+            ao, ak = four(AB, 64 * j), four(AB, 128 + 128 * j, 2, 0)
             if (t, p) not in TWICE:
                 add(ao, "Im8k", Ko, de); add(ak, "Im8k", Ke, do)
                 continue
             add(ao, "Im32k", ones4); add(ak, "Im32k", ones4); add(ak, "Im8k", Oo, do - 1)
             for f in (Oo, Oe, To, M): add(ao, "Im8k", f, de)
             for f in (Oe, M, Te): add(ak, "Im8k", f, do)
-        n = 400 if t < 2 else 384
-        scan(X(out, S(192, 192 + n)), X("d0a", S(0, n)), X("AB", S(0, n)), A.min, A.max)
-        if t < 2:
-            index_stage(p, out, "lo%d%d" % (t + 1, p))
-            send(1, "li%d%d" % (t + 1, p), X("lo%d%d" % (t + 1, p)))
-            send(1, "si%d%d" % (t + 1, p), X(out))
+        n, at = (400, 192) if t < 2 else (384, 256)
+        for a, b in ((0, 192), (192, n)): scan(X(out, S(at + a, at + b)), X("d0a", S(a, b)), X(AB, S(a, b)), A.min, A.max)
+        if t < 2: send(1, "si%d%d" % (t + 1, p), X(out))
         else:
-            act(X(out, S(64, 192)), X(gs, S(3, 512, 4)))
-            act(X(out, S(0, 64)), X(out, S(321, 448, 2)))
-            act(X(out, S(320, 384)), X(out, S(449, 576, 2)))
+            act(X(out, S(128, 256)), X(gs, S(3, 512, 4)))
+            act(X(out, S(0, 128)), X(out, S(385, 640, 2)))
             send(-2, "si3%d" % p, X(out, S(0, 384)), S(0, 384))
 
     def write(t, p):
-        m = CHUNK[p]
+        m, step[0] = CHUNK[p], "write%d" % p
         for c in range(16 - m, -1, -m):
             o, va, wn = X("dst%d" % p, S(2 * c, 2 * c + 1) if m == 1 else S(c, c + m)), X("vals%d" % p, S(16 * c, 16 * (c + m))), X(table(t + 1))
             put("v", lambda o=o, va=va, wn=wn: v.tensor_copy(wn[0].indirect(o[0]), va[0]), [o, va], [wn], 0.05 + 16 * m * 3.0 * CY)
@@ -411,14 +456,15 @@ def rank_program(g, core, T, topo):
         for k in range(COPIES):
             c = S(4096 // COPIES * k, 4096 // COPIES * (k + 1))
             dma("y", T[table(t + 1)][:, c], T[table(t)][:, c], [X(table(t), c)] + ([X("yo")] if t == 0 else []), [X(table(t + 1), c)], 1024 // COPIES * (k + 1))
-        for p in PIECES: decide(t, p)
+        parts = {p: decide(t, p) for p in PIECES}
+        for p in TURNS: next(parts[p], None)
         if t == 2: cp(X(table(3), S(4095, 4096)), X("ZI", S(143, 144)))
         for p in PIECES: write(t, p)
     dma("y", T.ox[:], T[table(3)][:, 0:4096], [X(table(3), S(0, 4096))], [], 1024)
     for j, (buf, dst) in enumerate((("og_", T.og), ("oa_", T.oa), ("ob_", T.ob))):
         for p in PIECES:
             st = "si3%d" % p
-            src = [four(st, b) for b in ((128, 64), (0, 192), (320, 256))[j]]
+            src = [four(st, b) for b in ((192, 128), (0, 256), (64, 320))[j]]
             for h in (0, 1): act(X(buf, S(0, 4), h, S(16 * p, 16 * p + 16)), src[h](), bias=2048.0, scale=-1.0)
         dma("s", dst[:], T[buf][:], [X(buf)], [], 128)
 

import numpy as np
from concourse.mybir import AluOpType as A, ActivationFunctionType as F

f32, f16, bf, i32, u16 = "float32", "float16", "bfloat16", "int32", "uint16"
PIECES = (1, 0)
BY_SCALAR = {1: (0, 1), 0: ()}
COPIES = 0
TWICE = ()
MARG, GV = {}, ("GB", "GB")
ROWS, ENDS = (("AB", "AB"), ("GP", "GP")), (("GP", "AB"), ("GP", "AB"))
GOAL, TAKE, KEEP = ("XV", "GB"), ("DB", "HS"), ("GA", "GA")
CHUNK, CROSS_Q, D8 = {1: 2, 0: 2}, "sv", ("XV", "DB")
BC, TURNS, STAGE = ("XV", "HS"), (1, 0, 1, 1, 0, 0, 1, 0), ("XV", "XV", "XV")
RULES, EARLY = (1, 1, 1, 0), (0,)
AE_Q = "vvs"
VAL_Q = ("sv", "sv")
WB = {"Im1": -1, "Hh": 1023 / 2048, "I8k": 8192, "Im8k": -8192, "I16k": 16384, "Im16k": -16384, "Im32k": -32768, "Imag": 12582912,
      "I64k": 65536, "Im3232": -3232, "Im4096": -4096, "Im31": -31, "Im32": -32, "Im2080": -2080, "H62k": 62336}
SCRATCH = {
    "win0": ("sbuf", [128, 4752], bf),
    "yr0": ("sbuf", [128, 1024], bf), "yr1": ("sbuf", [128, 1024], bf), "yr2": ("sbuf", [128, 1024], bf),
    "yo": ("sbuf", [128, 2, 512], bf),
    "gn": ("sbuf", [128, 4, 2, 32], i32), "an": ("sbuf", [128, 4, 2, 32], i32), "bn": ("sbuf", [128, 4, 2, 32], i32),
    "tn": ("sbuf", [128, 4, 2, 32], i32),
    "th0": ("sbuf", [128, 8, 32], f16), "th1": ("sbuf", [128, 8, 32], f16), "th2": ("sbuf", [128, 8, 32], f16),
    "og_": ("sbuf", [128, 4, 2, 32], f32), "oa_": ("sbuf", [128, 4, 2, 32], f32), "ob_": ("sbuf", [128, 4, 2, 32], f32),
    "ones": ("sbuf", [128, 256], bf), "I1": ("sbuf", [128, 128], bf), "Z": ("sbuf", [128, 144], bf), "SG": ("sbuf", [128, 128], bf),
    "BB": ("sbuf", [128, 16, 128], bf), "d0c": ("sbuf", [128, 384], bf), "cf": ("sbuf", [128, 16], f32),
    "ZI": ("sbuf", [128, 144], bf), "J1": ("sbuf", [128, 128], f32),
    "WD": ("sbuf", [128, 15, 128], bf), "pi": ("sbuf", [128, 2], i32), "rm": ("sbuf", [128, 128], f32), "pm": ("sbuf", [128, 1], f32),
    "fb": ("sbuf", [128, 5], f32), "iod": ("sbuf", [128, 320], f32),
    "pof": ("sbuf", [128, 64], f16), "pgc": ("sbuf", [128, 128], bf), "pdd": ("sbuf", [128, 2, 256], f16),
    "d0g": ("sbuf", [128, 128], f32), "SD": ("sbuf", [128, 128], bf), "d0p": ("sbuf", [128, 512], f16), "d0a": ("sbuf", [128, 400], f16),
}
for _n in WB: SCRATCH[_n] = ("sbuf", [128, 128], f16 if _n[0] == "H" else bf)
for _p in PIECES:
    for _n, _w, _d in (("dq", 3072, bf), ("ab", 3072, bf), ("w8", 128, f16), ("ae", 128, bf), ("dsb", 128, f16), ("mn", 64, f32),
                       ("sO", 128, bf), ("sM", 64, bf), ("sT", 128, bf), ("kn", 128, bf), ("gc", 128, f16), ("off", 16, u16),
                       ("dst", 32, u16), ("ge", 256, bf), ("go", 256, bf), ("vals", 256, bf),
                       ("gs", 512, f16), ("P", 128, f32), ("Q", 128, i32), ("IDX", 128, i32),
                       ("li0", 192, u16), ("li1", 192, u16), ("li2", 192, u16), ("lo1", 192, u16), ("lo2", 192, u16),
                       ("si0", 592, f16), ("si1", 592, f16), ("si2", 592, f16), ("si3", 384, f16),
                       ("so1", 592, f16), ("so2", 592, f16), ("so3", 640, f16)):
        SCRATCH[_n + str(_p)] = ("sbuf", [128, _w], _d)
    for _n in ("da", "dr"): SCRATCH[_n + str(_p)] = ("sbuf", [128, 384], f32)
for _n in ("XV", "DB", "GA", "GB", "GP", "AB", "HS"): SCRATCH[_n] = ("psum", [128, 512], f32)
SCRATCH["DD"] = ("psum", [128, 32, 16], f32)
NDMA = 30
ARR = ["yr1", "yr2", "th1", "th2"] + [n + str(p) for n in ("li1", "li2", "lj1", "lj2", "si1", "si2", "si3") for p in PIECES]
SEMAPHORES = ["qv", "qs", "qt", "qg", "loc"] + ["d%d" % k for k in range(NDMA)] + ["a_" + n for n in ARR]
_cache = {}
CY, WAKE, HOP = 0.83e-3, 0.2, 2.5
RATE, LAST, LOAD, SPLIT = 300, 0.5, 400, 0


def plan(ops):
    n = len(ops)
    pred, succ = [[] for _ in ops], [[] for _ in ops]
    for k, o in enumerate(ops):
        for d in o["dep"] | o["behind"]:
            wait = d in o["dep"] and not ops[d]["q"] == o["q"] == "t"
            w = WAKE + ops[d]["lat"] + MARG.get(o["q"], 0.0) if wait else 0.0
            pred[k].append((d, w)); succ[d].append((k, w))
    def lay(order, before, first):
        end, busy = [0.0] * n, {q: [] for q in "vstgy"}
        for k in order:
            t, c = max([end[d] + w for d, w in before[k]] + [first[k]]), ops[k]["cost"]
            if ops[k]["q"] != "r":
                b = busy[ops[k]["q"]]
                j = len(b)
                while j and b[j - 1][1] > t: j -= 1
                while j < len(b) and b[j][0] < t + c + GAP[ops[k]["q"] == "t"] - 1e-9:
                    t = max(t, b[j][1]); j += 1
                b.insert(j, (t, t + c))
            end[k] = t + c
        return end
    way = [0.0] * n
    for k in range(n - 1, -1, -1): way[k] = ops[k]["cost"] + max([way[j] + w for j, w in succ[k]] + [ops[k]["lat"]])
    best = None
    for _ in range(ROUNDS):
        way = [way[k] + URGENT.get(ops[k]["step"], 0.0) for k in range(n)]
        for k in range(n - 1, -1, -1): way[k] = max([way[k]] + [way[j] + 1e-6 for j, w in succ[k]])
        end = lay(sorted(range(n), key=lambda k: (-way[k], k)), pred, [0.0] * n)
        span = max(end[k] + ops[k]["lat"] for k in range(n))
        if best is None or span < best[0]: best = (span, end)
        way = lay(sorted(range(n), key=lambda k: (-end[k], -k)), succ, [o["lat"] for o in ops])
    _cache["span"] = best[0]
    return sorted(range(n), key=lambda k: (best[1][k] - ops[k]["cost"], best[1][k], k))
URGENT = {"rows0": 0.5}
ROUNDS = 2
GAP = (0.0, 0.0)
GC, PE, PLAT = 1.3, 0.5, 0.06


def rank_program(g, core, T, topo):
    rank = T.rank_of(core)
    if rank is None:
        return
    N = len(T.cores)
    eng = {"v": g.vector, "s": g.scalar, "t": g.tensor, "g": g, "y": g.sync}
    ops, hist, runs, group = [], {n: [] for n in SCRATCH}, {}, {}
    S = slice
    step, mark = [""], {}

    def X(name, *idx):
        key = (name,) + tuple(("s", i.start, i.stop, i.step) if isinstance(i, slice) else i for i in idx)
        if key not in _cache:
            shp = SCRATCH[name][1][1:]
            a = np.arange(int(np.prod(shp))).reshape(shp)[idx].ravel()
            b = np.zeros(int(np.prod(shp)), np.uint8)
            b[a] = 1
            _cache[key] = (int.from_bytes(np.packbits(b).tobytes(), "big"), int(a.size))
        return (T[name][(slice(None),) + idx], name) + _cache[key]

    def put(q, call, rd, wr, cost, lat=0.03, sem=None, inc=1, after=(), behind=(), first=False):
        k, dep = len(ops), set(after)
        for regs, w in ((rd, False), (wr, True)):
            for r in regs:
                if SCRATCH[r[1]][0] == "psum":
                    owner, now, before = runs.get(r[1], (q, [], []))
                    if owner != q: now, before = [], now
                    dep.update(before)
                    if q == "t":
                        if first: group[r[1]] = k
                        dep.update(now if first else [group[r[1]]])
                    runs[r[1]] = (q, now + [k], before)
                else:
                    h = hist[r[1]]
                    dep.update(e[2] for e in h if e[0] & r[2] and (e[1] or w))
                    if w: h[:] = [e for e in h if e[0] & ~r[2]]
                    h.append((r[2], w, k))
        dep.discard(k)
        ops.append(dict(q=q, call=call, dep=dep, behind=set(behind) - dep, cost=cost, lat=lat, sem=sem or "q" + q, inc=inc,
                        group=group[wr[0][1]] if q == "t" else None, step=step[0]))
        return k

    v, s, te = g.vector, g.scalar, g.tensor
    def wide(*regs): return 0.5 if all(SCRATCH[r[1]][2] in (f16, bf, u16) for r in regs) else 1.0
    def cy(n): return max(64, n) * CY
    def tt(o, a, b, op):
        both = 2 if SCRATCH[a[1]][0] == SCRATCH[b[1]][0] else 1
        put("v", lambda: v.tensor_tensor(o[0], a[0], b[0], op), [a, b], [o], cy(o[3] * both * wide(o, a, b)))
    def ts(o, a, s1, s2, op0, op1=None):
        sc = [x for x in (s1, s2) if isinstance(x, tuple)]
        p1, p2 = (x[0] if isinstance(x, tuple) else x for x in (s1, s2))
        if op1 is None: put("v", lambda: v.tensor_scalar(o[0], a[0], p1, None, op0), [a] + sc, [o], cy(o[3] * wide(o, a)))
        else: put("v", lambda: v.tensor_scalar(o[0], a[0], p1, p2, op0, op1), [a] + sc, [o], cy(o[3] * wide(o, a)))
    def cp(o, a): put("v", lambda: v.tensor_copy(o[0], a[0]), [a], [o], cy(o[3] * wide(o, a)))
    def ms(o, c): put("v", lambda: v.memset(o[0], c), [], [o], cy(o[3] * wide(o)))
    def scan(o, d0, d1, op0, op1): put("v", lambda: v.tensor_tensor_scan(o[0], d0[0], d1[0], 0.0, op0, op1), [d0, d1], [o], cy(o[3]))
    def act(o, a, f=F.Identity, bias=0.0, scale=1.0):
        if bias == 0.0: put("s", lambda: s.activation(o[0], a[0], f, scale=scale), [a], [o], cy(o[3]))
        else: put("s", lambda: s.activation(o[0], a[0], f, bias=bias, scale=scale), [a], [o], cy(o[3]))
    def mm(o, w, r, first=False, last=False, after=()):
        w = X(w) if isinstance(w, str) else w
        return put("t", lambda stop: te.matmul(o[0], w[0], r[0], first, stop), [w, r], [o], cy(r[3]) * (4 if w[1] == "J1" else 1) * PE, PLAT,
                   first=first, after=after)
    def pick(q, o, wn, off, sub=None, op=A.subtract):
        src, c = wn[0].indirect(off[0]), 0.06 + GC * o[3] * CY
        if sub: put("v", lambda: v.tensor_tensor(o[0], src, sub[0], op), [wn, off, sub], [o], c)
        elif q == "v": put("v", lambda: v.tensor_copy(o[0], src), [wn, off], [o], c)
        else: put("s", lambda: s.activation(o[0], src, F.Copy), [wn, off], [o], c)
    def own(call, rd, o): put("g", call, rd, [o], 0.17 + 2 * o[3] * CY)
    dmas = []
    def dma(q, o, a, rd, wr, kb, first=False):
        dmas.append(put(q, lambda: eng[q].dma_start(o, a), rd, wr, 0.05, 2.0 + kb / LOAD, "d%d" % len(dmas), 16, behind=dmas[-1:] if first else ()))
    def send(to, name, i, *idx, sem=None):
        dst, o, name = T.cores[(rank + to) % N], X(name, *idx), sem or name
        rid, pid, _ = topo.addr(dst)
        k = put("g", lambda: g.remote_dma(o[0], i[0], T.sem["a_" + name], T.sem.loc, pid, rid, topo.mask(core, dst)), [i], [], 0.3, 0.0,
                "loc", len(topo.engines(core, dst)))
        put("r", None, [], [o], HOP + o[3] / RATE + (LAST if to < 0 else 0), 0.0, "a_" + name, len(topo.engines(T.cores[(rank - to) % N], core)), [k])

    dma("y", T.gn[:], T.gl[:], [], [X("gn")], 128, True)
    dma("s", T.win0[:, 4088:4096], T.xt[:, 4088:4096], [], [X("win0", S(4088, 4096))], 0, True)
    dma("y", T.yr0[:, 256:768], T.yv[:, 0:512], [], [X("yr0", S(256, 768))], 256, True)
    dma("y", T.win0[:, 0:4088], T.xt[:, 0:4088], [], [X("win0", S(0, 4088))], 1280, True)
    for k, (n, src) in enumerate((("an", T.al), ("bn", T.bl), ("tn", T.th))): dma("y", T[n][:], src[:], [], [X(n)], 1408 + 128 * k, True)
    dma("y", T.yo[:], T.yv[:, 512:1536], [], [X("yo")], 2048, True)
    for p in PIECES: cp(X("yr0", S(768 * p, 768 * p + 256)), X("yr0", S(256 + 256 * p, 512 + 256 * p)))
    cp(X("ZI", S(143, 144)), X("win0", S(4095, 4096)))
    ms(X("win0", S(4095, 4096)), 512.0)

    big = dict(allow_small_or_imprecise_dtypes=True)
    one = lambda n: X("ones", S(0, n))
    ms(X("ones"), 1.0)
    own(lambda: g.affine_select(T.I1[:], T.ones[:, 0:128], [[-1, 128]], A.is_equal, 0.0, 0, 1), [one(128)], X("I1"))
    own(lambda: g.iota(T.pi[:, 0:1], [[0, 1]], 0, 1), [], X("pi", S(0, 1)))
    for k, n in enumerate(WB):
        if k % 2: act(X(n), X("I1"), scale=float(WB[n]))
        else: ts(X(n), X("I1"), float(WB[n]), None, A.mult)
    ms(X("Z"), 0.0)
    zc = X("Z", S(15, 143, 16))
    own(lambda: g.affine_select(zc[0], T.ones[:, 0:8], [[-16, 8]], A.is_ge, 0.0, 0, 1), [one(8)], zc)
    own(lambda: g.affine_select(zc[0], zc[0], [[16, 8]], A.is_ge, 0.0, 15, -1), [zc], zc)
    own(lambda: g.iota(T.iod[:, 0:256], [[0, 16], [1, 16]], 0, 0, **big), [], X("iod", S(0, 256)))
    own(lambda: g.iota(T.iod[:, 256:320], [[16, 16], [256, 4]], 0, 0, **big), [], X("iod", S(256, 320)))
    own(lambda: g.iota(T.pgc[:, 64:128], [[0, 16], [8192, 4]], 8192, 0, **big), [], X("pgc", S(64, 128)))
    ms(X("pgc", S(0, 64)), 8192.0)
    ts(X("pi", S(1, 2)), X("pi", S(0, 1)), 15, None, A.bitwise_and)
    cp(X("pm"), X("pi", S(1, 2)))
    fb = [X("fb", S(k, k + 1)) for k in range(5)]
    ts(fb[4], X("pm"), 2.0, 2050.0, A.mult, A.add)
    for u in range(2): ts(fb[u], X("pm"), 2.0, 4612.0 + 32 * u, A.mult, A.add)
    ts(X("SG"), X("iod", S(0, 128)), X("pm"), 0.5, A.is_equal, A.mult)
    ms(X("cf"), -2048.0)
    ts(X("pof"), X("iod", S(256, 320)), X("pm"), None, A.add)
    for p in PIECES:
        ts(X("pdd", p), X("iod", S(0, 256)), X("pm"), 4096.0, A.is_gt, A.mult)
        for u in range(CHUNK[p]): ts(X("pdd", p, S(16 * u, 256, 16 * CHUNK[p])), X("cf", S(0, 16 // CHUNK[p])), fb[u], 1 / 8192, A.add, A.mult)
    ms(X("d0g"), -60000.0); ms(X("d0g", S(0, 64, 4)), 1023.0)
    ts(X("d0g", S(64, 128, 4)), X("iod", S(256, 320, 4)), 2.0, fb[4], A.mult, A.add)
    ms(X("d0p"), 60000.0); ms(X("d0p", S(0, 512, 4)), -2047.0)
    ms(X("d0a"), -2047.0); ms(X("d0a", S(129, 384, 2)), 60000.0)
    ms(X("ZI", S(0, 16)), 0.0); cp(X("ZI", S(15, 143)), X("I8k"))
    for b, bank in enumerate(("XV", "GB", "AB", "DB")):
        ks = range(4 * b + 1, min(4 * b + 5, 16))
        for k in ks:
            o = X(bank, S(128 * (k - ks[0]), 128 * (k - ks[0] + 1)))
            mm(o, "I1", X("ZI", S(15 - k, 143 - k)), k == ks[0]); mm(o, "Im1", X("I8k"))
        act(X("WD", S(ks[0] - 1, ks[-1])), X(bank, S(0, 128 * len(ks))))
    act(X("J1"), X("I1"))
    tt(X("SD", S(0, 64)), X("I1", S(0, 64)), X("I1", S(64, 128)), A.subtract)
    tt(X("SD", S(64, 112)), X("I1", S(64, 112)), X("I1", S(16, 64)), A.subtract)
    tt(X("SD", S(112, 128)), X("I1", S(112, 128)), X("I1", S(0, 16)), A.subtract)
    m = max(CHUNK.values())
    if m > 1:
        ms(X("BB"), 0.0)
        own(lambda: g.affine_select(T.BB[:], T.BB[:], [[-1, 16], [-16, 8], [0, 16]], A.not_equal, 8192.0, 0, 1), [X("BB")], X("BB"))
        ms(X("d0c"), 0.0); ms(X("d0c", S(0, 128, 16)), 1e9); ms(X("d0c", S(128, 384, 32)), 1e9)

    def four(name, base, step=1, k=0): return lambda a=0, b=4: X(name, S(base + 16 * step * a + k, base + 16 * step * b, step))
    def add(out, w, src, sh=0, first=False, last=False):
        ps = {0: [(0, 4, 0)], 1: [(0, 3, 1), (3, 4, 0)], -1: [(1, 4, 0), (0, 1, 3)]}[sh]
        for j, (a, b, c) in enumerate(ps): mm(out(a, b), w, src(c, c + b - a), first and j == 0, last and j == len(ps) - 1)
    ones4 = four("ones", 0)
    def none(q, o, a):
        if q == "v": ts(o, a, -2047.0, None, A.is_equal)
        else: act(o, a, F.Relu, bias=-2046.0, scale=-1.0)

    def index_stage(p, st, ls):
        gs, P, Q, IDX = ("%s%d" % (n, p) for n in ("gs", "P", "Q", "IDX"))
        we, wo = four(gs, 0, 4, 3), four(gs, 256, 4, 3)
        none(AE_Q[2], X(st, S(0, 128)), X(gs, S(3, 512, 4)))
        act(X(st, S(128, 192)), we())
        add(four("HS", 0), "Im4096", we, 1, first=True)
        add(four("HS", 0), "Im31", we, 1)
        add(four("HS", 64), "I1", wo)
        add(four("HS", 64), "Im3232", ones4)
        add(four("HS", 128), "I64k", ones4)
        add(four("HS", 128), "Im32", wo)
        add(four("HS", 192), "Im2080", wo)
        add(four("HS", 0), "H62k", ones4)
        tt(X(P), X("HS", S(0, 128)), X(st, S(64, 192)), A.mult)
        tt(X(Q), X("HS", S(128, 256)), X(P), A.add)
        ts(X(IDX), X(Q), 5, 4095, A.arith_shift_right, A.bitwise_and)
        ts(X(ls, S(0, 64)), we(), -1.0, 2048.0, A.mult, A.add)
        cp(X(ls, S(64, 192)), X(IDX))

    for p in PIECES:
        c = S(16 * p, 16 * p + 16)
        for h in (0, 1): ts(four("gs%d" % p, 256 * h, 4, 3)(), X("gn", S(0, 4), h, c), -1.0, 2048.0, A.mult, A.add)
        index_stage(p, "si0%d" % p, "li0%d" % p)
        for j, n in enumerate(("an", "bn")):
            ts(four("si0%d" % p, 192 + 64 * j)(), X(n, S(0, 4), 0, c), -1.0, 2048.0, A.mult, A.add)
            ts(four("si0%d" % p, 320 + 128 * j, 2, 1)(), X(n, S(0, 4), 1, c), -1.0, 2048.0, A.mult, A.add)
    for h in (0, 1): ts(X("th0", S(4 * h, 4 * h + 4)), X("tn", S(0, 4), h), -2048.0, None, A.add)
    for k in (1, 2):
        send(k, "yr%d" % k, X("yo", k - 1), S(256, 768))
        send(k, "th%d" % k, X("th0"))
        n = "yr%d" % k
        for p in PIECES:
            o, a = X(n, S(768 * p, 768 * p + 256)), X(n, S(256 + 256 * p, 512 + 256 * p))
            dma("y", o[0], a[0], [a], [o], 64)

    def table(t): return "win%d" % (t % 2 if COPIES else 0)
    def decide(t, p):
        st, ls, yr, th = "si%d%d" % (t, p), "li%d%d" % (t, p), "yr%d" % t, "th%d" % t
        dq, ab, w8, ae, dsb, mn, sO, sM, sT, kn, gc, off, da, dr, dst, ge, go, vals, gs = (
            n + str(p) for n in ("dq", "ab", "w8", "ae", "dsb", "mn", "sO", "sM", "sT", "kn", "gc", "off", "da", "dr", "dst", "ge", "go", "vals", "gs"))
        Ee, Eo, Ge, Io, Ne = four(st, 0), four(st, 64), four(st, 128), four(w8, 0), four(w8, 64)
        Ae, Be, Ao, Bo = four(st, 192), four(st, 256), four(st, 320, 2, 1), four(st, 448, 2, 1)
        Oe, Oo, M, Te, To, Ke, Ko = four(sO, 0), four(sO, 64), four(sM, 0), four(sT, 0), four(sT, 64), four(kn, 0), four(kn, 64)
        view2, view = X(yr, S(512 * p, 512 * p + 512)), X(yr, S(256 + 256 * p, 512 + 256 * p))
        step[0] = "gather%d" % p
        def total(out, row, first, last):
            for j in range(16):
                mm(out, X("Z", S(15 - j, 143 - j)), X(ab, S(256 * row + j, 256 * row + 1024, 16)), first and j == 0, last and j == 15)
        for c in range(6):
            o, a, l, wn = X(dq, S(512 * c, 512 * c + 512)), X(ab, S(512 * c, 512 * c + 512)), X(ls, S(32 * c, 32 * c + 32)), X(table(t), S(0, 4096))
            if c in BY_SCALAR[p]:
                pick("s", o, wn, l)
                xv = X(STAGE[BY_SCALAR[p].index(c)])
                mm(xv, "Im1", view2, True)
                mm(xv, "I1", o)
                act(a, xv, F.Abs)
            elif SPLIT and p == 0 and c == 5:
                for h in (10, 11):
                    o = X(dq, S(256 * h, 256 * h + 256))
                    pick("v", o, wn, X(ls, S(16 * h, 16 * h + 16)), view)
                    act(X(ab, S(256 * h, 256 * h + 256)), o, F.Abs)
            else:
                step[0] = "pick%d" % p
                pick("v", o, wn, l, view2)
                step[0], mark[c] = "gather%d" % p, len(ops) - 1
                act(a, o, F.Abs)
        step[0] = "flags%d" % p
        for j in range(16): mm(X(D8[p], S(j, 128, 16)), X(ab, S(j, 2048, 16)), X("Z", S(15, 143, 16)), j == 0)
        mark["sums"] = range(len(ops) - 16, len(ops))
        act(X(dsb), X(D8[p], S(0, 128)), bias=-2047.0)
        yield
        step[0] = "flags%d" % p
        ts(X(w8), X(ls, S(64, 192)), -1.0, 2048.0, A.mult, A.add)
        none(AE_Q[0], four(ae, 0)(), Ae())
        none(AE_Q[1], four(ae, 64)(), Ao())
        tq = lambda h: (lambda a, b: X(th, S(4 * h + a, 4 * h + b), S(16 * p, 16 * p + 16)))
        ge_, go_ = four("GA", 0), four("GA", 64)
        mm(X("GA", S(0, 128)), "Im16k", X(st, S(0, 128)), True)
        add(ge_, "I16k", Eo); add(go_, "I16k", Ee, 1)
        add(ge_, "Im1", tq(t % 2)); add(go_, "Im1", tq(1 - t % 2), t % 2)
        mm(X("GA", S(0, 128)), "Im16k", X(ae))
        if t:
            for k in range(8): mm(X("GA", S(16 * k, 16 * k + 16)), "Im1", X(st, S(576, 592)))
        mm(X("GA", S(0, 128)), dsb, X("I1"))
        mm(X("GA", S(128, 192)), dsb, X("SD", S(0, 64)))
        act(X(sO), X("GA", S(0, 128)), F.Sign, bias=-16385.5 - (16 if t else 0))
        act(X(mn), X("GA", S(128, 192)), F.Relu)
        gm = four("DB", 128)
        add(gm, "I16k", Ee, first=True); add(gm, "I16k", Eo); add(gm, "J1", four(mn, 0)); add(gm, "I8k", Oo)
        mm(gm(), dsb, X("Im1", S(0, 64)))
        total(gm(), 8, False, True)
        gt = four("DB", 192)
        add(gt, "Im16k", Eo); add(gt, "I16k", Ee, 1); add(gt, "I8k", Oe)
        mm(gt(), dsb, X("SD", S(64, 128)))
        act(M(), gm(), F.Sign, bias=-6145.5, scale=-1.0)
        act(To(), gt(), F.Sign, bias=-24576.5, scale=-1.0)
        step[0] = "take%d" % p
        gt = four(TAKE[p], 384)
        if (t, p) in TWICE:
            add(gt, "Im16k", Ee, first=True); add(gt, "I16k", Eo); add(gt, "I8k", Oo, -1)
            mm(gt(), dsb, X("Im1", S(64, 128)))
            total(gt(), 8, False, True)
        else:
            rm = four("rm", 64 * p)
            act(rm(), gm())
            add(gt, "Im32k", Ee, first=True); add(gt, "Im8k", Oo); add(gt, "I8k", Oo, -1); add(gt, "J1", rm, last=True)
        act(Te(), gt(), F.Sign, bias=-22529.5, scale=-1.0)
        step[0] = "goal%d" % p
        gb = GOAL[p]
        mm(X(gb, S(0, 128)), "I1", X("pgc"), True)
        mm(X(gb, S(0, 64)), "I1", X("pof"))
        for a in range(4): mm(X(gb, S(64 + a, 128, 4)), "Im1", Ne(a, a + 1))
        for a in range(4):
            mm(X(gb, S(a, 64, 4)), "Im8k", M(a, a + 1))
            for b in range(a + 1): mm(X(gb, S(64 + a, 128, 4)), "Im8k" if b == a else "I8k", M(b, b + 1), False, a == 3 and b == 3)
        scan(X(gc), X("d0g"), X(gb, S(0, 128)), A.max, A.min)
        if p and RULES[0]: ops[-1]["behind"].update(mark[c] for c in range(2, 6))
        code = X(gc, S(67, 128, 4))
        cp(X(off), X(gc, S(3, 64, 4)))
        yield
        step[0] = "pairs%d" % p
        mm(X("DD", S(0, 16)), "I8k", X("pdd", p), True)
        if CHUNK[p] > 1:
            for j in range(16): mm(X("DD", S(16, 24), j) if BC[p] == "DD" else X(BC[p], S(256 + j, 384, 16)), X("BB", j), X(gc, S(67, 128, 8)), j == 0 and BC[p] != "DD")
        mm(X("DD", S(0, 16), 0), "Im1", code)
        for k in range(1, 16): mm(X("DD", S(0, 16), k), X("WD", k - 1), code, False, k == 15)
        mark["pairs"] = range(len(ops) - 32, len(ops))
        if RULES[2]:
            for o in ops[-16:]: o["behind"].update(range(len(ops) - 32, len(ops) - 16))
        if p and RULES[1]:
            for o in ops[-32:]: o["behind"].update(mark["sums"])
        m = CHUNK[p]
        if m == 1:
            act(X(da, S(0, 256)), X("DD", S(0, 16)), F.Abs)
            scan(X(dr, S(0, 256)), X("d0d"), X(da, S(0, 256)), A.add, A.min)
            ts(X(dst, S(0, 32, 2)), X(dr, S(15, 256, 16)), -1.0, fb[0], A.mult, A.add)
        else:
            ts(X("cf", S(0, 8)), X(gc, S(71, 128, 8)), 8192.0, None, A.mult)
            for k in range(8):
                o, a, c = X(da, S(129 + 32 * k, 160 + 32 * k, 2)), X("DD", 16 + k) if BC[p] == "DD" else X(BC[p], S(256 + 16 * k, 272 + 16 * k)), X("cf", S(k, k + 1))
                if CROSS_Q[p] == "v": ts(o, a, c, 8192.0, A.not_equal, A.mult)
                else: put("s", lambda o=o, a=a, c=c: s.activation(o[0], a[0], F.Abs, bias=c[0], scale=-1.0), [a, c], [o], cy(o[3]))
            act(X(da, S(0, 128)), X("DD", S(0, 16, 2)), F.Abs)
            act(X(da, S(128, 384, 2)), X("DD", S(1, 16, 2)), F.Abs)
            scan(X(dr), X("d0c"), X(da), A.add, A.min)
            ts(X(dst, S(0, 16, 2)), X(dr, S(15, 128, 16)), -1.0, fb[0], A.mult, A.add)
            ts(X(dst, S(1, 16, 2)), X(dr, S(159, 384, 32)), -1.0, fb[1], A.mult, A.add)
        step[0] = "values%d" % p
        less = 0
        for h, o in enumerate((ge, go)):
            q, raw = VAL_Q[p][h], 2 * h in BY_SCALAR[p]
            pick(q, X(o), X(dq, S(1024 * h, 1024 * h + 1024)), X(off), view if q == "v" and not raw else None, A.add)
            less += q == "s" and not raw
        gv = X(GV[p], S(128, 384))
        views = [mm(gv, "Hh", view, k == 0) for k in range(less)]
        halves = views + [mm(gv, "Hh", X(ge), not less), mm(gv, "Hh", X(go))]
        mm(gv, "Imag", one(256), after=halves)
        act(X(vals), gv, bias=-12582912.0)
        step[0] = "rows%d" % p if t < 2 else "home%d" % p
        de, do = ((0, 1), (-1, 0), (0, 0))[t]
        GP, AB = ENDS[p] if t == 2 else ROWS[p]
        fo, fe = (lambda k: four(GP, 0, 4, k)), (lambda k: four(GP, 256, 4, k))
        mm(X(GP, S(0, 256)), "Im8k", one(256), True)
        add(fe(1), "Im8k", ones4); add(fe(2), "Im8k", ones4)
        add(fo(1), "I1", Io, de); add(fo(2), "I1", Ao, de); add(fo(3), "I1", Be, de); add(fo(1), "Im16k", Eo, de)
        add(fe(0), "I1", Ge, do); add(fe(1), "I1", Ae, do); add(fe(2), "I1", Bo, do - 1); add(fe(3), "I1", Ne, do)
        add(fo(1), "Im8k", Oo, de); add(fo(2), "I8k", Oo, de); add(fo(3), "I8k", Oe, de)
        add(fe(1), "I8k", Oe, do); add(fe(2), "I8k", Oo, do - 1); add(fo(1), "I8k", To, de)
        add(fo(1), "Im8k", M, de); add(fe(3), "I8k", M, do); add(fe(3), "I8k", Te, do)
        add(fe(0), "Im16k", ones4); add(fe(0), "Im8k", Oe, do); add(fe(0), "Im8k", M, do)
        for c in (S(0, 256), S(256, 512)): scan(X(gs, c), X("d0p", c), X(GP, c), A.min, A.max)
        out = "so%d%d" % (t + 1, p)
        if t < 2:
            index_stage(p, out, "lo%d%d" % (t + 1, p))
            for sem, c in ((("lj", S(0, 64)), ("li", S(64, 192))) if p in EARLY else (("li", S(0, 192)),)):
                send(1, "li%d%d" % (t + 1, p), X("lo%d%d" % (t + 1, p), c), c, sem="%s%d%d" % (sem, t + 1, p))
        yield
        step[0] = "memory%d" % p if t < 2 else "home%d" % p
        ke, ko = four(KEEP[p], 256), four(KEEP[p], 320)
        if (t, p) not in TWICE:
            add(ke, "I1", Oe, first=True); add(ke, "I1", Oo, -1); add(ko, "I1", Oo); add(ko, "I1", Oe); add(ko, "I1", To)
            add(ke, "I1", M); add(ko, "I1", M); add(ke, "I1", Te, last=True)
            if RULES[3] and t < 2:
                for o in ops[-9:]: o["behind"].update(mark["pairs"])
            act(X(kn), X(KEEP[p], S(256, 384)), bias=4.0)
        mm(X(AB, S(129, 384, 2)), "Im8k", one(128), True)
        for j, (old_o, old_e, new) in enumerate(((Ao, Ae, Ge), (Bo, Be, Io))):
            add(four(AB, 64 * j), "I1", old_o, de); add(four(AB, 128 + 128 * j, 2, 0), "I1", old_e, do)
            add(four(AB, 128 + 128 * j, 2, 1), "I1", new, do)
        for j in (0, 1): add(four(AB, 128 + 128 * j, 2, 1), "I8k", M, do)
        if t < 2:
            for a in range(4): mm(X(AB, S(384, 400)), "SG", M(a, a + 1))
        for j in (0, 1):
            ao, ak = four(AB, 64 * j), four(AB, 128 + 128 * j, 2, 0)
            if (t, p) not in TWICE:
                add(ao, "Im8k", Ko, de); add(ak, "Im8k", Ke, do)
                continue
            add(ao, "Im32k", ones4); add(ak, "Im32k", ones4); add(ak, "Im8k", Oo, do - 1)
            for f in (Oo, Oe, To, M): add(ao, "Im8k", f, de)
            for f in (Oe, M, Te): add(ak, "Im8k", f, do)
        n, at = (400, 192) if t < 2 else (384, 256)
        for a, b in ((0, 192), (192, n)): scan(X(out, S(at + a, at + b)), X("d0a", S(a, b)), X(AB, S(a, b)), A.min, A.max)
        if t < 2: send(1, "si%d%d" % (t + 1, p), X(out))
        else:
            act(X(out, S(128, 256)), X(gs, S(3, 512, 4)))
            act(X(out, S(0, 128)), X(out, S(385, 640, 2)))
            send(-2, "si3%d" % p, X(out, S(0, 384)), S(0, 384))

    def write(t, p):
        m, step[0] = CHUNK[p], "write%d" % p
        for c in range(16 - m, -1, -m):
            o, va, wn = X("dst%d" % p, S(2 * c, 2 * c + 1) if m == 1 else S(c, c + m)), X("vals%d" % p, S(16 * c, 16 * (c + m))), X(table(t + 1))
            put("v", lambda o=o, va=va, wn=wn: v.tensor_copy(wn[0].indirect(o[0]), va[0]), [o, va], [wn], 0.05 + 16 * m * 3.0 * CY)

    for t in range(3):
        for k in range(COPIES):
            c = S(4096 // COPIES * k, 4096 // COPIES * (k + 1))
            dma("y", T[table(t + 1)][:, c], T[table(t)][:, c], [X(table(t), c)] + ([X("yo")] if t == 0 else []), [X(table(t + 1), c)], 1024 // COPIES * (k + 1))
        parts = {p: decide(t, p) for p in PIECES}
        for p in TURNS: next(parts[p], None)
        if t == 2: cp(X(table(3), S(4095, 4096)), X("ZI", S(143, 144)))
        for p in PIECES: write(t, p)
    dma("y", T.ox[:], T[table(3)][:, 0:4096], [X(table(3), S(0, 4096))], [], 1024)
    for j, (buf, dst) in enumerate((("og_", T.og), ("oa_", T.oa), ("ob_", T.ob))):
        for p in PIECES:
            st = "si3%d" % p
            src = [four(st, b) for b in ((192, 128), (0, 256), (64, 320))[j]]
            for h in (0, 1): act(X(buf, S(0, 4), h, S(16 * p, 16 * p + 16)), src[h](), bias=2048.0, scale=-1.0)
        dma("s", dst[:], T[buf][:], [X(buf)], [], 128)

    if "order" not in _cache: _cache["order"] = plan(ops)
    cnt, done, known, left = {}, {}, {q: {} for q in eng}, {}
    for o in ops: left[o["group"]] = left.get(o["group"], 0) + 1
    for k in _cache["order"]:
        o = ops[k]
        q, sem = o["q"], o["sem"]
        cnt[sem] = cnt.get(sem, 0) + o["inc"]
        if q == "r":
            done[k] = (sem, cnt[sem], {sem: cnt[sem]})
            continue
        for dsem, c, clk in sorted((done[j] for j in o["dep"] if not (q == "t" and ops[j]["q"] == "t")), key=lambda e: (-len(e[2]), -e[1])):
            if known[q].get(dsem, 0) >= c: continue
            eng[q].wait_ge(T.sem[dsem], c)
            for x in clk: known[q][x] = max(known[q].get(x, 0), clk[x])
        if q == "t":
            left[o["group"]] -= 1
            ins = o["call"](not left[o["group"]])
        else: ins = o["call"]()
        if sem != "loc": ins.then_inc(T.sem[sem], o["inc"])
        clk = dict(known[q]); clk[sem] = cnt[sem]
        done[k] = (sem, cnt[sem], clk)
    for sem in cnt: g.wait_ge(T.sem[sem], cnt[sem])
